import numpy as np, ml_dtypes
CORES = [24,25,26,27,28,29,30,31]
N = 8
BF = ml_dtypes.bfloat16
V, H, LB, K, T, TH = 4096, 2048, 12, 128, 4, 4
ODD = (np.arange(16) & 1)[:, None]
def before(w):
    return np.concatenate([np.zeros_like(w[..., :1, :]), w[..., :-1, :]], axis=-2) * ODD
def follow(rng, cyc):
    F = rng.integers(0, V, (8, 16, V))
    for g in range(8):
        for k in range(16):
            e = np.roll(cyc[g], -(k + 1))
            F[g, k, cyc[g]] = (e + np.roll(cyc[g], -1)) & (V - 1) if k & 1 else e
    return F
def chain(cyc, b):
    return np.take_along_axis(cyc[:, None, :], (b[:, None, :] - np.arange(16)[None, :, None]) % cyc.shape[1], 2)
def spoil(rng, F, share):
    return np.where(rng.random(F.shape) < share, rng.integers(0, V, F.shape), F)
def pack(F, x, w):
    return {"fld": (F[..., :H] + V * F[..., H:]).reshape(N, 128, H).astype(np.int32), "rec": np.ascontiguousarray(x).reshape(N, 128, V).astype(np.float32).astype(BF),
            "wnd": np.ascontiguousarray(w).reshape(N, 128, K).astype(np.int32)}
def setup_inputs(rng):
    cyc = np.argsort(rng.random((8, V)), axis=-1); F = np.stack([follow(rng, cyc)] * N)
    F = spoil(rng, F, rng.choice(np.array([0.12, 0.35, 0.55, 0.68]), (N, 8, 1, 1)))
    w = np.stack([chain(cyc, rng.integers(0, V, (8, K))) for r in range(N)])
    w = spoil(rng, w, rng.choice(np.array([0.0, 0.0, 0.06, 0.06, 0.06, 0.2, 0.2, 1.0]), (N, 8, 1, K)))
    return pack(F, rng.integers(0, 16, (N, 8, 16, V)), w)
def setup_inputs_spread(rng):
    cyc = np.argsort(rng.random((8, V)), axis=-1); F = np.stack([follow(rng, cyc)] * N)
    low = np.minimum((V * rng.random(F.shape) ** 4).astype(np.int64), V - 1)
    F = np.where(rng.random(F.shape) < 0.85 * rng.random((N, 8, 1, 1)) ** 1.5, low, F)
    w = np.stack([chain(cyc, np.minimum((V * rng.random((8, K)) ** 3).astype(np.int64), V - 1)) for r in range(N)])
    w = spoil(rng, w, 0.5 * rng.random((N, 8, 1, K)) ** 3)
    x = np.minimum((16 * rng.random(F.shape) ** np.exp2(rng.integers(-2, 4, (N, 8, 1, V)))).astype(np.int64), 15)
    return pack(F, x, w)
def setup_inputs_ends(rng):
    e = V - 1
    F = e * np.tile(rng.integers(0, 2, (N, 8, 16, H)), (1, 1, 1, 2))
    x = 15 * np.where(rng.random((N, 8, 1, V)) < 0.5, rng.integers(0, 2, (N, 8, 1, V)), rng.integers(0, 2, (N, 8, 16, V)))
    w = e * (rng.random((N, 8, 16, K)) < rng.choice(np.array([0.1, 0.5, 0.9]), (N, 8, 1, K))).astype(np.int64)
    F[:, 4:, :, 0] = 0; F[:, 4:, :, H] = 0; F[:, 4:, :, H - 1] = e; F[:, 4:, :, e] = e
    for c in (0, 1, e):
        x[:, 4, :, c] = 0; x[:, 5, :, c] = 15
    for g in (6, 7):
        x[:, g, :, 0] = 0; x[:, g, :, 1] = 0; x[:, g, :, e] = 15
    x[:, 6, 8:, 1] = 15
    pat = np.zeros((7, 16), np.int64)
    pat[0, 15] = 1; pat[1, 14] = 1; pat[2, 2] = 1; pat[2, 15] = 1; pat[3] = np.array([0, 1] * 7 + [1, 0]); pat[4] = np.array([0, 1] + [1, 0] * 7); pat[5] = 1
    pt = rng.integers(0, 7, (N, 4, K))
    pt[:, 0:2, K - 1] = 4; pt[:, 0:2, 0] = 4; pt[:, 2, K - 1] = 3; pt[:, 2, 1] = 3; pt[:, 3, K - 1] = 0; pt[:, 3, 0] = 2; pt[:, 3, 1] = 6
    pt[N - 1, 3] = 6; pt[N - 1, 3, K - 1] = 0
    w[:, 4:] = e * np.moveaxis(pat[pt], 3, 2)
    return pack(F, x, w)
def setup_inputs_corners(rng):
    R = V // 8; inner = 1 + np.argsort(rng.random((8, V - 2)), axis=-1)
    out = np.concatenate([np.tile(np.array([0, V - 1]), (8, 1)), inner[:, :R - 2]], axis=1); cyc = np.ascontiguousarray(inner[:, R - 2:])
    F = np.stack([follow(rng, cyc)] * N); x = rng.integers(0, 16, (N, 8, 16, V)); s0 = int(rng.integers(0, N)); q = [(s0 + i) % N for i in range(N)]
    b = np.argsort(rng.random((N, 8, V - R)), axis=-1)[..., :K]
    w = np.stack([chain(cyc, b[r]) for r in range(N)])
    for r in (q[1], q[3]):
        F[r] = spoil(rng, F[r], 0.58)
        F[r, :, :, ::16] = 16 * rng.integers(0, V // 16, (8, 16, V // 16)) + np.arange(16)[None, :, None]
        w[r] = 16 * rng.integers(0, V // 16 - 1, (8, 16, K))
    g = int(rng.integers(0, 8)); m = int(rng.integers(0, V))
    w[q[1], g, :, int(rng.integers(0, K))] = V - 16; F[q[1], g, 0::2, V - 16] = m; F[q[1], g, 1::2, V - 16] = (m + V - 16) & (V - 1)
    for r in [q[2]] + q[4:]:
        x[r] = 7 + rng.integers(0, 2, (8, 16, V))
        for h in range(8):
            x[r, h][:, out[h, ::2]] = 0; x[r, h][:, out[h, 1::2]] = 15
        w[r, 3] = cyc[3, b[r, 3]][None, :]; F[r, 3, 0::2] = np.arange(V); F[r, 3, 1::2] = (2 * np.arange(V)) & (V - 1)
        v = rng.choice(np.array([1, TH - 1, TH, TH + 1, 15, 16]), (8, 1, K)); o = np.argsort(rng.random((8, 16, K)), axis=1)
        y = np.take_along_axis(out[:, None, :], (rng.integers(0, R, (8, 1, K)) + o) % R, 2)
        new = (y + before(w[r])) & (V - 1); old = np.take_along_axis(F[r], w[r], 2)
        np.put_along_axis(F[r], w[r], np.where(o >= v, new, old), 2)
    return pack(F, x, w)
def setup_inputs_crowd(rng):
    cyc = np.argsort(rng.random((8, V)), axis=-1); F = np.stack([follow(rng, cyc)] * N)
    a = int(rng.integers(0, N)); e = (a - 1) % N; p = (a + 1) % N; q = (a + 2) % N
    share = np.tile(np.array([0.0, 0.0, 0.1, 0.0, 0.0, 0.1, 0.1, 0.3]).reshape(1, 8, 1, 1), (N, 1, 1, 1))
    for r in (e, a, p, q): share[r, 7] = 0.0
    share[p] = 0.0; share[q] = 0.0
    F = spoil(rng, F, share)
    x = rng.integers(0, 8, (N, 8, 16, V)); x[:, 7] = rng.integers(0, 16, (N, 16, V))
    b = rng.integers(64, V - 64, (N, 8, K))
    b[:, 3] = 64 + np.argsort(rng.random((N, V - 128)), axis=-1)[:, :K]
    b[:, 7] = H + 64 + np.argsort(rng.random((N, H - 128)), axis=-1)[:, :K]; b[a, 7] = b[a, 7] - H
    w = np.stack([chain(cyc, b[r]) for r in range(N)])
    for g in (0, 1, 2, 4, 5, 6):
        bad = cyc[g, :3]; o = int(cyc[g, 4]); x[:, g, :, o] = 15
        for c in bad: F[:, g, 0::2, c] = o
        for r in range(N):
            if r == p: continue
            k = 2 * rng.integers(0, 8, K); c = bad[rng.integers(0, 3, K)] if g == 6 else np.full(K, bad[0]); j = np.arange(K)
            if g in (4, 5): j = np.delete(j, int(rng.integers(0, K)))
            w[r, g, k[j], j] = c[j]
    o = int(cyc[3, 4]); x[:, 3, :, o] = 15; k0 = int(rng.integers(0, 16))
    for r in range(N):
        k = (k0 + 5 * r) % 16
        F[r, 3, k, w[r, 3, k]] = (o + before(w[r, 3])[k]) & (V - 1)
    out = cyc[7, 8:40]
    for r, whose, t in ((a, e, 1), (q, a, 2)):
        x[r, 7] = 7 + rng.integers(0, 2, (16, V)); x[r, 7][:, out[::2]] = 0; x[r, 7][:, out[1::2]] = 15
        then = chain(cyc[7:], b[whose, 7][None, :] + t)[0]
        v = rng.choice(np.array([TH - 1, TH, TH, TH + 1]), (1, K)); turn = np.argsort(rng.random((16, K)), axis=0)
        y = out[(rng.integers(0, 32, (1, K)) + turn) % 32]
        new = (y + before(then)) & (V - 1); old = np.take_along_axis(F[r, 7], then, 1)
        np.put_along_axis(F[r, 7], then, np.where(turn >= v, new, old), 1)
    for g in (2, 5): w[a, g] = rng.integers(0, V, (16, K))
    w[q, 7, :, int(rng.integers(0, K))] = rng.integers(0, V, 16)
    return pack(F, x, w)
def setup_inputs_ties(rng):
    cyc = np.argsort(rng.random((8, V)), axis=-1); F = np.stack([follow(rng, cyc)] * N)
    r0 = int(rng.integers(0, N)); r1 = (r0 + 1) % N; r2 = (r0 + 2) % N
    sf = rng.choice(np.array([0.05, 0.2, 0.45]), (N, 8, 1, 1)); sw = rng.choice(np.array([0.0, 0.05, 0.2]), (N, 8, 1, K))
    for s in (sf, sw):
        s[r1] = 0.0; s[r2] = 0.0; s[r0, 6:] = 0.0
    F = spoil(rng, F, sf)
    b = rng.integers(0, V, (N, 8, K))
    b[:, 6:] = H + 64 + np.argsort(rng.random((N, 2, H - 128)), axis=-1)[..., :K]; b[r0, 6:] = b[r0, 6:] - H
    w = np.stack([chain(cyc, b[r]) for r in range(N)]); w = spoil(rng, w, sw)
    kind = rng.integers(0, 4, (N, 8, 1, V)); kind[:, 0] = 0
    x = np.take_along_axis(rng.integers(0, 16, (N, 8, 16, 4)), kind, 3)
    w[r1, int(rng.integers(0, 6)), :, int(rng.integers(0, K))] = rng.integers(0, V, 16)
    two = chain(cyc[7:], b[r1, 7, rng.permutation(K)[:2]][None, :] + 1)[0]
    np.put_along_axis(F[r2, 7], two, rng.integers(0, V, (16, 2)), 1)
    for r, g, t in ((r1, 7, 1), (r2, 6, 2)):
        out = cyc[g, 8:40]
        x[r, g] = (7 + rng.integers(0, 2, (16, 4)))[:, kind[r, g, 0]]; x[r, g][:, out[::2]] = 0; x[r, g][:, out[1::2]] = 15
        then = chain(cyc[g:g + 1], b[r0, g][None, :] + t)[0]
        v = rng.choice(np.array([TH - 1, TH, TH, TH + 1]), (1, K)); turn = np.argsort(rng.random((16, K)), axis=0)
        y = out[(rng.integers(0, 32, (1, K)) + turn) % 32]
        new = (y + before(then)) & (V - 1); old = np.take_along_axis(F[r, g], then, 1)
        np.put_along_axis(F[r, g], then, np.where(turn >= v, new, old), 1)
    return pack(F, x, w)
def check_inputs(d):
    bad = []
    for k, hi in (("fld", V * V - 1), ("rec", 15), ("wnd", V - 1)):
        v = np.asarray(d[k]).astype(np.float64)
        if not (np.all(v >= 0) and np.all(v <= hi)): bad.append("range of " + k)
    v = np.asarray(d["rec"]).astype(np.float64)
    if not np.all(v == np.floor(v)): bad.append("whole numbers in rec")
    return bad
def reference(fld, rec, wnd):
    pk = fld.astype(np.int64).reshape(N, 8, 16, H); F = np.concatenate([pk & (V - 1), pk >> LB], axis=3)
    X = rec.astype(np.float32).astype(np.int64).reshape(N, 8, 16, V)
    here = [a for a in wnd.astype(np.int64).reshape(N, 8, 16, K)]
    A = np.zeros(N, np.int64); wt = (2 * np.arange(16) + 1)[None, :, None]
    for t in range(T):
        left = []
        for q in range(N):
            w = here[q]; pv = before(w)
            e = (np.take_along_axis(F[q], w, 2) - pv) & (V - 1)
            x = np.take_along_axis(X[q], e.reshape(8, 1, 16 * K), 2).reshape(8, 16, 16, K)
            M = np.add.reduce(x, axis=2) >> 4
            d = np.add.reduce(np.abs(x - M[:, :, None, :]), axis=1)
            lo = np.argmin(d, axis=1)[:, None, :]; hi = np.argmax(d, axis=1)[:, None, :]
            n = np.take_along_axis(e, lo, 1)
            s = np.add.reduce((e == n).astype(np.int64), axis=1)
            go = s >= TH + (A[q] & 1)
            want = go & (np.take_along_axis(e, hi, 1) != n)[:, 0]
            col = np.take_along_axis(w, hi, 1)[:, 0]; val = ((n + np.take_along_axis(pv, hi, 1)) & (V - 1))[:, 0]
            for g in range(8):
                i = np.flatnonzero(want[g]); c, first = np.unique(col[g, i], return_index=True); i = i[first]
                F[q, g, hi[g, 0, i], c] = val[g, i]
            u = np.add.reduce(M * wt, axis=1); z = ((u * u >> 5) + 37 * u) & (V - 1)
            A[q] = np.count_nonzero(~go)
            left.append(np.where(go[:, None, :], np.concatenate([n, w[:, :15]], axis=1), np.concatenate([z[:, None, :], w[:, 14::-1]], axis=1)))
        here = left if t == T - 1 else [left[(q - 1) % N] for q in range(N)]
    return {"yf": (F[..., :H] + V * F[..., H:]).reshape(N, 128, H).astype(np.float32), "yw": np.stack(here).reshape(N, 128, K).astype(np.float32)}

@@ -1,0 +1,453 @@
+from concourse.mybir import AluOpType as A, ActivationFunctionType as AF
+
+F32, BF, FH, I32, U16 = "float32", "bfloat16", "float16", "int32", "uint16"
+NV = 4
+CH = [0, 32, 64, 96, 128]
+NC = len(CH) - 1
+WT = 1
+XV = 0
+PAD = 256
+SCRATCH = {
+    "fs": ("sbuf", [128, 2048], I32), "U": ("sbuf", [128, PAD + 4096], I32), "fo": ("sbuf", [128, 2048], F32),
+    "r2": ("sbuf", [128, 8192], BF), "wi": ("sbuf", [128, 128], I32), "wo": ("sbuf", [128, 128], F32),
+    "G": ("sbuf", [128, 2048], FH), "X": ("sbuf", [128, 2048], BF), "MX": ("sbuf", [128, 2048], BF),
+    "W16": ("sbuf", [128, 128], FH), "e16": ("sbuf", [128, 128], FH), "off": ("sbuf", [128, 128], U16),
+    "tb": ("sbuf", [128, 128], F32), "Mt": ("sbuf", [128, 128], BF), "Mb": ("sbuf", [128, 128], BF),
+    "D0": ("sbuf", [128, 384], F32), "Nt": ("sbuf", [128, 128], FH), "gG": ("sbuf", [128, 128], BF),
+    "Ig": ("sbuf", [128, 128], BF), "Ih": ("sbuf", [128, 128], BF), "eT": ("sbuf", [128, 152], F32),
+    "R": ("sbuf", [128, 384], F32), "Ni": ("sbuf", [128, 8], I32), "Ri": ("sbuf", [128, 16], I32),
+    "NK": ("sbuf", [128, 16], I32), "NKf": ("sbuf", [128, 16], F32), "low": ("sbuf", [128, 16], I32),
+    "eq": ("sbuf", [128, 128], BF), "Sc": ("sbuf", [128, 128], BF), "go": ("sbuf", [128, 16], BF),
+    "tT": ("sbuf", [128, 128], F32), "ne": ("sbuf", [128, 8], F32), "c2": ("sbuf", [128, 8], F32),
+    "u2": ("sbuf", [128, 8], F32), "cw": ("sbuf", [128, 8], F32), "bC": ("sbuf", [128, 128], FH),
+    "bM": ("sbuf", [128, 128], FH), "nB": ("sbuf", [128, 8], F32), "cB": ("sbuf", [128, 16], F32),
+    "E": ("sbuf", [128, 576], BF), "Rd": ("sbuf", [128, 576], BF), "rr": ("sbuf", [128, 16], F32),
+    "o1": ("sbuf", [128, 8], U16), "gN": ("sbuf", [128, 128], F32), "gK": ("sbuf", [128, 128], BF),
+    "ab": ("sbuf", [128, 128], BF), "sg": ("sbuf", [128, 128], BF), "om": ("sbuf", [128, 128], F32),
+    "nw": ("sbuf", [128, 128], I32), "sq": ("sbuf", [128, 8], F32), "t74": ("sbuf", [128, 8], F32),
+    "yi": ("sbuf", [128, 8], I32), "zi": ("sbuf", [128, 8], I32), "Zt": ("sbuf", [128, 128], FH),
+    "jk": ("sbuf", [128, 8], F32), "Gs": ("sbuf", [128, 8], F32), "ri": ("sbuf", [128, 8], I32),
+    "par": ("sbuf", [128, 8], F32),
+    "pi": ("sbuf", [128, 8], I32), "sc": ("sbuf", [128, 32], F32), "Cm": ("sbuf", [128, 128], F32),
+    "Ck": ("sbuf", [128, 128], BF), "Cg": ("sbuf", [128, 128], BF), "I": ("sbuf", [128, 128], BF),
+    "If": ("sbuf", [128, 128], F32), "Dk": ("sbuf", [128, 2048], BF), "km": ("sbuf", [128, 16], F32),
+    "SoN": ("sbuf", [128, 128], BF), "SoP": ("sbuf", [128, 128], BF), "Sh": ("sbuf", [128, 128], BF),
+    "Rev": ("sbuf", [128, 128], BF), "J": ("sbuf", [128, 128], BF), "BN": ("sbuf", [128, 128], BF),
+    "m16": ("sbuf", [128, 128], BF), "rst": ("sbuf", [128, 128], BF), "T0": ("sbuf", [128, 128], BF),
+    "B8": ("sbuf", [128, 8], BF), "B8P": ("sbuf", [128, 8], BF), "B8N": ("sbuf", [128, 8], BF),
+    "wt": ("sbuf", [128, 8], BF), "SR": ("sbuf", [128, 128], BF), "Dm": ("sbuf", [128, 128], BF),
+    "Inz": ("sbuf", [128, 128], BF), "I16": ("sbuf", [128, 128], BF), "IN": ("sbuf", [128, 128], BF),
+    "Iod": ("sbuf", [128, 128], BF), "dm": ("sbuf", [128, 576], BF), "cd": ("sbuf", [128, 8], F32),
+    "C1": ("sbuf", [128, 384], BF), "cm": ("sbuf", [128, 64], BF), "c2k": ("sbuf", [128, 64], BF),
+    "zr": ("sbuf", [128, 128], BF), "on": ("sbuf", [128, 128], BF), "bc": ("sbuf", [128, 8], U16),
+    "en": ("sbuf", [128, 2], U16),
+}
+for _t in range(NV):
+    SCRATCH["Wu%d" % _t] = ("sbuf", [128, 128], U16)
+for _t in range(1, NV):
+    SCRATCH["Ws%d" % _t] = ("sbuf", [128, 128], U16)
+for _b in ("PY", "PA", "PB", "PM", "PK", "PD", "PT", "PW"):
+    SCRATCH[_b] = ("psum", [128, 512], F32)
+NDMA = 20
+SEMAPHORES = ["sV", "sS", "sP", "sG", "sent", "arr1", "arr2", "arr3"] + ["d%d" % i for i in range(NDMA)]
+MAGIC = 12582912.0
+BIG = 67108864.0
+
+
+def emit(g, T, ops):
+    q = {"V": g.vector, "S": g.scalar, "P": g.tensor, "G": g, "Y": g.sync}
+    wr, rd, bank = {}, {}, {}
+    pos = {e: 0 for e in "VSPG"}
+    known = {e: ({x: 0 for x in "VSPG"}, set()) for e in q}
+    last = {}
+    for i, o in enumerate(ops):
+        e = o["e"]
+        deps = set()
+        for k in o["r"]:
+            if k in wr: deps.add(wr[k])
+        for k in o["w"]:
+            if k in wr: deps.add(wr[k])
+            deps.update(rd.get(k, ()))
+        for b in o["b"]:
+            for x, j in bank.setdefault(b, {}).items():
+                if x != e: deps.add(j)
+        o["waits"] = []
+        if o["kind"] != "arrive":
+            kc, kd = known[e]
+            for j in sorted(deps, reverse=True):
+                p = ops[j]
+                if p["kind"] == "op":
+                    if p["e"] == "P" and e == "P": continue
+                    if kc[p["e"]] >= p["pos"]: continue
+                    kc[p["e"]] = p["pos"]
+                    p["sig"] = True
+                else:
+                    if j in kd: continue
+                    kd.add(j)
+                o["waits"].append(j)
+                if p["kind"] != "arrive":
+                    for x in "VSPG": kc[x] = max(kc[x], p["kc"][x])
+                    kd.update(p["kd"])
+            o["kc"], o["kd"] = dict(kc), set(kd)
+        if o["kind"] == "op":
+            pos[e] += 1
+            o["pos"] = pos[e]
+            last[e] = o
+        for k in o["r"]: rd.setdefault(k, []).append(i)
+        for k in o["w"]:
+            wr[k] = i
+            rd[k] = []
+        for b in o["b"]: bank[b][e] = i
+    for o in last.values(): o["sig"] = True
+    cnt = {e: 0 for e in "VSPG"}
+    nd, sent = 0, 0
+    for o in ops:
+        if o["kind"] == "op" and o.get("sig"):
+            cnt[o["e"]] += 1
+            o["sem"], o["val"] = T.sem["s" + o["e"]], cnt[o["e"]]
+        elif o["kind"] == "dma":
+            o["sem"], o["val"] = T.sem["d%d" % nd], 16
+            nd += 1
+    for o in ops:
+        if o["kind"] == "arrive": continue
+        for j in o["waits"]:
+            q[o["e"]].wait_ge(ops[j]["sem"], ops[j]["val"])
+        ins = o["f"]()
+        if o["kind"] == "send": sent += o["val"]
+        elif o["kind"] == "dma": ins.then_inc(o["sem"], 16)
+        elif o.get("sig"): ins.then_inc(o["sem"], 1)
+    for e in "VSPG":
+        g.wait_ge(T.sem["s" + e], cnt[e])
+    if sent: g.wait_ge(T.sem.sent, sent)
+    for o in ops:
+        if o["kind"] == "dma": g.wait_ge(o["sem"], 16)
+
+
+def rank_program(g, core, T, topo):
+    rank = T.rank_of(core)
+    if rank is None:
+        return
+    n = len(T.cores)
+    nxt, prv = T.cores[(rank + 1) % n], T.cores[(rank - 1) % n]
+    eng_out = topo.engines(core, nxt)[::2]
+    n_in = len(topo.engines(prv, core)[::2])
+    mask_out = sum(1 << x for x in eng_out)
+    rid, pid = topo.addr(nxt)[0], topo.addr(nxt)[1]
+    v, s, pe = g.vector, g.scalar, g.tensor
+    ops = []
+
+    def op(e, f, r, w, b=(), kind="op", **kw):
+        d = {"e": e, "f": f, "r": list(r), "w": list(w), "b": list(b), "kind": kind}
+        d.update(kw)
+        ops.append(d)
+
+    def ts(out, in0, s1, s2, o0, o1, r, w, b=()):
+        if s2 is None: op("V", lambda: v.tensor_scalar(out, in0, s1, None, o0), r, w, b)
+        else: op("V", lambda: v.tensor_scalar(out, in0, s1, s2, o0, o1), r, w, b)
+
+    def tt(out, a, c, o, r, w, b=()):
+        op("V", lambda: v.tensor_tensor(out, a, c, o), r, w, b)
+
+    def cp(out, a, r, w, b=()):
+        op("V", lambda: v.tensor_copy(out, a), r, w, b)
+
+    def scan(out, d0, d1, o0, o1, r, w, b=()):
+        op("V", lambda: v.tensor_tensor_scan(out, d0, d1, 0.0, o0, o1), r, w, b)
+
+    def ms(out, c, w):
+        op("V", lambda: v.memset(out, c), [], w)
+
+    def act(out, a, r, w, b=(), f=AF.Identity, bias=0.0, scale=1.0, acc=None):
+        if acc is None: op("S", lambda: s.activation(out, a, f, bias=bias, scale=scale), r, w, b)
+        else: op("S", lambda: s.activation(out, a, f, bias=bias, scale=scale, accum_out=acc), r, w, b)
+
+    def mm(out, l, rh, st, sp, r, w, b):
+        op("P", lambda: pe.matmul(out, l, rh, st, sp), r, w, [b])
+
+    def dma(e, out, a, r, w):
+        qq = g.sync if e == "Y" else g.scalar
+        op(e, lambda: qq.dma_start(out, a), r, w, kind="dma")
+
+    def col(i):
+        return T.sc[:, i:i + 1]
+
+    FC = [0, 256, 640, 1152, 1664, 2048]
+    UK = ["U%d" % i for i in range(2 * len(FC) - 2)] + ["Ud"]
+    LO, HI = PAD, PAD + 2048
+
+    dma("S", T.wi[:], T.wnd[:], [], ["wi"])
+    for c in range(len(FC) - 1):
+        dma("Y", T.fs[:, FC[c]:FC[c + 1]], T.fld[:, FC[c]:FC[c + 1]], [], ["fs%d" % c])
+    for c in range(2):
+        dma("Y", T.r2[:, 2048 * c:2048 * c + 2048], T.rec[:, 2048 * c:2048 * c + 2048], [], ["ra%d" % c])
+    op("Y", lambda: g.sync.dma_start(T.r2[:, 4096:8192], T.rec[:, :]), ["ra0", "ra1"], ["rb"], kind="dma")
+
+    op("G", lambda: g.iota(T.pi[:, 0:1], [[0, 1]], 0, 1), [], ["pi0"])
+    op("G", lambda: g.iota(T.Cm[:], [[1, 128]], 0, 0, allow_small_or_imprecise_dtypes=True), [], ["Cm"])
+    op("G", lambda: g.iota(T.Ck[:], [[0, 8], [1, 16]], 0, 0, allow_small_or_imprecise_dtypes=True), [], ["Ck"])
+    op("G", lambda: g.iota(T.Cg[:], [[1, 8], [0, 16]], 0, 0, allow_small_or_imprecise_dtypes=True), [], ["Cg"])
+    ms(T.C1[:, 0:128], -4096.0, ["C1a"]); ms(T.C1[:, 128:384], 4096.0, ["C1b"])
+    ms(T.zr[:], 0.0, ["zr"]); ms(T.on[:], 1.0, ["on"]); ms(T.cm[:], -15.0 / 32, ["cm"]); ms(T.c2k[:], 2048.0, ["c2k"])
+    ts(T.pi[:, 1:2], T.pi[:, 0:1], 15, None, A.bitwise_and, None, ["pi0"], ["pi1"])
+    ts(T.pi[:, 2:3], T.pi[:, 0:1], 4, None, A.logical_shift_right, None, ["pi0"], ["pi2"])
+    ts(T.pi[:, 3:4], T.pi[:, 0:1], 1, None, A.bitwise_and, None, ["pi0"], ["pi3"])
+    ms(T.C1[:, 0:128:16], BIG, ["C1a"]); ms(T.C1[:, 128:384:16], -BIG, ["C1b"])
+    cp(T.sc[:, 0:4], T.pi[:, 0:4], ["pi0", "pi1", "pi2", "pi3"], ["s0"])
+    ms(T.U[:, 0:PAD], 0, ["Ud"]); ms(T.par[:], 0.0, ["par"]); ms(T.cB[:], 0.0, ["cB"])
+    P_, K_, G_, O_ = 0, 1, 2, 3
+    for i, (src, sc_, bi) in {4: (P_, 1.0, 1.0), 5: (O_, 1.0, -1.0), 6: (P_, -1.0, 127.0), 7: (P_, 1.0, 15.0),
+                              9: (K_, -1.0, 15.0), 10: (K_, 8192.0, -15.0 * 8192), 11: (O_, -2048.0, 0.0),
+                              12: (P_, -2.0, float(PAD)), 13: (P_, 2.0, -2048.0 - PAD), 14: (K_, 2.0, 1.0),
+                              15: (K_, 2.0, 0.0)}.items():
+        act(col(i), col(src), ["s0"], ["s%d" % i], bias=bi, scale=sc_)
+    act(col(8), col(K_), ["s0", "s7"], ["s8"], bias=col(7), scale=-2.0)
+    act(col(16), col(9), ["s9"], ["s16"], f=AF.Sign)
+    act(col(17), col(K_), ["s0"], ["s17"], f=AF.Sign)
+    ts(T.I[:], T.Cm[:], col(P_), None, A.is_equal, None, ["Cm", "s0"], ["I"])
+    ts(T.km[:], T.Cm[:, 0:16], col(K_), None, A.is_equal, None, ["Cm", "s0"], ["km"])
+    ts(T.SoN[:], T.Cm[:], col(4), col(5), A.is_equal, A.mult, ["Cm", "s4", "s5"], ["SoN"])
+    ts(T.B8[:], T.Cm[:, 0:8], col(G_), None, A.is_equal, None, ["Cm", "s0"], ["B8"])
+    ts(T.T0[:], T.Cm[:], col(9), 1048576.0, A.is_le, A.mult, ["Cm", "s9"], ["T0"])
+    ts(col(18), col(K_), 7.0, 1.5, A.min, A.add, ["s0"], ["s18"])
+    cp(T.bc[:], T.Cm[:, 0:8], ["Cm"], ["bc"])
+    cp(T.Zt[:], T.zr[:], ["zr"], ["Zt"])
+    cp(T.Nt[:], T.zr[:], ["zr"], ["Nt"])
+    cp(T.Wu0[:], T.wi[:], ["wi"], ["Wu0"])
+    for k in range(16):
+        act(T.Dk[:, 128 * k:128 * k + 128], T.I[:], ["I", "km"], ["Dk%d" % k], scale=T.km[:, k:k + 1])
+    act(col(19), col(18), ["s18"], ["s19"], f=AF.Square)
+    act(T.I16[:], T.I[:], ["I"], ["I16"], scale=1.0 / 16)
+    act(T.If[:], T.I[:], ["I"], ["If"])
+    act(T.IN[:], T.I[:], ["I"], ["IN"], scale=-1.0)
+    act(T.Ig[:], T.I[:], ["I"], ["Ig"], scale=16384.0)
+    act(T.Ih[:], T.I[:], ["I"], ["Ih"], scale=-4096.0)
+    act(T.Iod[:], T.I[:], ["I", "s11"], ["Iod"], scale=col(11))
+    act(T.Inz[:], T.I[:], ["I", "s17"], ["Inz"], scale=col(17))
+    act(T.SoP[:], T.SoN[:], ["SoN"], ["SoP"], scale=-1.0)
+    act(T.B8P[:], T.B8[:], ["B8"], ["B8P"], scale=131072.0)
+    act(T.B8N[:], T.B8[:], ["B8"], ["B8N"], scale=-65536.0)
+    act(T.wt[:], T.B8[:], ["B8", "s14"], ["wt"], scale=col(14))
+    act(T.cd[:], T.Cm[:, 0:8], ["Cm", "s15"], ["cd"], bias=col(15), scale=32.0)
+    for h in range(8):
+        st = 8 * h * (h + 1)
+        act(T.dm[:, st:st + 16 * h + 16], T.T0[:, 0:16 * h + 16], ["T0", "cd"], ["dm%d" % h], bias=T.cd[:, h:h + 1])
+
+    late = [
+        lambda: ts(T.Sh[:], T.Cm[:], col(4), col(16), A.is_equal, A.mult, ["Cm", "s4", "s16"], ["Sh"]),
+        lambda: ts(T.Rev[:], T.Cm[:], col(8), col(16), A.is_equal, A.mult, ["Cm", "s8", "s16"], ["Rev"]),
+        lambda: ts(T.J[:], T.Cm[:], col(6), None, A.is_equal, None, ["Cm", "s6"], ["J"]),
+        lambda: ts(T.BN[:], T.Cg[:], col(G_), -65536.0, A.is_equal, A.mult, ["Cg", "s0"], ["BN"]),
+        lambda: ts(T.m16[:], T.Ck[:], col(K_), None, A.is_equal, None, ["Ck", "s0"], ["m16"]),
+        lambda: ts(T.rst[:], T.Ck[:], 0.0, None, A.not_equal, None, ["Ck"], ["rst"]),
+        lambda: tt(T.Dm[:], T.Sh[:], T.Inz[:], A.subtract, ["Sh", "Inz"], ["Dm"]),
+        lambda: tt(T.SR[:], T.Sh[:], T.Rev[:], A.subtract, ["Sh", "Rev"], ["SR"]),
+        lambda: ts(T.en[:, 0:1], col(19), 8.0, -3.0, A.mult, A.add, ["s19"], ["en"]),
+    ]
+
+    def filler(cnt):
+        for _ in range(min(cnt, len(late))): late.pop(0)()
+
+    for c in range(len(FC) - 1):
+        a, b = FC[c], FC[c + 1]
+        ts(T.U[:, LO + a:LO + b], T.fs[:, a:b], 4095, None, A.bitwise_and, None, ["fs%d" % c], ["U%d" % (2 * c)])
+        ts(T.U[:, HI + a:HI + b], T.fs[:, a:b], 12, None, A.logical_shift_right, None, ["fs%d" % c], ["U%d" % (2 * c + 1)])
+
+    for t in range(NV):
+        Wu, wk = T["Wu%d" % t], "Wu%d" % t
+        if t:
+            op("V", None, [], [wk], kind="arrive", sem=T.sem["arr%d" % t], val=n_in)
+
+        def fgather(c):
+            a, b = CH[c], CH[c + 1]
+            ts(T.G[:, 16 * a:16 * b], T.U[:, LO:LO + 4096].indirect(Wu[:, a:b]), -2048.0, None,
+               A.add, None, UK + [wk], ["G%d" % c])
+
+        def extract(c):
+            a, b = CH[c], CH[c + 1]
+            y = T.PY[:, a:b]
+            mm(y, T.SoN[:], T.c2k[:, 0:b - a], True, False, ["SoN", "c2k"], ["Y%d" % c], "PY")
+            if c: mm(y, T.SoN[:], T.W16[:, a:b], False, False, ["W16"], ["Y%d" % c], "PY")
+            for k in range(16):
+                mm(y, T.Dk[:, 128 * k:128 * k + 128], T.G[:, 16 * a + k:16 * b:16], False, k == 15 and c > 0,
+                   ["Dk%d" % k, "G%d" % c], ["Y%d" % c], "PY")
+            if not c: mm(y, T.SoN[:], T.W16[:, a:b], False, True, ["W16"], ["Y0"], "PY")
+
+        def names(c):
+            a, b = CH[c], CH[c + 1]
+            sl = slice(a, b)
+            if t:
+                ts(T.off[:, sl], T.PY[:, sl], 6144.0, None, A.add, None, ["Y%d" % c], ["off%d" % c], ["PY"])
+                win, rk = T.r2[:, 0:8192], ["ra0", "ra1", "rb"]
+            else:
+                ts(T.tb[:, sl], T.PY[:, sl], -2048.0, 4096.0, A.is_lt, A.mult, ["Y%d" % c], ["tb%d" % c], ["PY"])
+                if c < 3: filler(1)
+                tt(T.e16[:, sl], T.PY[:, sl], T.tb[:, sl], A.add, ["Y%d" % c, "tb%d" % c], ["e%d" % c], ["PY"])
+                if c < 3: filler(1)
+                ts(T.off[:, sl], T.e16[:, sl], 2048.0, None, A.add, None, ["e%d" % c], ["off%d" % c])
+                win, rk = T.r2[:, 0:4096], ["ra0", "ra1"]
+            m = b - XV if c == NC - 1 else b
+            if m > a: act(T.X[:, 16 * a:16 * m], win.indirect(T.off[:, a:m]), rk + ["off%d" % c], ["X%d" % c])
+            if m < b: cp(T.X[:, 16 * m:16 * b], win.indirect(T.off[:, m:b]), rk + ["off%d" % c], ["Xv"])
+
+        def wthings():
+            mm(T.PK[:, 0:128], T.I[:], T.zr[:], True, False, ["I", "zr"], ["K"], "PK")
+            mm(T.PD[:, 0:384], T.I[:], T.C1[:], True, False, ["C1a", "C1b"], ["D"], "PD")
+            mm(T.PD[:, 256:384], T.W16[:], T.Dm[:], False, False, ["W16", "Dm"], ["D"], "PD")
+            mm(T.PT[:, 272:280], T.W16[:], T.I[:, 15::16], True, True, ["W16"], ["Te"], "PT")
+            mm(T.PW[:, 0:128], T.Rev[:], T.W16[:], True, False, ["W16", "Rev"], ["WN"], "PW")
+
+        def total(hf):
+            ps, b = (T.PA, "PA") if hf == 0 else (T.PB, "PB")
+            mm(ps[:, 0:64], T.I[:], T.cm[:], True, False, ["cm"], ["S%d" % hf, "cS" if hf == 0 else "QK"], b)
+            for k in range(16):
+                mm(ps[:, 0:64], T.I16[:], T.X[:, 1024 * hf + k:1024 * hf + 1024:16], False, k == 15,
+                   ["I16"] + XH[hf], ["S%d" % hf], b)
+
+        def mx(k, lo, hi):
+            return T.MX[:, 128 * k + lo:128 * k + hi]
+
+        def mean(hf):
+            ps, b = (T.PA, "PA") if hf == 0 else (T.PB, "PB")
+            sl = slice(64 * hf, 64 * hf + 64)
+            ts(T.PM[:, sl], ps[:, 0:64], MAGIC, -MAGIC, A.add, A.add, ["S%d" % hf], ["M%d" % hf], [b, "PM"])
+            act(T.Mt[:, sl], ps[:, 0:64], ["S%d" % hf], ["Mt%d" % hf], [b], bias=192.0)
+            act(T.Mb[:, sl], T.Mt[:, sl], ["Mt%d" % hf], ["Mb%d" % hf], bias=-192.0)
+
+        def larger(hf, k):
+            tt(mx(k, 64 * hf, 64 * hf + 64), T.X[:, 1024 * hf + k:1024 * hf + 1024:16],
+               T.PM[:, 64 * hf:64 * hf + 64], A.max, XH[hf] + ["M%d" % hf], ["MX%d_%d" % (hf, k)], ["PM"])
+
+        EK = ["e%d" % c for c in range(NC)]
+        YK = ["Y%d" % c for c in range(NC)]
+        XH = [["X%d" % c for c in range(NC) if CH[c] < 64], ["X%d" % c for c in range(NC) if CH[c + 1] > 64] + ["Xv"]]
+        XK = XH[0] + XH[1]
+        fgather(0)
+        ts(T.W16[:], Wu[:], -2048.0, None, A.add, None, [wk], ["W16"])
+        extract(0)
+        for c in range(1, NC):
+            fgather(c); names(c - 1)
+            extract(c)
+            if t and c == WT: wthings()
+        if t:
+            ts(T.ri[:, 0:1], T.Gs[:, 0:1], 0.5, -0.25, A.mult, A.add, ["Gs"], ["ri"])
+            ts(T.par[:, 0:1], T.ri[:, 0:1], -2.0, T.Gs[:, 0:1], A.mult, A.add, ["Gs", "ri"], ["par"])
+        else:
+            filler(99)
+        names(NC - 1)
+        total(0)
+        if t:
+            ts(T.tb[:], T.PY[:, 0:128], -2048.0, 4096.0, A.is_lt, A.mult, YK, ["tb"], ["PY"])
+            tt(T.e16[:], T.PY[:, 0:128], T.tb[:], A.add, YK + ["tb"], EK, ["PY"])
+        else:
+            wthings()
+        mean(0)
+        mm(T.PD[:, 0:128], T.e16[:], T.Dm[:], False, False, EK + ["Dm"], ["D"], "PD")
+        mm(T.PD[:, 128:256], T.e16[:], T.Dm[:], False, True, EK, ["D"], "PD")
+        mm(T.PT[:, 128:256], T.e16[:], T.I[:], True, True, EK, ["Te"], "PT")
+        mm(T.PT[:, 256:264], T.e16[:], T.I[:, 15::16], True, True, EK, ["Te"], "PT")
+        mm(T.PT[:, 264:272], T.e16[:], T.I[:, 15::16], True, True, EK, ["Te"], "PT")
+        total(1)
+        for k in range(16):
+            mm(T.PK[:, k:128:16], T.X[:, k::16], T.B8N[:], False, False, XK + ["B8N"], ["K"], "PK")
+        for k in range(16): larger(0, k)
+        act(T.eT[:], T.PT[:, 128:280], ["Te"], ["eT"], ["PT"], bias=2048.0)
+        mean(1)
+        act(T.D0[:], T.PD[:, 0:384], ["D"], ["D0"], ["PD"])
+        for k in range(16):
+            larger(1, k)
+            mm(T.PK[:, k:128:16], mx(k, 0, 128), T.B8P[:], False, k == 15,
+               ["MX0_%d" % k, "MX1_%d" % k, "B8P"], ["K"], "PK")
+            if k == 4:
+                mm(T.PT[:, 288:296], T.Mb[:], T.wt[:], True, True, ["Mb0", "Mb1", "wt"], ["Tu"], "PT")
+                mm(T.PK[:, 0:128], T.Mb[:], T.BN[:], False, False, ["Mb0", "Mb1", "BN"], ["K"], "PK")
+                act(T.sq[:], T.PT[:, 288:296], ["Tu"], ["sq"], ["PT"], f=AF.Square, scale=0.25)
+                act(T.t74[:], T.PT[:, 288:296], ["Tu"], ["t74"], ["PT"], bias=-0.25, scale=74.0)
+        tt(T.yi[:], T.sq[:], T.t74[:], A.add, ["sq", "t74"], ["yi"])
+        key = T.PK[:, 0:128]
+        bc = T.bc[:, 0:8]
+        scan(T.R[:, 0:128], T.D0[:, 0:128], key, A.add, A.min, ["K", "D0"], ["R0"], ["PK"])
+        ts(T.zi[:], T.yi[:], 1, 4095, A.logical_shift_right, A.bitwise_and, ["yi"], ["zi"])
+        tt(T.Ni[:], T.R[:, 15:128:16], T.eT[:, 128:136], A.add, ["R0", "eT"], ["Ni"])
+        scan(T.R[:, 128:256], T.D0[:, 128:256], key, A.add, A.max, ["K", "D0"], ["R1"], ["PK"])
+        ts(T.NK[:, 0:8], T.Ni[:], 4095, None, A.bitwise_and, None, ["Ni"], ["n"])
+        ts(T.Zt[:, 0::16], T.zi[:], -2048.0, None, A.add, None, ["zi"], ["Zt"])
+        mm(T.PW[:, 0:128], T.Zt[:], T.I[:], False, False, ["Zt"], ["WN"], "PW")
+        tt(T.eq[:], T.NK[:, 0:8].indirect(bc), T.eT[:, 0:128], A.is_equal, ["n", "bc", "eT"], ["eq"])
+        mm(T.PD[:, 0:128], T.SR[:], T.W16[:], True, False, ["W16", "SR"], ["D"], "PD")
+        mm(T.PD[:, 0:128], T.Zt[:], T.IN[:], False, False, ["Zt", "IN"], ["D"], "PD")
+        ts(T.Nt[:, 0::16], T.NK[:, 0:8], -2048.0, None, A.add, None, ["n"], ["Nt"])
+        mm(T.PD[:, 0:128], T.Nt[:], T.I[:], False, False, ["Nt"], ["D"], "PD")
+        scan(T.R[:, 256:384], T.D0[:, 256:384], key, A.add, A.max, ["K", "D0"], ["R2"], ["PK"])
+        scan(T.Sc[:], T.rst[:], T.eq[:], A.mult, A.add, ["rst", "eq"], ["Sc"])
+        tt(T.Ri[:], T.R[:, 143:384:16], T.eT[:, 136:152], A.add, ["R1", "R2", "eT"], ["Ri"])
+        ts(T.go[:, 0:8], T.Sc[:, 15::16], T.par[:, 0:1], 4.0, A.subtract, A.is_ge, ["Sc", "par"], ["go"])
+        act(T.gG[:], T.go[:, 0:8].indirect(bc), ["go", "bc"], ["gG"])
+        mm(T.PD[:, 0:128], T.gG[:], T.Ig[:], False, True, ["gG", "Ig"], ["D"], "PD")
+        mm(T.PW[:, 0:128], T.gG[:], T.Ih[:], False, False, ["gG", "Ih"], ["WN"], "PW")
+        ts(T.low[:], T.Ri[:], 4095, None, A.bitwise_and, None, ["Ri"], ["low"])
+        ts(T.NK[:, 8:16], T.Ri[:, 0:8], 12, 15, A.logical_shift_right, A.bitwise_and, ["Ri"], ["kk"])
+        tt(T.ne[:], T.NK[:, 0:8], T.low[:, 0:8], A.not_equal, ["n", "low"], ["ne"])
+        ts(T.c2[:], T.low[:, 8:16], col(12), None, A.add, None, ["low", "s12"], ["c2"])
+        cp(T.NKf[:], T.NK[:], ["n", "kk"], ["NKf"])
+        tt(T.u2[:], T.c2[:], T.ne[:], A.mult, ["c2", "ne"], ["u2"])
+        act(T.tT[:], T.PD[:, 0:128], ["D"], ["tT"], ["PD"], f=AF.Relu, bias=-12288.0)
+        mm(T.PW[:, 0:128], T.If[:], T.tT[:], False, True, ["tT", "If"], ["WN"], "PW")
+        act(T.gK[:], T.NKf[:, 8:16].indirect(bc), ["NKf", "bc"], ["gK"])
+        act(T.gN[:], T.NKf[:, 0:8].indirect(bc), ["NKf", "bc"], ["gN"])
+        tt(T.cw[:], T.go[:, 0:8], T.u2[:], A.mult, ["go", "u2"], ["cw"])
+        ts(T.bC[:], T.cw[:, 0:8].indirect(bc), col(13), None, A.add, None, ["cw", "bc", "s13"], ["bC"])
+        tt(T.bM[:], T.bC[:], T.m16[:], A.mult, ["bC", "m16"], ["bM"])
+        if t < NV - 1:
+            ws = T["Ws%d" % (t + 1)]
+            ts(ws[:], T.PW[:, 0:128], 2048.0, None, A.add, None, ["WN"], ["Ws%d" % t], ["PW"])
+            op("G", lambda ws=ws, t=t: g.remote_dma(T["Wu%d" % (t + 1)][:], ws[:], T.sem["arr%d" % (t + 1)], T.sem.sent,
+                                                   pid, rid, mask_out), ["Ws%d" % t], [], kind="send", val=len(eng_out))
+        mm(T.PY[:, 0:128], T.bC[:], T.J[:], True, True, ["bC", "J"], YK, "PY")
+        mm(T.PA[:, 0:128], T.bC[:], T.J[:], True, True, ["bC"], ["cS", "S0"], "PA")
+        mm(T.PA[:, 128:136], T.bM[:], T.B8[:], True, True, ["bM", "B8"], ["bS"], "PA")
+        mm(T.PY[:, 128:136], T.bM[:], T.B8[:], True, True, ["bM"], ["bV"], "PY")
+        mm(T.PB[:, 0:128], T.gK[:], T.I[:], True, True, ["gK"], ["QK"], "PB")
+        mm(T.PD[:, 0:128], T.gN[:], T.If[:], True, False, ["gN"], ["D"], "PD")
+        mm(T.PD[:, 0:128], T.SoP[:], T.W16[:], False, True, ["SoP", "W16"], ["D"], "PD")
+        mm(T.PK[:, 0:128], T.gN[:], T.If[:], True, False, ["gN"], ["K"], "PK")
+        mm(T.PK[:, 0:128], T.SoP[:], T.W16[:], False, False, ["SoP", "W16"], ["K"], "PK")
+        act(T.nB[:], T.PA[:, 128:136], ["bS"], ["nB"], ["PA"], scale=-8192.0)
+        for h in range(7, -1, -1):
+            st, ln = 8 * h * (h + 1), 16 * h + 16
+            if h >= 4:
+                ts(T.E[:, st:st + ln], T.PY[:, 128 - ln:128], T.PY[:, 128 + h:129 + h], 8192.0, A.not_equal, A.mult,
+                   ["Y0", "bV"], ["E%d" % h], ["PY"])
+            else:
+                act(T.E[:, st:st + ln], T.PA[:, 128 - ln:128], ["cS", "nB"], ["E%d" % h], ["PA"], f=AF.Abs,
+                    bias=T.nB[:, h:h + 1], scale=8192.0)
+        act(T.cB[:, 0:8], T.PA[:, 128:136], ["bS"], ["cB"], ["PA"], bias=2048.0 + PAD)
+        act(T.ab[:], T.PB[:, 0:128], ["QK", "s10"], ["ab"], ["PB"], f=AF.Abs, bias=col(10), scale=8192.0)
+        act(T.sg[:], T.PD[:, 0:128], ["D"], ["sg"], ["PD"], f=AF.Sign, bias=-2047.5)
+        mm(T.PK[:, 0:128], T.IN[:], T.ab[:], False, False, ["IN", "ab"], ["K"], "PK")
+        mm(T.PK[:, 0:128], T.Iod[:], T.sg[:], False, True, ["Iod", "sg"], ["K"], "PK")
+        if t < NV - 1:
+            mm(T.PT[:, 304:312], T.on[:], T.go[:, 0:8], True, True, ["on", "go"], ["Tc"], "PT")
+            act(T.jk[:], T.PT[:, 304:312], ["Tc"], ["jk", "Gs"], ["PT"], acc=T.Gs[:, 0:1])
+        else:
+            act(T.wo[:], T.PW[:, 0:128], ["WN"], ["wo"], ["PW"], bias=2048.0)
+            dma("Y", T.yw[:], T.wo[:], ["wo"], [])
+        scan(T.Rd[:], T.E[:], T.dm[:], A.min, A.max, ["E%d" % h for h in range(8)] + ["dm%d" % h for h in range(8)], ["Rd"])
+        tt(T.rr[:], T.Rd[:].indirect(T.en[:, 0:1]), T.cB[:], A.min, ["Rd", "en", "cB"], ["rr"])
+        cp(T.o1[:], T.rr[:, 0:8], ["rr"], ["o1"])
+        tt(T.om[:], T.U[:].indirect(T.o1[:]), T.ab[:], A.min, UK + ["o1", "ab"], ["om"])
+        tt(T.nw[:], T.om[:], T.PK[:, 0:128], A.max, ["om", "K"], ["nw"], ["PK"])
+        cp(T.U[:].indirect(T.o1[:]), T.nw[:], ["o1", "nw"], UK)
+
+    cuts = [0, 384, 896, 1408, 1792, 2048]
+    def high(c):
+        a, b = cuts[c], cuts[c + 1]
+        ps, bk = (T.PM, "PM") if c % 2 == 0 else (T.PK, "PK")
+        ts(ps[:, 0:b - a], T.U[:, HI + a:HI + b], 4096.0, None, A.mult, None, UK, ["H%d" % (c % 2)], [bk])
+    high(0)
+    for c in range(len(cuts) - 1):
+        a, b = cuts[c], cuts[c + 1]
+        ps, bk = (T.PM, "PM") if c % 2 == 0 else (T.PK, "PK")
+        if c + 2 < len(cuts): high(c + 1)
+        tt(T.fo[:, a:b], T.U[:, LO + a:LO + b], ps[:, 0:b - a], A.add, UK + ["H%d" % (c % 2)], ["fo%d" % c], [bk])
+        dma("Y" if c % 2 == 0 else "S", T.yf[:, a:b], T.fo[:, a:b], ["fo%d" % c], [])
+    emit(g, T, ops)

@@ -1,10 +1,13 @@
+from concourse.bass import DstId, RemoteDMATransfer
 from concourse.mybir import AluOpType as A, ActivationFunctionType as AF
 
 F32, BF, FH, I32, U16 = "float32", "bfloat16", "float16", "int32", "uint16"
 NV = 4
 CH = [0, 32, 64, 96, 128]
 NC = len(CH) - 1
-WT = 1
+MP = 13
+HV = 3
+XV0 = 0
 XV = 0
 PAD = 256
 SCRATCH = {
@@ -18,11 +21,13 @@ SCRATCH = {
     "R": ("sbuf", [128, 384], F32), "Ni": ("sbuf", [128, 8], I32), "Ri": ("sbuf", [128, 16], I32),
     "NK": ("sbuf", [128, 16], I32), "NKf": ("sbuf", [128, 16], F32), "low": ("sbuf", [128, 16], I32),
     "eq": ("sbuf", [128, 128], BF), "Sc": ("sbuf", [128, 128], BF), "go": ("sbuf", [128, 16], BF),
-    "tT": ("sbuf", [128, 128], F32), "ne": ("sbuf", [128, 8], F32), "c2": ("sbuf", [128, 8], F32),
+    "b2": ("sbuf", [128, 8], U16), "nth": ("sbuf", [128, 8], F32),
+    "tT": ("sbuf", [128, 256], F32), "ne": ("sbuf", [128, 8], F32), "c2": ("sbuf", [128, 8], F32),
     "u2": ("sbuf", [128, 8], F32), "cw": ("sbuf", [128, 8], F32), "bC": ("sbuf", [128, 128], FH),
-    "bM": ("sbuf", [128, 128], FH), "nB": ("sbuf", [128, 8], F32), "cB": ("sbuf", [128, 16], F32),
+    "cf": ("sbuf", [128, 8], FH), "B8f": ("sbuf", [128, 8], F32),
+    "bM": ("sbuf", [128, 128], F32), "nB": ("sbuf", [128, 8], F32), "cB": ("sbuf", [128, 16], F32),
     "E": ("sbuf", [128, 576], BF), "Rd": ("sbuf", [128, 576], BF), "rr": ("sbuf", [128, 16], F32),
-    "o1": ("sbuf", [128, 8], U16), "gN": ("sbuf", [128, 128], F32), "gK": ("sbuf", [128, 128], BF),
+    "o1": ("sbuf", [128, 8], U16), "o0": ("sbuf", [128, 8], U16), "gN": ("sbuf", [128, 128], F32), "gK": ("sbuf", [128, 128], BF),
     "ab": ("sbuf", [128, 128], BF), "sg": ("sbuf", [128, 128], BF), "om": ("sbuf", [128, 128], F32),
     "nw": ("sbuf", [128, 128], I32), "sq": ("sbuf", [128, 8], F32), "t74": ("sbuf", [128, 8], F32),
     "yi": ("sbuf", [128, 8], I32), "zi": ("sbuf", [128, 8], I32), "Zt": ("sbuf", [128, 128], FH),
@@ -35,7 +40,7 @@ SCRATCH = {
     "Rev": ("sbuf", [128, 128], BF), "J": ("sbuf", [128, 128], BF), "BN": ("sbuf", [128, 128], BF),
     "m16": ("sbuf", [128, 128], BF), "rst": ("sbuf", [128, 128], BF), "T0": ("sbuf", [128, 128], BF),
     "B8": ("sbuf", [128, 8], BF), "B8P": ("sbuf", [128, 8], BF), "B8N": ("sbuf", [128, 8], BF),
-    "wt": ("sbuf", [128, 8], BF), "SR": ("sbuf", [128, 128], BF), "Dm": ("sbuf", [128, 128], BF),
+    "wt": ("sbuf", [128, 8], BF), "Dm": ("sbuf", [128, 128], BF),
     "Inz": ("sbuf", [128, 128], BF), "I16": ("sbuf", [128, 128], BF), "IN": ("sbuf", [128, 128], BF),
     "Iod": ("sbuf", [128, 128], BF), "dm": ("sbuf", [128, 576], BF), "cd": ("sbuf", [128, 8], F32),
     "C1": ("sbuf", [128, 384], BF), "cm": ("sbuf", [128, 64], BF), "c2k": ("sbuf", [128, 64], BF),
@@ -45,7 +50,7 @@ SCRATCH = {
 for _t in range(NV):
     SCRATCH["Wu%d" % _t] = ("sbuf", [128, 128], U16)
 for _t in range(1, NV):
-    SCRATCH["Ws%d" % _t] = ("sbuf", [128, 128], U16)
+    SCRATCH["Ws%d" % _t] = ("sbuf", [128, 256], U16)
 for _b in ("PY", "PA", "PB", "PM", "PK", "PD", "PT", "PW"):
     SCRATCH[_b] = ("psum", [128, 512], F32)
 NDMA = 20
@@ -129,8 +134,8 @@ def rank_program(g, core, T, topo):
         return
     n = len(T.cores)
     nxt, prv = T.cores[(rank + 1) % n], T.cores[(rank - 1) % n]
-    eng_out = topo.engines(core, nxt)[::2]
-    n_in = len(topo.engines(prv, core)[::2])
+    eng_out = topo.engines(core, nxt)
+    n_in = len(topo.engines(prv, core))
     mask_out = sum(1 << x for x in eng_out)
     rid, pid = topo.addr(nxt)[0], topo.addr(nxt)[1]
     v, s, pe = g.vector, g.scalar, g.tensor
@@ -178,8 +183,7 @@ def rank_program(g, core, T, topo):
     dma("S", T.wi[:], T.wnd[:], [], ["wi"])
     for c in range(len(FC) - 1):
         dma("Y", T.fs[:, FC[c]:FC[c + 1]], T.fld[:, FC[c]:FC[c + 1]], [], ["fs%d" % c])
-    for c in range(2):
-        dma("Y", T.r2[:, 2048 * c:2048 * c + 2048], T.rec[:, 2048 * c:2048 * c + 2048], [], ["ra%d" % c])
+    dma("Y", T.r2[:, 0:4096], T.rec[:, :], [], ["ra0", "ra1"])
     op("Y", lambda: g.sync.dma_start(T.r2[:, 4096:8192], T.rec[:, :]), ["ra0", "ra1"], ["rb"], kind="dma")
 
     op("G", lambda: g.iota(T.pi[:, 0:1], [[0, 1]], 0, 1), [], ["pi0"])
@@ -219,11 +223,12 @@ def rank_program(g, core, T, topo):
     act(T.I16[:], T.I[:], ["I"], ["I16"], scale=1.0 / 16)
     act(T.If[:], T.I[:], ["I"], ["If"])
     act(T.IN[:], T.I[:], ["I"], ["IN"], scale=-1.0)
-    act(T.Ig[:], T.I[:], ["I"], ["Ig"], scale=16384.0)
+    act(T.Ig[:], T.I[:], ["I"], ["Ig"], scale=4096.0)
     act(T.Ih[:], T.I[:], ["I"], ["Ih"], scale=-4096.0)
     act(T.Iod[:], T.I[:], ["I", "s11"], ["Iod"], scale=col(11))
     act(T.Inz[:], T.I[:], ["I", "s17"], ["Inz"], scale=col(17))
     act(T.SoP[:], T.SoN[:], ["SoN"], ["SoP"], scale=-1.0)
+    act(T.B8f[:], T.B8[:], ["B8"], ["B8f"])
     act(T.B8P[:], T.B8[:], ["B8"], ["B8P"], scale=131072.0)
     act(T.B8N[:], T.B8[:], ["B8"], ["B8N"], scale=-65536.0)
     act(T.wt[:], T.B8[:], ["B8", "s14"], ["wt"], scale=col(14))
@@ -240,7 +245,8 @@ def rank_program(g, core, T, topo):
         lambda: ts(T.m16[:], T.Ck[:], col(K_), None, A.is_equal, None, ["Ck", "s0"], ["m16"]),
         lambda: ts(T.rst[:], T.Ck[:], 0.0, None, A.not_equal, None, ["Ck"], ["rst"]),
         lambda: tt(T.Dm[:], T.Sh[:], T.Inz[:], A.subtract, ["Sh", "Inz"], ["Dm"]),
-        lambda: tt(T.SR[:], T.Sh[:], T.Rev[:], A.subtract, ["Sh", "Rev"], ["SR"]),
+        lambda: ts(T.b2[:], T.Cm[:, 0:8], 16.0, 15.0, A.mult, A.add, ["Cm"], ["b2"]),
+        lambda: ts(T.cf[:], T.cd[:], -2048.0 - PAD, None, A.add, None, ["cd"], ["cf"]),
         lambda: ts(T.en[:, 0:1], col(19), 8.0, -3.0, A.mult, A.add, ["s19"], ["en"]),
     ]
 
@@ -264,37 +270,43 @@ def rank_program(g, core, T, topo):
 
         def extract(c):
             a, b = CH[c], CH[c + 1]
-            y = T.PY[:, a:b]
-            mm(y, T.SoN[:], T.c2k[:, 0:b - a], True, False, ["SoN", "c2k"], ["Y%d" % c], "PY")
-            if c: mm(y, T.SoN[:], T.W16[:, a:b], False, False, ["W16"], ["Y%d" % c], "PY")
+            yb = "PB" if c == NC - 1 else "PY"
+            y = T[yb][:, a:b]
+            yk = ["Y%d" % c, "QK"] if c == NC - 1 else ["Y%d" % c]
+            mm(y, T.SoN[:], T.c2k[:, 0:b - a], True, False, ["SoN", "c2k"], yk, yb)
+            mm(y, T.SoN[:], T.W16[:, a:b], False, False, ["W16"], yk, yb)
             for k in range(16):
-                mm(y, T.Dk[:, 128 * k:128 * k + 128], T.G[:, 16 * a + k:16 * b:16], False, k == 15 and c > 0,
-                   ["Dk%d" % k, "G%d" % c], ["Y%d" % c], "PY")
-            if not c: mm(y, T.SoN[:], T.W16[:, a:b], False, True, ["W16"], ["Y0"], "PY")
+                mm(y, T.Dk[:, 128 * k:128 * k + 128], T.G[:, 16 * a + k:16 * b:16], False, k == 15,
+                   ["Dk%d" % k, "G%d" % c], yk, yb)
 
         def names(c):
             a, b = CH[c], CH[c + 1]
             sl = slice(a, b)
+            yb = "PB" if c == NC - 1 else "PY"
             if t:
-                ts(T.off[:, sl], T.PY[:, sl], 6144.0, None, A.add, None, ["Y%d" % c], ["off%d" % c], ["PY"])
+                ts(T.off[:, sl], T[yb][:, sl], 6144.0, None, A.add, None, ["Y%d" % c], ["off%d" % c], [yb])
                 win, rk = T.r2[:, 0:8192], ["ra0", "ra1", "rb"]
             else:
-                ts(T.tb[:, sl], T.PY[:, sl], -2048.0, 4096.0, A.is_lt, A.mult, ["Y%d" % c], ["tb%d" % c], ["PY"])
+                ts(T.tb[:, sl], T[yb][:, sl], -2048.0, 4096.0, A.is_lt, A.mult, ["Y%d" % c], ["tb%d" % c], [yb])
                 if c < 3: filler(1)
-                tt(T.e16[:, sl], T.PY[:, sl], T.tb[:, sl], A.add, ["Y%d" % c, "tb%d" % c], ["e%d" % c], ["PY"])
+                tt(T.e16[:, sl], T[yb][:, sl], T.tb[:, sl], A.add, ["Y%d" % c, "tb%d" % c], ["e%d" % c], [yb])
                 if c < 3: filler(1)
                 ts(T.off[:, sl], T.e16[:, sl], 2048.0, None, A.add, None, ["e%d" % c], ["off%d" % c])
                 win, rk = T.r2[:, 0:4096], ["ra0", "ra1"]
-            m = b - XV if c == NC - 1 else b
+            m = b - (XV if t else XV0) if c == NC - 1 else b
             if m > a: act(T.X[:, 16 * a:16 * m], win.indirect(T.off[:, a:m]), rk + ["off%d" % c], ["X%d" % c])
             if m < b: cp(T.X[:, 16 * m:16 * b], win.indirect(T.off[:, m:b]), rk + ["off%d" % c], ["Xv"])
 
-        def wthings():
-            mm(T.PK[:, 0:128], T.I[:], T.zr[:], True, False, ["I", "zr"], ["K"], "PK")
-            mm(T.PD[:, 0:384], T.I[:], T.C1[:], True, False, ["C1a", "C1b"], ["D"], "PD")
-            mm(T.PD[:, 256:384], T.W16[:], T.Dm[:], False, False, ["W16", "Dm"], ["D"], "PD")
+        def wthings(part):
+            if part == 0:
+                mm(T.PK[:, 0:128], T.I[:], T.zr[:], True, False, ["I", "zr"], ["K"], "PK")
+                mm(T.PD[:, 0:384], T.I[:], T.C1[:], True, False, ["C1a", "C1b"], ["D"], "PD")
+                mm(T.PD[:, 256:384], T.W16[:], T.Dm[:], False, False, ["W16", "Dm"], ["D"], "PD")
+                return
             mm(T.PT[:, 272:280], T.W16[:], T.I[:, 15::16], True, True, ["W16"], ["Te"], "PT")
-            mm(T.PW[:, 0:128], T.Rev[:], T.W16[:], True, False, ["W16", "Rev"], ["WN"], "PW")
+            mm(T.PW[:, 0:256], T.zr[:], T.Dk[:, 0:256], True, False, ["zr"], ["WN"], "PW")
+            mm(T.PW[:, 0:128], T.Sh[:], T.W16[:], False, False, ["W16", "Sh"], ["WN"], "PW")
+            mm(T.PW[:, 128:256], T.Rev[:], T.W16[:], False, False, ["W16", "Rev"], ["WN"], "PW")
 
         def total(hf):
             ps, b = (T.PA, "PA") if hf == 0 else (T.PB, "PB")
@@ -321,26 +333,29 @@ def rank_program(g, core, T, topo):
         YK = ["Y%d" % c for c in range(NC)]
         XH = [["X%d" % c for c in range(NC) if CH[c] < 64], ["X%d" % c for c in range(NC) if CH[c + 1] > 64] + ["Xv"]]
         XK = XH[0] + XH[1]
-        fgather(0)
+        la = CH[NC - 1]
         ts(T.W16[:], Wu[:], -2048.0, None, A.add, None, [wk], ["W16"])
+        fgather(0)
         extract(0)
+        if t: wthings(0)
         for c in range(1, NC):
             fgather(c); names(c - 1)
             extract(c)
-            if t and c == WT: wthings()
+            if t and c == NC - 2: wthings(1)
         if t:
-            ts(T.ri[:, 0:1], T.Gs[:, 0:1], 0.5, -0.25, A.mult, A.add, ["Gs"], ["ri"])
-            ts(T.par[:, 0:1], T.ri[:, 0:1], -2.0, T.Gs[:, 0:1], A.mult, A.add, ["Gs", "ri"], ["par"])
+            ts(T.tb[:, 0:la], T.PY[:, 0:la], -2048.0, 4096.0, A.is_lt, A.mult, YK[:-1], ["tb"], ["PY"])
+            tt(T.e16[:, 0:la], T.PY[:, 0:la], T.tb[:, 0:la], A.add, YK[:-1] + ["tb"], EK[:-1], ["PY"])
         else:
             filler(99)
         names(NC - 1)
         total(0)
         if t:
-            ts(T.tb[:], T.PY[:, 0:128], -2048.0, 4096.0, A.is_lt, A.mult, YK, ["tb"], ["PY"])
-            tt(T.e16[:], T.PY[:, 0:128], T.tb[:], A.add, YK + ["tb"], EK, ["PY"])
+            ts(T.tb[:, la:128], T.PB[:, la:128], -2048.0, 4096.0, A.is_lt, A.mult, YK[-1:], ["tbl"], ["PB"])
+            mean(0)
+            tt(T.e16[:, la:128], T.PB[:, la:128], T.tb[:, la:128], A.add, YK[-1:] + ["tbl"], EK[-1:], ["PB"])
         else:
-            wthings()
-        mean(0)
+            wthings(0); wthings(1)
+            mean(0)
         mm(T.PD[:, 0:128], T.e16[:], T.Dm[:], False, False, EK + ["Dm"], ["D"], "PD")
         mm(T.PD[:, 128:256], T.e16[:], T.Dm[:], False, True, EK, ["D"], "PD")
         mm(T.PT[:, 128:256], T.e16[:], T.I[:], True, True, EK, ["Te"], "PT")
@@ -349,64 +364,70 @@ def rank_program(g, core, T, topo):
         total(1)
         for k in range(16):
             mm(T.PK[:, k:128:16], T.X[:, k::16], T.B8N[:], False, False, XK + ["B8N"], ["K"], "PK")
-        for k in range(16): larger(0, k)
+        for k in range(MP): larger(0, k)
         act(T.eT[:], T.PT[:, 128:280], ["Te"], ["eT"], ["PT"], bias=2048.0)
-        mean(1)
+        act(T.nth[:, 0:1], T.par[:, 0:1], ["par"], ["nth"], bias=-3.5, scale=-1.0)
         act(T.D0[:], T.PD[:, 0:384], ["D"], ["D0"], ["PD"])
+        mean(1)
+        for k in range(MP, 16): larger(0, k)
         for k in range(16):
             larger(1, k)
             mm(T.PK[:, k:128:16], mx(k, 0, 128), T.B8P[:], False, k == 15,
                ["MX0_%d" % k, "MX1_%d" % k, "B8P"], ["K"], "PK")
-            if k == 4:
+            if k == 0:
                 mm(T.PT[:, 288:296], T.Mb[:], T.wt[:], True, True, ["Mb0", "Mb1", "wt"], ["Tu"], "PT")
                 mm(T.PK[:, 0:128], T.Mb[:], T.BN[:], False, False, ["Mb0", "Mb1", "BN"], ["K"], "PK")
                 act(T.sq[:], T.PT[:, 288:296], ["Tu"], ["sq"], ["PT"], f=AF.Square, scale=0.25)
                 act(T.t74[:], T.PT[:, 288:296], ["Tu"], ["t74"], ["PT"], bias=-0.25, scale=74.0)
         tt(T.yi[:], T.sq[:], T.t74[:], A.add, ["sq", "t74"], ["yi"])
+        ts(T.zi[:], T.yi[:], 1, 4095, A.logical_shift_right, A.bitwise_and, ["yi"], ["zi"])
         key = T.PK[:, 0:128]
         bc = T.bc[:, 0:8]
         scan(T.R[:, 0:128], T.D0[:, 0:128], key, A.add, A.min, ["K", "D0"], ["R0"], ["PK"])
-        ts(T.zi[:], T.yi[:], 1, 4095, A.logical_shift_right, A.bitwise_and, ["yi"], ["zi"])
-        tt(T.Ni[:], T.R[:, 15:128:16], T.eT[:, 128:136], A.add, ["R0", "eT"], ["Ni"])
         scan(T.R[:, 128:256], T.D0[:, 128:256], key, A.add, A.max, ["K", "D0"], ["R1"], ["PK"])
-        ts(T.NK[:, 0:8], T.Ni[:], 4095, None, A.bitwise_and, None, ["Ni"], ["n"])
         ts(T.Zt[:, 0::16], T.zi[:], -2048.0, None, A.add, None, ["zi"], ["Zt"])
-        mm(T.PW[:, 0:128], T.Zt[:], T.I[:], False, False, ["Zt"], ["WN"], "PW")
-        tt(T.eq[:], T.NK[:, 0:8].indirect(bc), T.eT[:, 0:128], A.is_equal, ["n", "bc", "eT"], ["eq"])
-        mm(T.PD[:, 0:128], T.SR[:], T.W16[:], True, False, ["W16", "SR"], ["D"], "PD")
-        mm(T.PD[:, 0:128], T.Zt[:], T.IN[:], False, False, ["Zt", "IN"], ["D"], "PD")
-        ts(T.Nt[:, 0::16], T.NK[:, 0:8], -2048.0, None, A.add, None, ["n"], ["Nt"])
-        mm(T.PD[:, 0:128], T.Nt[:], T.I[:], False, False, ["Nt"], ["D"], "PD")
+        mm(T.PW[:, 128:256], T.Zt[:], T.I[:], False, False, ["Zt"], ["WN"], "PW")
+        tt(T.Ni[:], T.R[:, 15:128:16], T.eT[:, 128:136], A.add, ["R0", "eT"], ["Ni"])
         scan(T.R[:, 256:384], T.D0[:, 256:384], key, A.add, A.max, ["K", "D0"], ["R2"], ["PK"])
-        scan(T.Sc[:], T.rst[:], T.eq[:], A.mult, A.add, ["rst", "eq"], ["Sc"])
+        ts(T.NK[:, 0:8], T.Ni[:], 4095, None, A.bitwise_and, None, ["Ni"], ["n"])
         tt(T.Ri[:], T.R[:, 143:384:16], T.eT[:, 136:152], A.add, ["R1", "R2", "eT"], ["Ri"])
-        ts(T.go[:, 0:8], T.Sc[:, 15::16], T.par[:, 0:1], 4.0, A.subtract, A.is_ge, ["Sc", "par"], ["go"])
-        act(T.gG[:], T.go[:, 0:8].indirect(bc), ["go", "bc"], ["gG"])
-        mm(T.PD[:, 0:128], T.gG[:], T.Ig[:], False, True, ["gG", "Ig"], ["D"], "PD")
-        mm(T.PW[:, 0:128], T.gG[:], T.Ih[:], False, False, ["gG", "Ih"], ["WN"], "PW")
+        tt(T.eq[:], T.NK[:, 0:8].indirect(bc), T.eT[:, 0:128], A.is_equal, ["n", "bc", "eT"], ["eq"])
         ts(T.low[:], T.Ri[:], 4095, None, A.bitwise_and, None, ["Ri"], ["low"])
+        ts(T.Nt[:, 0::16], T.NK[:, 0:8], -2048.0, None, A.add, None, ["n"], ["Nt"])
+        mm(T.PW[:, 0:128], T.Nt[:], T.I[:], False, False, ["Nt"], ["WN"], "PW")
         ts(T.NK[:, 8:16], T.Ri[:, 0:8], 12, 15, A.logical_shift_right, A.bitwise_and, ["Ri"], ["kk"])
+        scan(T.Sc[:], T.rst[:], T.eq[:], A.mult, A.add, ["rst", "eq"], ["Sc"])
+        act(T.gG[:], T.Sc[:].indirect(T.b2[:]), ["Sc", "b2", "nth"], ["gG"], f=AF.Sign, bias=T.nth[:, 0:1])
+        mm(T.PW[:, 0:128], T.gG[:], T.Ig[:], False, False, ["gG", "Ig"], ["WN"], "PW")
+        mm(T.PW[:, 128:256], T.gG[:], T.Ih[:], False, True, ["gG", "Ih"], ["WN"], "PW")
         tt(T.ne[:], T.NK[:, 0:8], T.low[:, 0:8], A.not_equal, ["n", "low"], ["ne"])
         ts(T.c2[:], T.low[:, 8:16], col(12), None, A.add, None, ["low", "s12"], ["c2"])
         cp(T.NKf[:], T.NK[:], ["n", "kk"], ["NKf"])
+        ts(T.go[:, 0:8], T.Sc[:, 15::16], T.par[:, 0:1], 4.0, A.subtract, A.is_ge, ["Sc", "par"], ["go"])
         tt(T.u2[:], T.c2[:], T.ne[:], A.mult, ["c2", "ne"], ["u2"])
-        act(T.tT[:], T.PD[:, 0:128], ["D"], ["tT"], ["PD"], f=AF.Relu, bias=-12288.0)
-        mm(T.PW[:, 0:128], T.If[:], T.tT[:], False, True, ["tT", "If"], ["WN"], "PW")
         act(T.gK[:], T.NKf[:, 8:16].indirect(bc), ["NKf", "bc"], ["gK"])
         act(T.gN[:], T.NKf[:, 0:8].indirect(bc), ["NKf", "bc"], ["gN"])
+        if t < NV - 1:
+            mm(T.PT[:, 304:312], T.on[:], T.go[:, 0:8], True, True, ["on", "go"], ["Tc"], "PT")
+            act(T.jk[:], T.PT[:, 304:312], ["Tc"], ["jk", "Gs"], ["PT"], acc=T.Gs[:, 0:1])
+        mm(T.PB[:, 0:128], T.gK[:], T.I[:], True, True, ["gK"], ["QK"], "PB")
+        act(T.ab[:], T.PB[:, 0:128], ["QK", "s10"], ["ab"], ["PB"], f=AF.Abs, bias=col(10), scale=8192.0)
+        mm(T.PA[:, 128:136], T.I[:], T.cf[:], True, False, ["cf"], ["bS", "S0"], "PA")
+        mm(T.PY[:, 128:136], T.I[:], T.cf[:], True, False, ["cf"], ["bV"] + YK, "PY")
         tt(T.cw[:], T.go[:, 0:8], T.u2[:], A.mult, ["go", "u2"], ["cw"])
+        tt(T.bM[:], T.cw[:, 0:8].indirect(bc), T.m16[:], A.mult, ["cw", "bc", "m16"], ["bM"])
         ts(T.bC[:], T.cw[:, 0:8].indirect(bc), col(13), None, A.add, None, ["cw", "bc", "s13"], ["bC"])
-        tt(T.bM[:], T.bC[:], T.m16[:], A.mult, ["bC", "m16"], ["bM"])
         if t < NV - 1:
             ws = T["Ws%d" % (t + 1)]
-            ts(ws[:], T.PW[:, 0:128], 2048.0, None, A.add, None, ["WN"], ["Ws%d" % t], ["PW"])
-            op("G", lambda ws=ws, t=t: g.remote_dma(T["Wu%d" % (t + 1)][:], ws[:], T.sem["arr%d" % (t + 1)], T.sem.sent,
-                                                   pid, rid, mask_out), ["Ws%d" % t], [], kind="send", val=len(eng_out))
+            ts(ws[:], T.PW[:, 0:256], -2048.0, None, A.add, None, ["WN"], ["Ws%d" % t], ["PW"])
+            op("G", lambda ws=ws, t=t: g.remote_dma_fused([RemoteDMATransfer(
+                dst_ids=[DstId(rid=rid, pnc=pid)], dma_engine_mask=mask_out, remote_sem=T.sem["arr%d" % (t + 1)],
+                srcs=[ws[:, 0:128], ws[:, 128:256]], dsts=[T["Wu%d" % (t + 1)][:]], alu_op=2)], local_sem=T.sem.sent),
+               ["Ws%d" % t], [], kind="send", val=len(eng_out))
+        mm(T.PA[:, 128:136], T.bM[:], T.B8f[:], False, True, ["bM", "B8f"], ["bS"], "PA")
+        mm(T.PY[:, 128:136], T.bM[:], T.B8f[:], False, True, ["bM"], ["bV"], "PY")
         mm(T.PY[:, 0:128], T.bC[:], T.J[:], True, True, ["bC", "J"], YK, "PY")
         mm(T.PA[:, 0:128], T.bC[:], T.J[:], True, True, ["bC"], ["cS", "S0"], "PA")
-        mm(T.PA[:, 128:136], T.bM[:], T.B8[:], True, True, ["bM", "B8"], ["bS"], "PA")
-        mm(T.PY[:, 128:136], T.bM[:], T.B8[:], True, True, ["bM"], ["bV"], "PY")
-        mm(T.PB[:, 0:128], T.gK[:], T.I[:], True, True, ["gK"], ["QK"], "PB")
         mm(T.PD[:, 0:128], T.gN[:], T.If[:], True, False, ["gN"], ["D"], "PD")
         mm(T.PD[:, 0:128], T.SoP[:], T.W16[:], False, True, ["SoP", "W16"], ["D"], "PD")
         mm(T.PK[:, 0:128], T.gN[:], T.If[:], True, False, ["gN"], ["K"], "PK")
@@ -414,40 +435,41 @@ def rank_program(g, core, T, topo):
         act(T.nB[:], T.PA[:, 128:136], ["bS"], ["nB"], ["PA"], scale=-8192.0)
         for h in range(7, -1, -1):
             st, ln = 8 * h * (h + 1), 16 * h + 16
-            if h >= 4:
+            if h >= HV:
                 ts(T.E[:, st:st + ln], T.PY[:, 128 - ln:128], T.PY[:, 128 + h:129 + h], 8192.0, A.not_equal, A.mult,
                    ["Y0", "bV"], ["E%d" % h], ["PY"])
             else:
                 act(T.E[:, st:st + ln], T.PA[:, 128 - ln:128], ["cS", "nB"], ["E%d" % h], ["PA"], f=AF.Abs,
                     bias=T.nB[:, h:h + 1], scale=8192.0)
         act(T.cB[:, 0:8], T.PA[:, 128:136], ["bS"], ["cB"], ["PA"], bias=2048.0 + PAD)
-        act(T.ab[:], T.PB[:, 0:128], ["QK", "s10"], ["ab"], ["PB"], f=AF.Abs, bias=col(10), scale=8192.0)
         act(T.sg[:], T.PD[:, 0:128], ["D"], ["sg"], ["PD"], f=AF.Sign, bias=-2047.5)
         mm(T.PK[:, 0:128], T.IN[:], T.ab[:], False, False, ["IN", "ab"], ["K"], "PK")
         mm(T.PK[:, 0:128], T.Iod[:], T.sg[:], False, True, ["Iod", "sg"], ["K"], "PK")
-        if t < NV - 1:
-            mm(T.PT[:, 304:312], T.on[:], T.go[:, 0:8], True, True, ["on", "go"], ["Tc"], "PT")
-            act(T.jk[:], T.PT[:, 304:312], ["Tc"], ["jk", "Gs"], ["PT"], acc=T.Gs[:, 0:1])
-        else:
-            act(T.wo[:], T.PW[:, 0:128], ["WN"], ["wo"], ["PW"], bias=2048.0)
+        if t == NV - 1:
+            act(T.tT[:], T.PW[:, 0:256], ["WN"], ["tT"], ["PW"], f=AF.Relu, bias=-2048.0)
+            mm(T.PT[:, 0:128], T.If[:], T.tT[:, 0:128], True, False, ["tT"], ["Tw"], "PT")
+            mm(T.PT[:, 0:128], T.If[:], T.tT[:, 128:256], False, True, ["tT"], ["Tw"], "PT")
+            act(T.wo[:], T.PT[:, 0:128], ["Tw"], ["wo"], ["PT"])
             dma("Y", T.yw[:], T.wo[:], ["wo"], [])
+        ts(T.o0[:], T.PY[:, 128:136], 2048.0 + PAD, None, A.add, None, ["bV"], ["o0"], ["PY"])
         scan(T.Rd[:], T.E[:], T.dm[:], A.min, A.max, ["E%d" % h for h in range(8)] + ["dm%d" % h for h in range(8)], ["Rd"])
+        tt(T.om[:], T.U[:].indirect(T.o0[:]), T.ab[:], A.min, UK + ["o0", "ab"], ["om"])
         tt(T.rr[:], T.Rd[:].indirect(T.en[:, 0:1]), T.cB[:], A.min, ["Rd", "en", "cB"], ["rr"])
-        cp(T.o1[:], T.rr[:, 0:8], ["rr"], ["o1"])
-        tt(T.om[:], T.U[:].indirect(T.o1[:]), T.ab[:], A.min, UK + ["o1", "ab"], ["om"])
+        if t < NV - 1: ts(T.ri[:, 0:1], T.Gs[:, 0:1], 0.5, -0.25, A.mult, A.add, ["Gs"], ["ri"])
         tt(T.nw[:], T.om[:], T.PK[:, 0:128], A.max, ["om", "K"], ["nw"], ["PK"])
+        cp(T.o1[:], T.rr[:, 0:8], ["rr"], ["o1"])
+        if t < NV - 1: ts(T.par[:, 0:1], T.ri[:, 0:1], -2.0, T.Gs[:, 0:1], A.mult, A.add, ["Gs", "ri"], ["par"])
         cp(T.U[:].indirect(T.o1[:]), T.nw[:], ["o1", "nw"], UK)
 
     cuts = [0, 384, 896, 1408, 1792, 2048]
     def high(c):
         a, b = cuts[c], cuts[c + 1]
-        ps, bk = (T.PM, "PM") if c % 2 == 0 else (T.PK, "PK")
-        ts(ps[:, 0:b - a], T.U[:, HI + a:HI + b], 4096.0, None, A.mult, None, UK, ["H%d" % (c % 2)], [bk])
+        ts(T[HB[c]][:, 0:b - a], T.U[:, HI + a:HI + b], 4096.0, None, A.mult, None, UK, ["H%d" % c], [HB[c]])
+    HB = ["PM", "PY", "PA", "PB", "PD", "PK"]
     high(0)
     for c in range(len(cuts) - 1):
         a, b = cuts[c], cuts[c + 1]
-        ps, bk = (T.PM, "PM") if c % 2 == 0 else (T.PK, "PK")
         if c + 2 < len(cuts): high(c + 1)
-        tt(T.fo[:, a:b], T.U[:, LO + a:LO + b], ps[:, 0:b - a], A.add, UK + ["H%d" % (c % 2)], ["fo%d" % c], [bk])
+        tt(T.fo[:, a:b], T.U[:, LO + a:LO + b], T[HB[c]][:, 0:b - a], A.add, UK + ["H%d" % c], ["fo%d" % c], [HB[c]])
         dma("Y" if c % 2 == 0 else "S", T.yf[:, a:b], T.fo[:, a:b], ["fo%d" % c], [])
     emit(g, T, ops)

@@ -5,7 +5,11 @@ F32, BF, FH, I32, U16 = "float32", "bfloat16", "float16", "int32", "uint16"
 NV = 4
 CH = [0, 32, 64, 96, 128]
 NC = len(CH) - 1
-MP = 13
+YB = ["PY", "PA", "PY", "PB"]
+PC = [0, 64, 96, 128]
+SB = ["PA", "PY", "PB"]
+LA = 5
+MP = 4
 HV = 3
 XV0 = 0
 XV = 0
@@ -15,7 +19,7 @@ SCRATCH = {
     "r2": ("sbuf", [128, 8192], BF), "wi": ("sbuf", [128, 128], I32), "wo": ("sbuf", [128, 128], F32),
     "G": ("sbuf", [128, 2048], FH), "X": ("sbuf", [128, 2048], BF), "MX": ("sbuf", [128, 2048], BF),
     "W16": ("sbuf", [128, 128], FH), "e16": ("sbuf", [128, 128], FH), "off": ("sbuf", [128, 128], U16),
-    "tb": ("sbuf", [128, 128], F32), "Mt": ("sbuf", [128, 128], BF), "Mb": ("sbuf", [128, 128], BF),
+    "tb": ("sbuf", [128, 128], F32), "Mt": ("sbuf", [128, 128], BF), "k0": ("sbuf", [128, 128], BF),
     "D0": ("sbuf", [128, 384], F32), "Nt": ("sbuf", [128, 128], FH), "gG": ("sbuf", [128, 128], BF),
     "Ig": ("sbuf", [128, 128], BF), "Ih": ("sbuf", [128, 128], BF), "eT": ("sbuf", [128, 152], F32),
     "R": ("sbuf", [128, 384], F32), "Ni": ("sbuf", [128, 8], I32), "Ri": ("sbuf", [128, 16], I32),
@@ -177,6 +181,7 @@ def rank_program(g, core, T, topo):
         return T.sc[:, i:i + 1]
 
     FC = [0, 256, 640, 1152, 1664, 2048]
+    FL = [2, 1]
     UK = ["U%d" % i for i in range(2 * len(FC) - 2)] + ["Ud"]
     LO, HI = PAD, PAD + 2048
 
@@ -191,6 +196,7 @@ def rank_program(g, core, T, topo):
     op("G", lambda: g.iota(T.Ck[:], [[0, 8], [1, 16]], 0, 0, allow_small_or_imprecise_dtypes=True), [], ["Ck"])
     op("G", lambda: g.iota(T.Cg[:], [[1, 8], [0, 16]], 0, 0, allow_small_or_imprecise_dtypes=True), [], ["Cg"])
     ms(T.C1[:, 0:128], -4096.0, ["C1a"]); ms(T.C1[:, 128:384], 4096.0, ["C1b"])
+    ms(T.k0[:], 3072.0 * 65536, ["k0"])
     ms(T.zr[:], 0.0, ["zr"]); ms(T.on[:], 1.0, ["on"]); ms(T.cm[:], -15.0 / 32, ["cm"]); ms(T.c2k[:], 2048.0, ["c2k"])
     ts(T.pi[:, 1:2], T.pi[:, 0:1], 15, None, A.bitwise_and, None, ["pi0"], ["pi1"])
     ts(T.pi[:, 2:3], T.pi[:, 0:1], 4, None, A.logical_shift_right, None, ["pi0"], ["pi2"])
@@ -217,6 +223,7 @@ def rank_program(g, core, T, topo):
     cp(T.Zt[:], T.zr[:], ["zr"], ["Zt"])
     cp(T.Nt[:], T.zr[:], ["zr"], ["Nt"])
     cp(T.Wu0[:], T.wi[:], ["wi"], ["Wu0"])
+    act(T.Inz[:], T.I[:], ["I", "s17"], ["Inz"], scale=col(17))
     for k in range(16):
         act(T.Dk[:, 128 * k:128 * k + 128], T.I[:], ["I", "km"], ["Dk%d" % k], scale=T.km[:, k:k + 1])
     act(col(19), col(18), ["s18"], ["s19"], f=AF.Square)
@@ -226,7 +233,6 @@ def rank_program(g, core, T, topo):
     act(T.Ig[:], T.I[:], ["I"], ["Ig"], scale=4096.0)
     act(T.Ih[:], T.I[:], ["I"], ["Ih"], scale=-4096.0)
     act(T.Iod[:], T.I[:], ["I", "s11"], ["Iod"], scale=col(11))
-    act(T.Inz[:], T.I[:], ["I", "s17"], ["Inz"], scale=col(17))
     act(T.SoP[:], T.SoN[:], ["SoN"], ["SoP"], scale=-1.0)
     act(T.B8f[:], T.B8[:], ["B8"], ["B8f"])
     act(T.B8P[:], T.B8[:], ["B8"], ["B8P"], scale=131072.0)
@@ -240,11 +246,11 @@ def rank_program(g, core, T, topo):
     late = [
         lambda: ts(T.Sh[:], T.Cm[:], col(4), col(16), A.is_equal, A.mult, ["Cm", "s4", "s16"], ["Sh"]),
         lambda: ts(T.Rev[:], T.Cm[:], col(8), col(16), A.is_equal, A.mult, ["Cm", "s8", "s16"], ["Rev"]),
+        lambda: tt(T.Dm[:], T.Sh[:], T.Inz[:], A.subtract, ["Sh", "Inz"], ["Dm"]),
         lambda: ts(T.J[:], T.Cm[:], col(6), None, A.is_equal, None, ["Cm", "s6"], ["J"]),
         lambda: ts(T.BN[:], T.Cg[:], col(G_), -65536.0, A.is_equal, A.mult, ["Cg", "s0"], ["BN"]),
         lambda: ts(T.m16[:], T.Ck[:], col(K_), None, A.is_equal, None, ["Ck", "s0"], ["m16"]),
         lambda: ts(T.rst[:], T.Ck[:], 0.0, None, A.not_equal, None, ["Ck"], ["rst"]),
-        lambda: tt(T.Dm[:], T.Sh[:], T.Inz[:], A.subtract, ["Sh", "Inz"], ["Dm"]),
         lambda: ts(T.b2[:], T.Cm[:, 0:8], 16.0, 15.0, A.mult, A.add, ["Cm"], ["b2"]),
         lambda: ts(T.cf[:], T.cd[:], -2048.0 - PAD, None, A.add, None, ["cd"], ["cf"]),
         lambda: ts(T.en[:, 0:1], col(19), 8.0, -3.0, A.mult, A.add, ["s19"], ["en"]),
@@ -257,6 +263,7 @@ def rank_program(g, core, T, topo):
         a, b = FC[c], FC[c + 1]
         ts(T.U[:, LO + a:LO + b], T.fs[:, a:b], 4095, None, A.bitwise_and, None, ["fs%d" % c], ["U%d" % (2 * c)])
         ts(T.U[:, HI + a:HI + b], T.fs[:, a:b], 12, None, A.logical_shift_right, None, ["fs%d" % c], ["U%d" % (2 * c + 1)])
+        if c < 2: filler(FL[c])
 
     for t in range(NV):
         Wu, wk = T["Wu%d" % t], "Wu%d" % t
@@ -268,13 +275,14 @@ def rank_program(g, core, T, topo):
             ts(T.G[:, 16 * a:16 * b], T.U[:, LO:LO + 4096].indirect(Wu[:, a:b]), -2048.0, None,
                A.add, None, UK + [wk], ["G%d" % c])
 
-        def extract(c):
+        def extract(c, between=None):
             a, b = CH[c], CH[c + 1]
-            yb = "PB" if c == NC - 1 else "PY"
+            yb = YB[c]
             y = T[yb][:, a:b]
-            yk = ["Y%d" % c, "QK"] if c == NC - 1 else ["Y%d" % c]
+            yk = ["Y%d" % c, {"PB": "QK", "PA": "cS", "PY": "cV"}[yb]]
             mm(y, T.SoN[:], T.c2k[:, 0:b - a], True, False, ["SoN", "c2k"], yk, yb)
             mm(y, T.SoN[:], T.W16[:, a:b], False, False, ["W16"], yk, yb)
+            if between: between()
             for k in range(16):
                 mm(y, T.Dk[:, 128 * k:128 * k + 128], T.G[:, 16 * a + k:16 * b:16], False, k == 15,
                    ["Dk%d" % k, "G%d" % c], yk, yb)
@@ -282,7 +290,7 @@ def rank_program(g, core, T, topo):
         def names(c):
             a, b = CH[c], CH[c + 1]
             sl = slice(a, b)
-            yb = "PB" if c == NC - 1 else "PY"
+            yb = YB[c]
             if t:
                 ts(T.off[:, sl], T[yb][:, sl], 6144.0, None, A.add, None, ["Y%d" % c], ["off%d" % c], [yb])
                 win, rk = T.r2[:, 0:8192], ["ra0", "ra1", "rb"]
@@ -299,7 +307,7 @@ def rank_program(g, core, T, topo):
 
         def wthings(part):
             if part == 0:
-                mm(T.PK[:, 0:128], T.I[:], T.zr[:], True, False, ["I", "zr"], ["K"], "PK")
+                mm(T.PK[:, 0:128], T.I[:], T.k0[:], True, False, ["I", "k0"], ["K"], "PK")
                 mm(T.PD[:, 0:384], T.I[:], T.C1[:], True, False, ["C1a", "C1b"], ["D"], "PD")
                 mm(T.PD[:, 256:384], T.W16[:], T.Dm[:], False, False, ["W16", "Dm"], ["D"], "PD")
                 return
@@ -309,102 +317,112 @@ def rank_program(g, core, T, topo):
             mm(T.PW[:, 128:256], T.Rev[:], T.W16[:], False, False, ["W16", "Rev"], ["WN"], "PW")
 
         def total(hf):
-            ps, b = (T.PA, "PA") if hf == 0 else (T.PB, "PB")
-            mm(ps[:, 0:64], T.I[:], T.cm[:], True, False, ["cm"], ["S%d" % hf, "cS" if hf == 0 else "QK"], b)
+            a, b = PC[hf], PC[hf + 1]
+            ps = T[SB[hf]][:, 320:320 + b - a]
+            mm(ps, T.I[:], T.cm[:, 0:b - a], True, False, ["cm"], ["S%d" % hf], SB[hf])
             for k in range(16):
-                mm(ps[:, 0:64], T.I16[:], T.X[:, 1024 * hf + k:1024 * hf + 1024:16], False, k == 15,
-                   ["I16"] + XH[hf], ["S%d" % hf], b)
-
-        def mx(k, lo, hi):
-            return T.MX[:, 128 * k + lo:128 * k + hi]
+                mm(ps, T.I16[:], T.X[:, 16 * a + k:16 * b:16], False, k == 15, ["I16"] + XH[hf], ["S%d" % hf], SB[hf])
 
         def mean(hf):
-            ps, b = (T.PA, "PA") if hf == 0 else (T.PB, "PB")
-            sl = slice(64 * hf, 64 * hf + 64)
-            ts(T.PM[:, sl], ps[:, 0:64], MAGIC, -MAGIC, A.add, A.add, ["S%d" % hf], ["M%d" % hf], [b, "PM"])
-            act(T.Mt[:, sl], ps[:, 0:64], ["S%d" % hf], ["Mt%d" % hf], [b], bias=192.0)
-            act(T.Mb[:, sl], T.Mt[:, sl], ["Mt%d" % hf], ["Mb%d" % hf], bias=-192.0)
+            a, b = PC[hf], PC[hf + 1]
+            ps = T[SB[hf]][:, 320:320 + b - a]
+            for j in range(2):
+                ts(T.PM[:, 2 * a + j:2 * b:2], ps, MAGIC, -MAGIC, A.add, A.add, ["S%d" % hf],
+                   ["M%d_%d" % (hf, j)], [SB[hf], "PM"])
+            act(T.Mt[:, a:b], ps, ["S%d" % hf], ["Mt%d" % hf], [SB[hf]], bias=192.0)
 
         def larger(hf, k):
-            tt(mx(k, 64 * hf, 64 * hf + 64), T.X[:, 1024 * hf + k:1024 * hf + 1024:16],
-               T.PM[:, 64 * hf:64 * hf + 64], A.max, XH[hf] + ["M%d" % hf], ["MX%d_%d" % (hf, k)], ["PM"])
+            a, b = PC[hf], PC[hf + 1]
+            tt(T.MX[:, 256 * k + 2 * a:256 * k + 2 * b], T.X[:, 16 * a + k:16 * b:8], T.PM[:, 2 * a:2 * b],
+               A.max, XH[hf] + ["M%d_0" % hf, "M%d_1" % hf], ["MX%d_%d" % (hf, k)], ["PM"])
 
         EK = ["e%d" % c for c in range(NC)]
         YK = ["Y%d" % c for c in range(NC)]
-        XH = [["X%d" % c for c in range(NC) if CH[c] < 64], ["X%d" % c for c in range(NC) if CH[c + 1] > 64] + ["Xv"]]
-        XK = XH[0] + XH[1]
+        XH = [["X0", "X1"], ["X2"], ["X3", "Xv"]]
+        XK = XH[0] + XH[1] + XH[2]
         la = CH[NC - 1]
         ts(T.W16[:], Wu[:], -2048.0, None, A.add, None, [wk], ["W16"])
         fgather(0)
         extract(0)
-        if t: wthings(0)
+        wthings(0)
         for c in range(1, NC):
             fgather(c); names(c - 1)
             extract(c)
-            if t and c == NC - 2: wthings(1)
+            if c == 1: wthings(1)
         if t:
-            ts(T.tb[:, 0:la], T.PY[:, 0:la], -2048.0, 4096.0, A.is_lt, A.mult, YK[:-1], ["tb"], ["PY"])
-            tt(T.e16[:, 0:la], T.PY[:, 0:la], T.tb[:, 0:la], A.add, YK[:-1] + ["tb"], EK[:-1], ["PY"])
+            for c in (1, 0, 2):
+                sl = slice(CH[c], CH[c + 1])
+                ts(T.tb[:, sl], T[YB[c]][:, sl], -2048.0, 4096.0, A.is_lt, A.mult, [YK[c]], ["tb%d" % c], [YB[c]])
+            for c in (1, 0, 2):
+                sl = slice(CH[c], CH[c + 1])
+                tt(T.e16[:, sl], T[YB[c]][:, sl], T.tb[:, sl], A.add, [YK[c], "tb%d" % c], [EK[c]], [YB[c]])
         else:
             filler(99)
         names(NC - 1)
         total(0)
         if t:
             ts(T.tb[:, la:128], T.PB[:, la:128], -2048.0, 4096.0, A.is_lt, A.mult, YK[-1:], ["tbl"], ["PB"])
-            mean(0)
             tt(T.e16[:, la:128], T.PB[:, la:128], T.tb[:, la:128], A.add, YK[-1:] + ["tbl"], EK[-1:], ["PB"])
-        else:
-            wthings(0); wthings(1)
-            mean(0)
+        mean(0)
+        total(1)
+        for k in range(LA): larger(0, k)
+        mean(1)
+        for k in range(LA, 8): larger(0, k)
         mm(T.PD[:, 0:128], T.e16[:], T.Dm[:], False, False, EK + ["Dm"], ["D"], "PD")
         mm(T.PD[:, 128:256], T.e16[:], T.Dm[:], False, True, EK, ["D"], "PD")
         mm(T.PT[:, 128:256], T.e16[:], T.I[:], True, True, EK, ["Te"], "PT")
         mm(T.PT[:, 256:264], T.e16[:], T.I[:, 15::16], True, True, EK, ["Te"], "PT")
         mm(T.PT[:, 264:272], T.e16[:], T.I[:, 15::16], True, True, EK, ["Te"], "PT")
-        total(1)
+        total(2)
         for k in range(16):
             mm(T.PK[:, k:128:16], T.X[:, k::16], T.B8N[:], False, False, XK + ["B8N"], ["K"], "PK")
-        for k in range(MP): larger(0, k)
+        for k in range(MP): larger(1, k)
         act(T.eT[:], T.PT[:, 128:280], ["Te"], ["eT"], ["PT"], bias=2048.0)
         act(T.nth[:, 0:1], T.par[:, 0:1], ["par"], ["nth"], bias=-3.5, scale=-1.0)
         act(T.D0[:], T.PD[:, 0:384], ["D"], ["D0"], ["PD"])
-        mean(1)
-        for k in range(MP, 16): larger(0, k)
-        for k in range(16):
-            larger(1, k)
-            mm(T.PK[:, k:128:16], mx(k, 0, 128), T.B8P[:], False, k == 15,
-               ["MX0_%d" % k, "MX1_%d" % k, "B8P"], ["K"], "PK")
+        mean(2)
+        MK = ["Mt%d" % j for j in range(3)]
+        for k in range(MP, 8): larger(1, k)
+        for k in range(8):
+            for j in range(2):
+                mm(T.PK[0:96, k + 8 * j:128:16], T.MX[:, 256 * k + j:256 * k + 192:2], T.B8P[:], False, False,
+                   ["MX%d_%d" % (c, k) for c in range(2)] + ["B8P"], ["K"], "PK")
+        for k in range(8):
+            larger(2, k)
+            for j in range(2):
+                mm(T.PK[96:128, k + 8 * j:128:16], T.MX[:, 256 * k + 192 + j:256 * k + 256:2], T.B8P[:], False,
+                   False, ["MX2_%d" % k], ["K"], "PK")
+            if k == 7: mm(T.PK[:, 0:128], T.Mt[:], T.BN[:], False, True, MK + ["BN"], ["K"], "PK")
             if k == 0:
-                mm(T.PT[:, 288:296], T.Mb[:], T.wt[:], True, True, ["Mb0", "Mb1", "wt"], ["Tu"], "PT")
-                mm(T.PK[:, 0:128], T.Mb[:], T.BN[:], False, False, ["Mb0", "Mb1", "BN"], ["K"], "PK")
-                act(T.sq[:], T.PT[:, 288:296], ["Tu"], ["sq"], ["PT"], f=AF.Square, scale=0.25)
-                act(T.t74[:], T.PT[:, 288:296], ["Tu"], ["t74"], ["PT"], bias=-0.25, scale=74.0)
-        tt(T.yi[:], T.sq[:], T.t74[:], A.add, ["sq", "t74"], ["yi"])
-        ts(T.zi[:], T.yi[:], 1, 4095, A.logical_shift_right, A.bitwise_and, ["yi"], ["zi"])
+                mm(T.PT[:, 288:296], T.Mt[:], T.wt[:], True, True, MK + ["wt"], ["Tu"], "PT")
+                act(T.sq[:], T.PT[:, 288:296], ["Tu"], ["sq"], ["PT"], f=AF.Square, scale=0.25, bias=-12288.0)
+                act(T.t74[:], T.PT[:, 288:296], ["Tu"], ["t74"], ["PT"], bias=-3637248.25, scale=74.0)
         key = T.PK[:, 0:128]
         bc = T.bc[:, 0:8]
         scan(T.R[:, 0:128], T.D0[:, 0:128], key, A.add, A.min, ["K", "D0"], ["R0"], ["PK"])
         scan(T.R[:, 128:256], T.D0[:, 128:256], key, A.add, A.max, ["K", "D0"], ["R1"], ["PK"])
-        ts(T.Zt[:, 0::16], T.zi[:], -2048.0, None, A.add, None, ["zi"], ["Zt"])
-        mm(T.PW[:, 128:256], T.Zt[:], T.I[:], False, False, ["Zt"], ["WN"], "PW")
-        tt(T.Ni[:], T.R[:, 15:128:16], T.eT[:, 128:136], A.add, ["R0", "eT"], ["Ni"])
         scan(T.R[:, 256:384], T.D0[:, 256:384], key, A.add, A.max, ["K", "D0"], ["R2"], ["PK"])
-        ts(T.NK[:, 0:8], T.Ni[:], 4095, None, A.bitwise_and, None, ["Ni"], ["n"])
+        tt(T.Ni[:], T.R[:, 15:128:16], T.eT[:, 128:136], A.add, ["R0", "eT"], ["Ni"])
+        tt(T.yi[:], T.sq[:], T.t74[:], A.add, ["sq", "t74"], ["yi"])
         tt(T.Ri[:], T.R[:, 143:384:16], T.eT[:, 136:152], A.add, ["R1", "R2", "eT"], ["Ri"])
-        tt(T.eq[:], T.NK[:, 0:8].indirect(bc), T.eT[:, 0:128], A.is_equal, ["n", "bc", "eT"], ["eq"])
+        ts(T.NK[:, 0:8], T.Ni[:], 4095, None, A.bitwise_and, None, ["Ni"], ["n"])
+        ts(T.zi[:], T.yi[:], 1, 4095, A.logical_shift_right, A.bitwise_and, ["yi"], ["zi"])
         ts(T.low[:], T.Ri[:], 4095, None, A.bitwise_and, None, ["Ri"], ["low"])
-        ts(T.Nt[:, 0::16], T.NK[:, 0:8], -2048.0, None, A.add, None, ["n"], ["Nt"])
-        mm(T.PW[:, 0:128], T.Nt[:], T.I[:], False, False, ["Nt"], ["WN"], "PW")
+        tt(T.eq[:], T.NK[:, 0:8].indirect(bc), T.eT[:, 0:128], A.is_equal, ["n", "bc", "eT"], ["eq"])
+        tt(T.ne[:], T.NK[:, 0:8], T.low[:, 0:8], A.not_equal, ["n", "low"], ["ne"])
+        ts(T.c2[:], T.low[:, 8:16], col(12), None, A.add, None, ["low", "s12"], ["c2"])
         ts(T.NK[:, 8:16], T.Ri[:, 0:8], 12, 15, A.logical_shift_right, A.bitwise_and, ["Ri"], ["kk"])
         scan(T.Sc[:], T.rst[:], T.eq[:], A.mult, A.add, ["rst", "eq"], ["Sc"])
         act(T.gG[:], T.Sc[:].indirect(T.b2[:]), ["Sc", "b2", "nth"], ["gG"], f=AF.Sign, bias=T.nth[:, 0:1])
         mm(T.PW[:, 0:128], T.gG[:], T.Ig[:], False, False, ["gG", "Ig"], ["WN"], "PW")
-        mm(T.PW[:, 128:256], T.gG[:], T.Ih[:], False, True, ["gG", "Ih"], ["WN"], "PW")
-        tt(T.ne[:], T.NK[:, 0:8], T.low[:, 0:8], A.not_equal, ["n", "low"], ["ne"])
-        ts(T.c2[:], T.low[:, 8:16], col(12), None, A.add, None, ["low", "s12"], ["c2"])
+        mm(T.PW[:, 128:256], T.gG[:], T.Ih[:], False, False, ["gG", "Ih"], ["WN"], "PW")
+        tt(T.u2[:], T.c2[:], T.ne[:], A.mult, ["c2", "ne"], ["u2"])
         cp(T.NKf[:], T.NK[:], ["n", "kk"], ["NKf"])
         ts(T.go[:, 0:8], T.Sc[:, 15::16], T.par[:, 0:1], 4.0, A.subtract, A.is_ge, ["Sc", "par"], ["go"])
-        tt(T.u2[:], T.c2[:], T.ne[:], A.mult, ["c2", "ne"], ["u2"])
+        ts(T.Nt[:, 0::16], T.NK[:, 0:8], -2048.0, None, A.add, None, ["n"], ["Nt"])
+        ts(T.Zt[:, 0::16], T.zi[:], -2048.0, None, A.add, None, ["zi"], ["Zt"])
+        mm(T.PW[:, 0:128], T.Nt[:], T.I[:], False, False, ["Nt"], ["WN"], "PW")
+        mm(T.PW[:, 128:256], T.Zt[:], T.I[:], False, True, ["Zt"], ["WN"], "PW")
         act(T.gK[:], T.NKf[:, 8:16].indirect(bc), ["NKf", "bc"], ["gK"])
         act(T.gN[:], T.NKf[:, 0:8].indirect(bc), ["NKf", "bc"], ["gN"])
         if t < NV - 1:
@@ -461,7 +479,7 @@ def rank_program(g, core, T, topo):
         if t < NV - 1: ts(T.par[:, 0:1], T.ri[:, 0:1], -2.0, T.Gs[:, 0:1], A.mult, A.add, ["Gs", "ri"], ["par"])
         cp(T.U[:].indirect(T.o1[:]), T.nw[:], ["o1", "nw"], UK)
 
-    cuts = [0, 384, 896, 1408, 1792, 2048]
+    cuts = [0, 256, 768, 1280, 1664, 1920, 2048]
     def high(c):
         a, b = cuts[c], cuts[c + 1]
         ts(T[HB[c]][:, 0:b - a], T.U[:, HI + a:HI + b], 4096.0, None, A.mult, None, UK, ["H%d" % c], [HB[c]])

@@ -1,55 +1,51 @@
 from concourse.bass import DstId, RemoteDMATransfer
-from concourse.mybir import AluOpType as A, ActivationFunctionType as AF
+from concourse.mybir import AluOpType as A, ActivationFunctionType as AF, AxisListType as AX
 
 F32, BF, FH, I32, U16 = "float32", "bfloat16", "float16", "int32", "uint16"
 NV = 4
-CH = [0, 32, 64, 96, 128]
-NC = len(CH) - 1
-YB = ["PY", "PA", "PY", "PB"]
-PC = [0, 64, 96, 128]
-SB = ["PA", "PY", "PB"]
-LA = 5
-MP = 4
-HV = 3
-XV0 = 0
-XV = 0
+FP = [("V", 0, 32), ("S", 32, 64), ("V", 64, 96), ("S", 96, 128)]
+XP = [("V", 0, 32), ("S", 32, 64), ("V", 64, 84), ("S", 84, 128)]
+TG = [(0, 64), (64, 128)]
+XT = [(0, 64), (64, 128)]
+NB = 4
 PAD = 256
+NDM = 328
+FC = [0, 256, 640, 1152, 1664, 2048]
+FS = [0, 128, 256, 320, 384]
+CUTS = [0, 256, 768, 1280, 1664, 1920, 2048]
 SCRATCH = {
     "fs": ("sbuf", [128, 2048], I32), "U": ("sbuf", [128, PAD + 4096], I32), "fo": ("sbuf", [128, 2048], F32),
+    "th": ("sbuf", [128, 2048], I32),
     "r2": ("sbuf", [128, 8192], BF), "wi": ("sbuf", [128, 128], I32), "wo": ("sbuf", [128, 128], F32),
     "G": ("sbuf", [128, 2048], FH), "X": ("sbuf", [128, 2048], BF), "MX": ("sbuf", [128, 2048], BF),
-    "W16": ("sbuf", [128, 128], FH), "e16": ("sbuf", [128, 128], FH), "off": ("sbuf", [128, 128], U16),
-    "tb": ("sbuf", [128, 128], F32), "Mt": ("sbuf", [128, 128], BF), "k0": ("sbuf", [128, 128], BF),
-    "D0": ("sbuf", [128, 384], F32), "Nt": ("sbuf", [128, 128], FH), "gG": ("sbuf", [128, 128], BF),
-    "Ig": ("sbuf", [128, 128], BF), "Ih": ("sbuf", [128, 128], BF), "eT": ("sbuf", [128, 152], F32),
-    "R": ("sbuf", [128, 384], F32), "Ni": ("sbuf", [128, 8], I32), "Ri": ("sbuf", [128, 16], I32),
-    "NK": ("sbuf", [128, 16], I32), "NKf": ("sbuf", [128, 16], F32), "low": ("sbuf", [128, 16], I32),
-    "eq": ("sbuf", [128, 128], BF), "Sc": ("sbuf", [128, 128], BF), "go": ("sbuf", [128, 16], BF),
-    "b2": ("sbuf", [128, 8], U16), "nth": ("sbuf", [128, 8], F32),
-    "tT": ("sbuf", [128, 256], F32), "ne": ("sbuf", [128, 8], F32), "c2": ("sbuf", [128, 8], F32),
-    "u2": ("sbuf", [128, 8], F32), "cw": ("sbuf", [128, 8], F32), "bC": ("sbuf", [128, 128], FH),
-    "cf": ("sbuf", [128, 8], FH), "B8f": ("sbuf", [128, 8], F32),
-    "bM": ("sbuf", [128, 128], F32), "nB": ("sbuf", [128, 8], F32), "cB": ("sbuf", [128, 16], F32),
-    "E": ("sbuf", [128, 576], BF), "Rd": ("sbuf", [128, 576], BF), "rr": ("sbuf", [128, 16], F32),
-    "o1": ("sbuf", [128, 8], U16), "o0": ("sbuf", [128, 8], U16), "gN": ("sbuf", [128, 128], F32), "gK": ("sbuf", [128, 128], BF),
-    "ab": ("sbuf", [128, 128], BF), "sg": ("sbuf", [128, 128], BF), "om": ("sbuf", [128, 128], F32),
-    "nw": ("sbuf", [128, 128], I32), "sq": ("sbuf", [128, 8], F32), "t74": ("sbuf", [128, 8], F32),
-    "yi": ("sbuf", [128, 8], I32), "zi": ("sbuf", [128, 8], I32), "Zt": ("sbuf", [128, 128], FH),
-    "jk": ("sbuf", [128, 8], F32), "Gs": ("sbuf", [128, 8], F32), "ri": ("sbuf", [128, 8], I32),
-    "par": ("sbuf", [128, 8], F32),
-    "pi": ("sbuf", [128, 8], I32), "sc": ("sbuf", [128, 32], F32), "Cm": ("sbuf", [128, 128], F32),
+    "W16": ("sbuf", [128, 256], FH), "e16": ("sbuf", [128, 128], FH), "off": ("sbuf", [128, 128], U16),
+    "tb": ("sbuf", [128, 128], F32), "Mt": ("sbuf", [128, 128], BF), "eT": ("sbuf", [128, 128], F32),
+    "R": ("sbuf", [128, 256], I32), "NK": ("sbuf", [128, 40], I32), "eq": ("sbuf", [128, 128], BF),
+    "Sc": ("sbuf", [128, 128], BF), "ngo": ("sbuf", [128, 128], BF), "ne": ("sbuf", [128, 8], F32),
+    "c2": ("sbuf", [128, 8], F32), "u2": ("sbuf", [128, 8], F32), "cb": ("sbuf", [128, 128], FH),
+    "cM": ("sbuf", [128, 128], FH), "E": ("sbuf", [128, NDM], BF), "Rd": ("sbuf", [128, NDM], BF),
+    "o0": ("sbuf", [128, 16], U16), "o1": ("sbuf", [128, 16], U16),
+    "gK": ("sbuf", [128, 128], BF), "gN": ("sbuf", [128, 128], FH), "ab": ("sbuf", [128, 128], BF),
+    "sg": ("sbuf", [128, 128], BF), "om": ("sbuf", [128, 128], F32), "nw": ("sbuf", [128, 128], I32),
+    "Nt": ("sbuf", [128, 128], FH), "Zt": ("sbuf", [128, 128], FH), "sq": ("sbuf", [128, 8], F32),
+    "yi": ("sbuf", [128, 8], I32),
+    "tT": ("sbuf", [128, 256], F32), "jk": ("sbuf", [128, 8], F32), "Gs": ("sbuf", [128, 8], F32),
+    "ri": ("sbuf", [128, 8], I32), "par": ("sbuf", [128, 8], F32),
+    "pi": ("sbuf", [128, 8], I32), "sc": ("sbuf", [128, 32], F32), "Cm": ("sbuf", [128, 130], BF),
     "Ck": ("sbuf", [128, 128], BF), "Cg": ("sbuf", [128, 128], BF), "I": ("sbuf", [128, 128], BF),
     "If": ("sbuf", [128, 128], F32), "Dk": ("sbuf", [128, 2048], BF), "km": ("sbuf", [128, 16], F32),
     "SoN": ("sbuf", [128, 128], BF), "SoP": ("sbuf", [128, 128], BF), "Sh": ("sbuf", [128, 128], BF),
-    "Rev": ("sbuf", [128, 128], BF), "J": ("sbuf", [128, 128], BF), "BN": ("sbuf", [128, 128], BF),
-    "m16": ("sbuf", [128, 128], BF), "rst": ("sbuf", [128, 128], BF), "T0": ("sbuf", [128, 128], BF),
-    "B8": ("sbuf", [128, 8], BF), "B8P": ("sbuf", [128, 8], BF), "B8N": ("sbuf", [128, 8], BF),
-    "wt": ("sbuf", [128, 8], BF), "Dm": ("sbuf", [128, 128], BF),
-    "Inz": ("sbuf", [128, 128], BF), "I16": ("sbuf", [128, 128], BF), "IN": ("sbuf", [128, 128], BF),
-    "Iod": ("sbuf", [128, 128], BF), "dm": ("sbuf", [128, 576], BF), "cd": ("sbuf", [128, 8], F32),
-    "C1": ("sbuf", [128, 384], BF), "cm": ("sbuf", [128, 64], BF), "c2k": ("sbuf", [128, 64], BF),
-    "zr": ("sbuf", [128, 128], BF), "on": ("sbuf", [128, 128], BF), "bc": ("sbuf", [128, 8], U16),
-    "en": ("sbuf", [128, 2], U16),
+    "Rev": ("sbuf", [128, 128], BF), "BN": ("sbuf", [128, 256], BF),
+    "m16": ("sbuf", [128, 128], BF), "rst": ("sbuf", [128, 128], BF), "d0": ("sbuf", [128, 128], BF),
+    "B8": ("sbuf", [128, 8], BF), "BX": ("sbuf", [128, 16], BF), "BM": ("sbuf", [128, 16], BF),
+    "wt": ("sbuf", [128, 8], BF), "Kc": ("sbuf", [128, 256], BF),
+    "I16": ("sbuf", [128, 128], BF), "IN": ("sbuf", [128, 128], BF), "Iod": ("sbuf", [128, 128], BF),
+    "Ig": ("sbuf", [128, 128], BF), "Ih": ("sbuf", [128, 128], BF), "Cw": ("sbuf", [128, 256], BF),
+    "cm": ("sbuf", [128, 64], BF), "c2k": ("sbuf", [128, 128], BF), "on": ("sbuf", [128, 136], BF),
+    "Sel": ("sbuf", [128, NDM], BF), "Blk": ("sbuf", [128, NDM], BF), "Own": ("sbuf", [128, NDM], BF),
+    "dm": ("sbuf", [128, NDM], BF), "Up": ("sbuf", [128, NDM], BF),
+    "bc": ("sbuf", [128, 8], U16), "b2": ("sbuf", [128, 8], U16), "en": ("sbuf", [128, 2], U16),
+    "ends": ("sbuf", [128, 8], F32), "pick": ("sbuf", [128, 8], F32),
 }
 for _t in range(NV):
     SCRATCH["Wu%d" % _t] = ("sbuf", [128, 128], U16)
@@ -170,6 +166,11 @@ def rank_program(g, core, T, topo):
         if acc is None: op("S", lambda: s.activation(out, a, f, bias=bias, scale=scale), r, w, b)
         else: op("S", lambda: s.activation(out, a, f, bias=bias, scale=scale, accum_out=acc), r, w, b)
 
+    def lin(e, out, a, scale, bias, r, w, b=()):
+        if e == "S": act(out, a, r, w, b, bias=bias, scale=scale)
+        elif scale == 1.0: ts(out, a, bias, None, A.add, None, r, w, b)
+        else: ts(out, a, scale, bias, A.mult, A.add, r, w, b)
+
     def mm(out, l, rh, st, sp, r, w, b):
         op("P", lambda: pe.matmul(out, l, rh, st, sp), r, w, [b])
 
@@ -177,317 +178,334 @@ def rank_program(g, core, T, topo):
         qq = g.sync if e == "Y" else g.scalar
         op(e, lambda: qq.dma_start(out, a), r, w, kind="dma")
 
+    def iota(out, pat, base, w):
+        op("G", lambda: g.iota(out, pat, base, 0, allow_small_or_imprecise_dtypes=True), [], w)
+
+    def select(out, a, pat, cmp, base, mul, r, w):
+        op("G", lambda: g.affine_select(out, a, pat, cmp, 0.0, base, mul), r, w)
+
     def col(i):
         return T.sc[:, i:i + 1]
 
-    FC = [0, 256, 640, 1152, 1664, 2048]
-    FL = [2, 1]
-    UK = ["U%d" % i for i in range(2 * len(FC) - 2)] + ["Ud"]
+    NP = len(FC) - 1
+    UK = ["U%d" % i for i in range(3 * NP)] + ["Ud"]
     LO, HI = PAD, PAD + 2048
+    NS = 8 // NB
+    RL = [16 * r + 17 for r in range(NB)]
+    RS = [NS * sum(RL[:r]) for r in range(NB + 1)]
+    ND = RS[NB]
 
     dma("S", T.wi[:], T.wnd[:], [], ["wi"])
-    for c in range(len(FC) - 1):
+    for c in range(NP):
         dma("Y", T.fs[:, FC[c]:FC[c + 1]], T.fld[:, FC[c]:FC[c + 1]], [], ["fs%d" % c])
-    dma("Y", T.r2[:, 0:4096], T.rec[:, :], [], ["ra0", "ra1"])
-    op("Y", lambda: g.sync.dma_start(T.r2[:, 4096:8192], T.rec[:, :]), ["ra0", "ra1"], ["rb"], kind="dma")
+    dma("Y", T.r2[:, 0:4096], T.rec[:, :], [], ["ra"])
+    dma("Y", T.r2[:, 4096:8192], T.rec[:, :], ["ra"], ["rb"])
 
     op("G", lambda: g.iota(T.pi[:, 0:1], [[0, 1]], 0, 1), [], ["pi0"])
-    op("G", lambda: g.iota(T.Cm[:], [[1, 128]], 0, 0, allow_small_or_imprecise_dtypes=True), [], ["Cm"])
-    op("G", lambda: g.iota(T.Ck[:], [[0, 8], [1, 16]], 0, 0, allow_small_or_imprecise_dtypes=True), [], ["Ck"])
-    op("G", lambda: g.iota(T.Cg[:], [[1, 8], [0, 16]], 0, 0, allow_small_or_imprecise_dtypes=True), [], ["Cg"])
-    ms(T.C1[:, 0:128], -4096.0, ["C1a"]); ms(T.C1[:, 128:384], 4096.0, ["C1b"])
-    ms(T.k0[:], 3072.0 * 65536, ["k0"])
-    ms(T.zr[:], 0.0, ["zr"]); ms(T.on[:], 1.0, ["on"]); ms(T.cm[:], -15.0 / 32, ["cm"]); ms(T.c2k[:], 2048.0, ["c2k"])
-    ts(T.pi[:, 1:2], T.pi[:, 0:1], 15, None, A.bitwise_and, None, ["pi0"], ["pi1"])
-    ts(T.pi[:, 2:3], T.pi[:, 0:1], 4, None, A.logical_shift_right, None, ["pi0"], ["pi2"])
-    ts(T.pi[:, 3:4], T.pi[:, 0:1], 1, None, A.bitwise_and, None, ["pi0"], ["pi3"])
-    ms(T.C1[:, 0:128:16], BIG, ["C1a"]); ms(T.C1[:, 128:384:16], -BIG, ["C1b"])
-    cp(T.sc[:, 0:4], T.pi[:, 0:4], ["pi0", "pi1", "pi2", "pi3"], ["s0"])
-    ms(T.U[:, 0:PAD], 0, ["Ud"]); ms(T.par[:], 0.0, ["par"]); ms(T.cB[:], 0.0, ["cB"])
-    P_, K_, G_, O_ = 0, 1, 2, 3
-    for i, (src, sc_, bi) in {4: (P_, 1.0, 1.0), 5: (O_, 1.0, -1.0), 6: (P_, -1.0, 127.0), 7: (P_, 1.0, 15.0),
-                              9: (K_, -1.0, 15.0), 10: (K_, 8192.0, -15.0 * 8192), 11: (O_, -2048.0, 0.0),
-                              12: (P_, -2.0, float(PAD)), 13: (P_, 2.0, -2048.0 - PAD), 14: (K_, 2.0, 1.0),
-                              15: (K_, 2.0, 0.0)}.items():
-        act(col(i), col(src), ["s0"], ["s%d" % i], bias=bi, scale=sc_)
-    act(col(8), col(K_), ["s0", "s7"], ["s8"], bias=col(7), scale=-2.0)
-    act(col(16), col(9), ["s9"], ["s16"], f=AF.Sign)
-    act(col(17), col(K_), ["s0"], ["s17"], f=AF.Sign)
-    ts(T.I[:], T.Cm[:], col(P_), None, A.is_equal, None, ["Cm", "s0"], ["I"])
-    ts(T.km[:], T.Cm[:, 0:16], col(K_), None, A.is_equal, None, ["Cm", "s0"], ["km"])
-    ts(T.SoN[:], T.Cm[:], col(4), col(5), A.is_equal, A.mult, ["Cm", "s4", "s5"], ["SoN"])
-    ts(T.B8[:], T.Cm[:, 0:8], col(G_), None, A.is_equal, None, ["Cm", "s0"], ["B8"])
-    ts(T.T0[:], T.Cm[:], col(9), 1048576.0, A.is_le, A.mult, ["Cm", "s9"], ["T0"])
-    ts(col(18), col(K_), 7.0, 1.5, A.min, A.add, ["s0"], ["s18"])
-    cp(T.bc[:], T.Cm[:, 0:8], ["Cm"], ["bc"])
-    cp(T.Zt[:], T.zr[:], ["zr"], ["Zt"])
-    cp(T.Nt[:], T.zr[:], ["zr"], ["Nt"])
-    cp(T.Wu0[:], T.wi[:], ["wi"], ["Wu0"])
-    act(T.Inz[:], T.I[:], ["I", "s17"], ["Inz"], scale=col(17))
+    iota(T.Cm[:], [[1, 130]], -2, ["Cm"])
+    iota(T.Ck[:], [[0, 8], [1, 16]], 0, ["Ck"])
+    iota(T.Cg[:], [[1, 8], [0, 16]], 0, ["Cg"])
+    for r in range(NB):
+        iota(T.ends[:, r::NB], [[RL[r], NS]], RS[r] + RL[r] - 1, ["ends%d" % r])
+    Cm, C1 = T.Cm[:, 2:130], T.Cm[:, 1:129]
+    ms(T.on[:], 1.0, ["on"]); ms(T.cm[:], -15.0 / 32, ["cm"]); ms(T.c2k[:], 2048.0, ["c2k"])
+    ms(T.d0[:], 4096.0, ["d0"]); ms(T.U[:, 0:PAD], 0, ["Ud"])
+    for i, m in enumerate((15, 1, 16 * NB - 1)):
+        ts(T.pi[:, 1 + i:2 + i], T.pi[:, 0:1], m, None, A.bitwise_and, None, ["pi0"], ["pi%d" % (1 + i)])
+    ts(T.pi[:, 4:5], T.pi[:, 0:1], 4, None, A.logical_shift_right, None, ["pi0"], ["pi4"])
+    ms(T.d0[:, 0:128:16], -BIG, ["d0"]); ms(T.par[:], 0.0, ["par"])
+    cp(T.sc[:, 0:5], T.pi[:, 0:5], ["pi0", "pi1", "pi2", "pi3", "pi4"], ["s0"])
+    P_, K_, O_, Q_, G_ = 0, 1, 2, 3, 4
+    ms(T.Kc[0:64, 0:128], -(16.0 * 192 - 16) * 1024, ["Kc0"])
+    ms(T.Kc[0:64, 128:256], (16.0 * 192 - 16) * 1024, ["Kc1"])
+    ts(T.I[:], Cm, col(P_), None, A.is_equal, None, ["Cm", "s0"], ["I"])
+    ts(T.km[:], T.Cm[:, 2:18], col(K_), None, A.is_equal, None, ["Cm", "s0"], ["km"])
+    ts(col(6), col(O_), -1.0, None, A.add, None, ["s0"], ["s6"])
+    ts(T.B8[:], T.Cm[:, 2:10], col(G_), None, A.is_equal, None, ["Cm", "s0"], ["B8"])
     for k in range(16):
-        act(T.Dk[:, 128 * k:128 * k + 128], T.I[:], ["I", "km"], ["Dk%d" % k], scale=T.km[:, k:k + 1])
-    act(col(19), col(18), ["s18"], ["s19"], f=AF.Square)
-    act(T.I16[:], T.I[:], ["I"], ["I16"], scale=1.0 / 16)
-    act(T.If[:], T.I[:], ["I"], ["If"])
-    act(T.IN[:], T.I[:], ["I"], ["IN"], scale=-1.0)
-    act(T.Ig[:], T.I[:], ["I"], ["Ig"], scale=4096.0)
-    act(T.Ih[:], T.I[:], ["I"], ["Ih"], scale=-4096.0)
-    act(T.Iod[:], T.I[:], ["I", "s11"], ["Iod"], scale=col(11))
-    act(T.SoP[:], T.SoN[:], ["SoN"], ["SoP"], scale=-1.0)
-    act(T.B8f[:], T.B8[:], ["B8"], ["B8f"])
-    act(T.B8P[:], T.B8[:], ["B8"], ["B8P"], scale=131072.0)
-    act(T.B8N[:], T.B8[:], ["B8"], ["B8N"], scale=-65536.0)
-    act(T.wt[:], T.B8[:], ["B8", "s14"], ["wt"], scale=col(14))
-    act(T.cd[:], T.Cm[:, 0:8], ["Cm", "s15"], ["cd"], bias=col(15), scale=32.0)
-    for h in range(8):
-        st = 8 * h * (h + 1)
-        act(T.dm[:, st:st + 16 * h + 16], T.T0[:, 0:16 * h + 16], ["T0", "cd"], ["dm%d" % h], bias=T.cd[:, h:h + 1])
+        if k % 2: act(T.Dk[:, 128 * k:128 * k + 128], T.I[:], ["I", "km"], ["Dk%d" % k], scale=T.km[:, k:k + 1])
+        else: ts(T.Dk[:, 128 * k:128 * k + 128], T.I[:], T.km[:, k:k + 1], None, A.mult, None, ["I", "km"], ["Dk%d" % k])
+    ts(T.SoN[:], C1, col(P_), col(6), A.is_equal, A.mult, ["Cm", "s0", "s6"], ["SoN"])
+    cp(T.bc[:], T.Cm[:, 2:10], ["Cm"], ["bc"])
+    ms(T.Kc[64:128, :], 32.0, ["Kc2"])
+    ms(T.Cw[:, 0:128], 0.0, ["Cw0"]); ms(T.Cw[:, 128:256], -8192.0, ["Cw1"])
+    cp(T.Wu0[:], T.wi[:], ["wi"], ["Wu0"])
+    for r in range(NB):
+        a, b, ln = RS[r], RS[r + 1], RL[r]
+        on = T.on[:, 0:b - a]
+        top = [[16 * NB, NS], [-1, ln]]
+        own = [[16 * NB, NS], [0, ln]]
+        select(T.Up[:, a:b], on, [[-16 * NB, NS], [0, ln]], A.is_ge, -16 * r, 1, ["on"], ["Up%d" % r])
+        select(T.Sel[:, a:b], on, top, A.is_equal, 16 * r + 16, -1, ["on"], ["Sel%d" % r])
+        select(T.Blk[:, a:b], T.Up[:, a:b], own, A.is_ge, 16 * r + 15, -1, ["Up%d" % r], ["Blk%d" % r])
+        select(T.Own[:, a:b], T.Blk[:, a:b], top, A.is_equal, 16 * r + 16, -1, ["Blk%d" % r], ["Own%d" % r])
+        select(T.Up[:, a:b], T.Blk[:, a:b], top, A.is_gt, 16 * r + 16, -1, ["Blk%d" % r], ["Up%d" % r])
 
-    late = [
-        lambda: ts(T.Sh[:], T.Cm[:], col(4), col(16), A.is_equal, A.mult, ["Cm", "s4", "s16"], ["Sh"]),
-        lambda: ts(T.Rev[:], T.Cm[:], col(8), col(16), A.is_equal, A.mult, ["Cm", "s8", "s16"], ["Rev"]),
-        lambda: tt(T.Dm[:], T.Sh[:], T.Inz[:], A.subtract, ["Sh", "Inz"], ["Dm"]),
-        lambda: ts(T.J[:], T.Cm[:], col(6), None, A.is_equal, None, ["Cm", "s6"], ["J"]),
-        lambda: ts(T.BN[:], T.Cg[:], col(G_), -65536.0, A.is_equal, A.mult, ["Cg", "s0"], ["BN"]),
-        lambda: ts(T.m16[:], T.Ck[:], col(K_), None, A.is_equal, None, ["Ck", "s0"], ["m16"]),
+    def allr(name):
+        return [name + str(r) for r in range(NB)]
+
+    def cols(*ids):
+        how = {7: (P_, 1.0, 15.0), 9: (K_, -1.0, 15.0), 10: (K_, 8192.0, -15.0 * 8192), 11: (O_, -2048.0, 0.0),
+               12: (Q_, -2.0, PAD - 128.0), 13: (Q_, -2.0 / 8192, (PAD + 2048.0 - 128) / 8192), 14: (K_, 2.0, 1.0)}
+        return [lambda i=i: act(col(i), col(how[i][0]), ["s0"], ["s%d" % i], bias=how[i][2], scale=how[i][1])
+                for i in ids]
+    lateS = cols(7, 9) + [
+        lambda: act(T.I16[:], T.I[:], ["I"], ["I16"], scale=1.0 / 16),
+        lambda: act(col(8), col(K_), ["s0", "s7"], ["s8"], bias=col(7), scale=-2.0),
+        lambda: act(col(16), col(9), ["s9"], ["s16"], f=AF.Sign),
+        lambda: act(T.BX[:, 0:8], T.B8[:], ["B8"], ["BX0"], scale=65536.0),
+        lambda: act(T.BX[:, 8:16], T.B8[:], ["B8"], ["BX1"], scale=-65536.0),
+    ] + cols(14, 11, 10, 12, 13) + [
+        lambda: act(T.BM[:], T.BX[:], ["BX0", "BX1"], ["BM"], scale=-2.0),
+        lambda: act(T.wt[:], T.B8[:], ["B8", "s14"], ["wt"], scale=col(14)),
+    ]
+    lastS = [
+        lambda: act(T.IN[:], T.I[:], ["I"], ["IN"], scale=-1.0),
+        lambda: act(T.Ig[:], T.I[:], ["I"], ["Ig"], scale=8192.0),
+        lambda: act(T.Ih[:], T.I[:], ["I"], ["Ih"], scale=-8192.0),
+        lambda: act(T.Iod[:], T.I[:], ["I", "s11"], ["Iod"], scale=col(11)),
+        lambda: act(T.SoP[:], T.SoN[:], ["SoN"], ["SoP"], scale=-1.0),
+        lambda: act(T.If[:], T.I[:], ["I"], ["If"]),
+    ]
+    lateV = [
+        lambda: ts(T.BN[:, 0:128], T.Cg[:], col(G_), 65536.0, A.is_equal, A.mult, ["Cg", "s0"], ["BN0"]),
+        lambda: ts(T.BN[:, 128:256], T.Cg[:], col(G_), -65536.0, A.is_equal, A.mult, ["Cg", "s0"], ["BN1"]),
+        lambda: ts(T.m16[:], T.Ck[:], col(K_), -1.0, A.is_equal, A.mult, ["Ck", "s0"], ["m16"]),
         lambda: ts(T.rst[:], T.Ck[:], 0.0, None, A.not_equal, None, ["Ck"], ["rst"]),
-        lambda: ts(T.b2[:], T.Cm[:, 0:8], 16.0, 15.0, A.mult, A.add, ["Cm"], ["b2"]),
-        lambda: ts(T.cf[:], T.cd[:], -2048.0 - PAD, None, A.add, None, ["cd"], ["cf"]),
-        lambda: ts(T.en[:, 0:1], col(19), 8.0, -3.0, A.mult, A.add, ["s19"], ["en"]),
+        lambda: ts(T.b2[:], T.Cm[:, 2:10], 16.0, 15.0, A.mult, A.add, ["Cm"], ["b2"]),
+        lambda: tt(T.pick[:], T.km[:, 0:8], T.ends[:], A.mult, ["km"] + allr("ends"), ["pick"]),
+        lambda: ms(T.Zt[:], 0.0, ["Zt"]),
+        lambda: ts(T.sc[:, 20:20 + NB], T.Cm[:, 2:2 + NB], 16.0, col(K_), A.mult, A.add, ["Cm", "s0"], ["s20"]),
+        lambda: op("V", lambda: v.tensor_reduce(col(19), T.pick[:], AX.X, A.add), ["pick"], ["s19"]),
+        lambda: ms(T.Nt[:], 0.0, ["Nt"]),
+        lambda: ms(T.o0[:], 0, ["o0"]),
+        lambda: cp(T.en[:, 0:1], col(19), ["s19"], ["en"]),
+        lambda: ts(T.Sh[:], C1, col(P_), col(16), A.is_equal, A.mult, ["Cm", "s0", "s16"], ["Sh"]),
+        lambda: ts(T.Rev[:], Cm, col(8), col(16), A.is_equal, A.mult, ["Cm", "s8", "s16"], ["Rev"]),
     ]
 
-    def filler(cnt):
+    def filler(late, cnt):
         for _ in range(min(cnt, len(late))): late.pop(0)()
 
-    for c in range(len(FC) - 1):
-        a, b = FC[c], FC[c + 1]
-        ts(T.U[:, LO + a:LO + b], T.fs[:, a:b], 4095, None, A.bitwise_and, None, ["fs%d" % c], ["U%d" % (2 * c)])
-        ts(T.U[:, HI + a:HI + b], T.fs[:, a:b], 12, None, A.logical_shift_right, None, ["fs%d" % c], ["U%d" % (2 * c + 1)])
-        if c < 2: filler(FL[c])
+    def floors():
+        mm(T.PD[:, 0:ND], T.m16[:], T.Up[:, 0:ND], True, True, ["m16"] + allr("Up"), ["D"], "PD")
+        for r in range(NB):
+            act(T.dm[:, RS[r]:RS[r + 1]], T.PD[:, RS[r]:RS[r + 1]], ["D", "s20"], ["dm%d" % r], ["PD"],
+                bias=col(20 + r), scale=-8192.0)
 
+    def upper(c):
+        m, b = FC[c] + FS[c], FC[c + 1]
+        if m < b: act(T.U[:, HI + m:HI + b], T.th[:, m:b], ["th%d" % c], ["U%d" % (3 * c + 2)], bias=2047.0)
+
+    lin("S", T.W16[:, 0:128], T.Wu0[:], 1.0, -2048.0, ["Wu0"], ["W16_0"])
+    for c in range(NP):
+        a, b = FC[c], FC[c + 1]
+        m = min(a + FS[c], b)
+        k = ["fs%d" % c]
+        ts(T.U[:, LO + a:LO + b], T.fs[:, a:b], 4095, None, A.bitwise_and, None, k, ["U%d" % (3 * c)])
+        if m > a: ts(T.U[:, HI + a:HI + m], T.fs[:, a:m], 12, None, A.logical_shift_right, None, k, ["U%d" % (3 * c + 1)])
+        if m < b:
+            act(T.th[:, m:b], T.fs[:, m:b], k, ["th%d" % c], bias=-2047.5 + 2.0 ** -13, scale=2.0 ** -12)
+        if c: upper(c - 1)
+        else: filler(lateS, 2)
+        if c < 2: filler(lateV, 2)
+    filler(lateS, 3)
+    upper(NP - 1)
+
+    HV = [(0, 64), (64, 128)]
+    YB, SB = ["PY", "PA"], ["PB", "PY", "PA"]
+    NG = len(TG)
+    bc = T.bc[:, 0:8]
     for t in range(NV):
         Wu, wk = T["Wu%d" % t], "Wu%d" % t
+        W16, w16 = T.W16[:, 128 * (t % 2):128 * (t % 2) + 128], "W16_%d" % (t % 2)
         if t:
             op("V", None, [], [wk], kind="arrive", sem=T.sem["arr%d" % t], val=n_in)
 
-        def fgather(c):
-            a, b = CH[c], CH[c + 1]
-            ts(T.G[:, 16 * a:16 * b], T.U[:, LO:LO + 4096].indirect(Wu[:, a:b]), -2048.0, None,
-               A.add, None, UK + [wk], ["G%d" % c])
+        def parts(P, ab, name):
+            return [name + str(i) for i, p in enumerate(P) if p[-2] < ab[1] and ab[0] < p[-1]]
 
-        def extract(c, between=None):
-            a, b = CH[c], CH[c + 1]
-            yb = YB[c]
-            y = T[yb][:, a:b]
-            yk = ["Y%d" % c, {"PB": "QK", "PA": "cS", "PY": "cV"}[yb]]
-            mm(y, T.SoN[:], T.c2k[:, 0:b - a], True, False, ["SoN", "c2k"], yk, yb)
-            mm(y, T.SoN[:], T.W16[:, a:b], False, False, ["W16"], yk, yb)
-            if between: between()
+        def fgather(c):
+            e, a, b = FP[c]
+            lin(e, T.G[:, 16 * a:16 * b], T.U[:, LO:LO + 4096].indirect(Wu[:, a:b]), 1.0, -2048.0, UK + [wk], ["G%d" % c])
+
+        def xgather(c):
+            e, a, b = XP[c]
+            win, rk = (T.r2[:, 0:8192], ["ra", "rb"]) if t else (T.r2[:, 0:4096], ["ra"])
+            lin(e, T.X[:, 16 * a:16 * b], win.indirect(T.off[:, a:b]), 1.0, -8.0, rk + parts(HV, (a, b), "off"), ["X%d" % c])
+
+        def extract(h):
+            a, b = HV[h]
+            y, yb, yk = T[YB[h]][:, 0:64], YB[h], ["Y%d" % h]
+            mm(y, T.SoN[:], T.c2k[:, 0:64], True, False, ["SoN", "c2k"], yk, yb)
+            mm(y, T.SoN[:], T.W16[:, 128 * (t % 2) + a:128 * (t % 2) + b], False, False, [w16], yk, yb)
             for k in range(16):
                 mm(y, T.Dk[:, 128 * k:128 * k + 128], T.G[:, 16 * a + k:16 * b:16], False, k == 15,
-                   ["Dk%d" % k, "G%d" % c], yk, yb)
+                   ["Dk%d" % k] + parts(FP, HV[h], "G"), yk, yb)
 
-        def names(c):
-            a, b = CH[c], CH[c + 1]
-            sl = slice(a, b)
-            yb = YB[c]
+        def below(h):
+            a, b = HV[h]
+            ts(T.tb[:, a:b], T[YB[h]][:, 0:64], -2048.0, 4096.0, A.is_lt, A.mult, ["Y%d" % h], ["tb%d" % h], [YB[h]])
+
+        def name(h):
+            a, b = HV[h]
+            tt(T.e16[:, a:b], T[YB[h]][:, 0:64], T.tb[:, a:b], A.add, ["Y%d" % h, "tb%d" % h], ["e%d" % h], [YB[h]])
+
+        def offsets(h):
+            a, b = HV[h]
             if t:
-                ts(T.off[:, sl], T[yb][:, sl], 6144.0, None, A.add, None, ["Y%d" % c], ["off%d" % c], [yb])
-                win, rk = T.r2[:, 0:8192], ["ra0", "ra1", "rb"]
+                lin("V", T.off[:, a:b], T[YB[h]][:, 0:64], 1.0, 6144.0, ["Y%d" % h], ["off%d" % h], [YB[h]])
             else:
-                ts(T.tb[:, sl], T[yb][:, sl], -2048.0, 4096.0, A.is_lt, A.mult, ["Y%d" % c], ["tb%d" % c], [yb])
-                if c < 3: filler(1)
-                tt(T.e16[:, sl], T[yb][:, sl], T.tb[:, sl], A.add, ["Y%d" % c, "tb%d" % c], ["e%d" % c], [yb])
-                if c < 3: filler(1)
-                ts(T.off[:, sl], T.e16[:, sl], 2048.0, None, A.add, None, ["e%d" % c], ["off%d" % c])
-                win, rk = T.r2[:, 0:4096], ["ra0", "ra1"]
-            m = b - (XV if t else XV0) if c == NC - 1 else b
-            if m > a: act(T.X[:, 16 * a:16 * m], win.indirect(T.off[:, a:m]), rk + ["off%d" % c], ["X%d" % c])
-            if m < b: cp(T.X[:, 16 * m:16 * b], win.indirect(T.off[:, m:b]), rk + ["off%d" % c], ["Xv"])
+                below(h); filler(lateV, 2); name(h); filler(lateV, 2)
+                lin("V", T.off[:, a:b], T.e16[:, a:b], 1.0, 2048.0, ["e%d" % h], ["off%d" % h])
 
-        def wthings(part):
-            if part == 0:
-                mm(T.PK[:, 0:128], T.I[:], T.k0[:], True, False, ["I", "k0"], ["K"], "PK")
-                mm(T.PD[:, 0:384], T.I[:], T.C1[:], True, False, ["C1a", "C1b"], ["D"], "PD")
-                mm(T.PD[:, 256:384], T.W16[:], T.Dm[:], False, False, ["W16", "Dm"], ["D"], "PD")
-                return
-            mm(T.PT[:, 272:280], T.W16[:], T.I[:, 15::16], True, True, ["W16"], ["Te"], "PT")
-            mm(T.PW[:, 0:256], T.zr[:], T.Dk[:, 0:256], True, False, ["zr"], ["WN"], "PW")
-            mm(T.PW[:, 0:128], T.Sh[:], T.W16[:], False, False, ["W16", "Sh"], ["WN"], "PW")
-            mm(T.PW[:, 128:256], T.Rev[:], T.W16[:], False, False, ["W16", "Rev"], ["WN"], "PW")
-
-        def total(hf):
-            a, b = PC[hf], PC[hf + 1]
-            ps = T[SB[hf]][:, 320:320 + b - a]
-            mm(ps, T.I[:], T.cm[:, 0:b - a], True, False, ["cm"], ["S%d" % hf], SB[hf])
+        def total(h):
+            a, b = TG[h]
+            ps = T[SB[h]][:, 320:320 + b - a]
+            mm(ps, T.I[:], T.cm[:, 0:b - a], True, False, ["cm"], ["S%d" % h], SB[h])
             for k in range(16):
-                mm(ps, T.I16[:], T.X[:, 16 * a + k:16 * b:16], False, k == 15, ["I16"] + XH[hf], ["S%d" % hf], SB[hf])
+                mm(ps, T.I16[:], T.X[:, 16 * a + k:16 * b:16], False, k == 15, ["I16"] + parts(XP, TG[h], "X"),
+                   ["S%d" % h], SB[h])
 
-        def mean(hf):
-            a, b = PC[hf], PC[hf + 1]
-            ps = T[SB[hf]][:, 320:320 + b - a]
+        def xterm(h):
+            a, b = XT[h]
+            for k in range(16):
+                mm(T.PK[a:b, k:256:16], T.X[:, 16 * a + k:16 * b:16], T.BX[:], False, False,
+                   parts(XP, XT[h], "X") + ["BX0", "BX1"], ["K"], "PK")
+
+        def mean(h):
+            a, b = TG[h]
+            ps = T[SB[h]][:, 320:320 + b - a]
             for j in range(2):
-                ts(T.PM[:, 2 * a + j:2 * b:2], ps, MAGIC, -MAGIC, A.add, A.add, ["S%d" % hf],
-                   ["M%d_%d" % (hf, j)], [SB[hf], "PM"])
-            act(T.Mt[:, a:b], ps, ["S%d" % hf], ["Mt%d" % hf], [SB[hf]], bias=192.0)
+                ts(T.PM[:, 2 * a + j:2 * b:2], ps, MAGIC, -MAGIC, A.add, A.add, ["S%d" % h],
+                   ["M%d_%d" % (h, j)], [SB[h], "PM"])
+            lin("V" if h == NG - 1 else "S", T.Mt[:, a:b], ps, 1.0, 192.0, ["S%d" % h], ["Mt%d" % h], [SB[h]])
 
-        def larger(hf, k):
-            a, b = PC[hf], PC[hf + 1]
-            tt(T.MX[:, 256 * k + 2 * a:256 * k + 2 * b], T.X[:, 16 * a + k:16 * b:8], T.PM[:, 2 * a:2 * b],
-               A.max, XH[hf] + ["M%d_0" % hf, "M%d_1" % hf], ["MX%d_%d" % (hf, k)], ["PM"])
+        def larger(h, k):
+            a, b = TG[h]
+            tt(T.MX[:, 256 * k + 2 * a:256 * k + 2 * b], T.X[:, 16 * a + k:16 * b:8], T.PM[:, 2 * a:2 * b], A.max,
+               parts(XP, TG[h], "X") + ["M%d_0" % h, "M%d_1" % h], ["MX%d_%d" % (h, k)], ["PM"])
 
-        EK = ["e%d" % c for c in range(NC)]
-        YK = ["Y%d" % c for c in range(NC)]
-        XH = [["X0", "X1"], ["X2"], ["X3", "Xv"]]
-        XK = XH[0] + XH[1] + XH[2]
-        la = CH[NC - 1]
-        ts(T.W16[:], Wu[:], -2048.0, None, A.add, None, [wk], ["W16"])
-        fgather(0)
+        EK, MK = ["e0", "e1"], ["Mt%d" % h for h in range(NG)]
+        if t: lin("S", W16, Wu[:], 1.0, -2048.0, [wk], [w16])
+        fgather(0); fgather(1)
         extract(0)
-        wthings(0)
-        for c in range(1, NC):
-            fgather(c); names(c - 1)
-            extract(c)
-            if c == 1: wthings(1)
-        if t:
-            for c in (1, 0, 2):
-                sl = slice(CH[c], CH[c + 1])
-                ts(T.tb[:, sl], T[YB[c]][:, sl], -2048.0, 4096.0, A.is_lt, A.mult, [YK[c]], ["tb%d" % c], [YB[c]])
-            for c in (1, 0, 2):
-                sl = slice(CH[c], CH[c + 1])
-                tt(T.e16[:, sl], T[YB[c]][:, sl], T.tb[:, sl], A.add, [YK[c], "tb%d" % c], [EK[c]], [YB[c]])
-        else:
-            filler(99)
-        names(NC - 1)
+        fgather(2); fgather(3)
+        if t: act(T.ri[:, 0:1], T.Gs[:, 0:1], ["Gs"], ["ri"], scale=0.5, bias=-0.25)
+        mm(T.PK[:, 0:256], T.on[:, 0:128], T.Kc[:], True, False, ["on", "Kc0", "Kc1", "Kc2"], ["K"], "PK")
+        extract(1)
+        offsets(0)
+        if not t: filler(lateS, 99)
+        xgather(0); xgather(1)
+        if t: act(T.par[:, 0:1], T.ri[:, 0:1], ["Gs", "ri"], ["par"], scale=-2.0, bias=T.Gs[:, 0:1])
+        else: filler(lastS, 2)
+        offsets(1)
+        if not t: filler(lateV, 99)
+        mm(T.PW[:, 0:256], T.I[:], T.Cw[:], True, False, ["Cw0", "Cw1"], ["WN"], "PW")
+        mm(T.PW[:, 0:128], T.Sh[:], W16, False, False, [w16, "Sh"], ["WN"], "PW")
+        mm(T.PW[:, 128:256], T.Rev[:], W16, False, False, [w16, "Rev"], ["WN"], "PW")
+        for c in range(2, len(XP)): xgather(c)
+        if not t: filler(lastS, 99)
         total(0)
+        xterm(0)
         if t:
-            ts(T.tb[:, la:128], T.PB[:, la:128], -2048.0, 4096.0, A.is_lt, A.mult, YK[-1:], ["tbl"], ["PB"])
-            tt(T.e16[:, la:128], T.PB[:, la:128], T.tb[:, la:128], A.add, YK[-1:] + ["tbl"], EK[-1:], ["PB"])
-        mean(0)
-        total(1)
-        for k in range(LA): larger(0, k)
-        mean(1)
-        for k in range(LA, 8): larger(0, k)
-        mm(T.PD[:, 0:128], T.e16[:], T.Dm[:], False, False, EK + ["Dm"], ["D"], "PD")
-        mm(T.PD[:, 128:256], T.e16[:], T.Dm[:], False, True, EK, ["D"], "PD")
-        mm(T.PT[:, 128:256], T.e16[:], T.I[:], True, True, EK, ["Te"], "PT")
-        mm(T.PT[:, 256:264], T.e16[:], T.I[:, 15::16], True, True, EK, ["Te"], "PT")
-        mm(T.PT[:, 264:272], T.e16[:], T.I[:, 15::16], True, True, EK, ["Te"], "PT")
-        total(2)
-        for k in range(16):
-            mm(T.PK[:, k:128:16], T.X[:, k::16], T.B8N[:], False, False, XK + ["B8N"], ["K"], "PK")
-        for k in range(MP): larger(1, k)
-        act(T.eT[:], T.PT[:, 128:280], ["Te"], ["eT"], ["PT"], bias=2048.0)
-        act(T.nth[:, 0:1], T.par[:, 0:1], ["par"], ["nth"], bias=-3.5, scale=-1.0)
-        act(T.D0[:], T.PD[:, 0:384], ["D"], ["D0"], ["PD"])
-        mean(2)
-        MK = ["Mt%d" % j for j in range(3)]
-        for k in range(MP, 8): larger(1, k)
+            below(0); below(1); name(0); name(1)
+        mm(T.PT[:, 0:128], T.e16[:], T.I[:], True, True, EK, ["Te"], "PT")
+        for h in range(NG):
+            if h + 1 < NG: total(h + 1)
+            if h + 2 == NG:
+                for x in range(1, len(XT)): xterm(x)
+            mean(h)
+            if h == 0:
+                act(T.eT[:], T.PT[:, 0:128], ["Te"], ["eT"], ["PT"], bias=2048.0)
+                if not t: floors()
+            if h + 1 < NG:
+                for k in range(8): larger(h, k)
+        mm(T.PK[:, 0:256], T.Mt[:], T.BN[:], False, False, MK + ["BN0", "BN1"], ["K"], "PK")
+        mm(T.PK[:, 0:128], T.e16[:], T.I[:], False, False, EK, ["K"], "PK")
+        mm(T.PK[:, 128:256], W16, T.I[:], False, False, [w16], ["K"], "PK")
+        mm(T.PT[:, 128:136], T.Mt[:], T.wt[:], True, True, MK + ["wt"], ["Tu"], "PT")
         for k in range(8):
+            larger(NG - 1, k)
             for j in range(2):
-                mm(T.PK[0:96, k + 8 * j:128:16], T.MX[:, 256 * k + j:256 * k + 192:2], T.B8P[:], False, False,
-                   ["MX%d_%d" % (c, k) for c in range(2)] + ["B8P"], ["K"], "PK")
-        for k in range(8):
-            larger(2, k)
-            for j in range(2):
-                mm(T.PK[96:128, k + 8 * j:128:16], T.MX[:, 256 * k + 192 + j:256 * k + 256:2], T.B8P[:], False,
-                   False, ["MX2_%d" % k], ["K"], "PK")
-            if k == 7: mm(T.PK[:, 0:128], T.Mt[:], T.BN[:], False, True, MK + ["BN"], ["K"], "PK")
-            if k == 0:
-                mm(T.PT[:, 288:296], T.Mt[:], T.wt[:], True, True, MK + ["wt"], ["Tu"], "PT")
-                act(T.sq[:], T.PT[:, 288:296], ["Tu"], ["sq"], ["PT"], f=AF.Square, scale=0.25, bias=-12288.0)
-                act(T.t74[:], T.PT[:, 288:296], ["Tu"], ["t74"], ["PT"], bias=-3637248.25, scale=74.0)
-        key = T.PK[:, 0:128]
-        bc = T.bc[:, 0:8]
-        scan(T.R[:, 0:128], T.D0[:, 0:128], key, A.add, A.min, ["K", "D0"], ["R0"], ["PK"])
-        scan(T.R[:, 128:256], T.D0[:, 128:256], key, A.add, A.max, ["K", "D0"], ["R1"], ["PK"])
-        scan(T.R[:, 256:384], T.D0[:, 256:384], key, A.add, A.max, ["K", "D0"], ["R2"], ["PK"])
-        tt(T.Ni[:], T.R[:, 15:128:16], T.eT[:, 128:136], A.add, ["R0", "eT"], ["Ni"])
-        tt(T.yi[:], T.sq[:], T.t74[:], A.add, ["sq", "t74"], ["yi"])
-        tt(T.Ri[:], T.R[:, 143:384:16], T.eT[:, 136:152], A.add, ["R1", "R2", "eT"], ["Ri"])
-        ts(T.NK[:, 0:8], T.Ni[:], 4095, None, A.bitwise_and, None, ["Ni"], ["n"])
-        ts(T.zi[:], T.yi[:], 1, 4095, A.logical_shift_right, A.bitwise_and, ["yi"], ["zi"])
-        ts(T.low[:], T.Ri[:], 4095, None, A.bitwise_and, None, ["Ri"], ["low"])
-        tt(T.eq[:], T.NK[:, 0:8].indirect(bc), T.eT[:, 0:128], A.is_equal, ["n", "bc", "eT"], ["eq"])
-        tt(T.ne[:], T.NK[:, 0:8], T.low[:, 0:8], A.not_equal, ["n", "low"], ["ne"])
-        ts(T.c2[:], T.low[:, 8:16], col(12), None, A.add, None, ["low", "s12"], ["c2"])
-        ts(T.NK[:, 8:16], T.Ri[:, 0:8], 12, 15, A.logical_shift_right, A.bitwise_and, ["Ri"], ["kk"])
+                mm(T.PK[:, k + 8 * j:256:16], T.MX[:, 256 * k + j:256 * k + 256:2], T.BM[:], False, k == 7 and j == 1,
+                   ["MX%d_%d" % (h, k) for h in range(NG)] + ["BM"], ["K"], "PK")
+        act(T.sq[:], T.PT[:, 128:136], ["Tu"], ["sq"], ["PT"], f=AF.Square, scale=0.25, bias=(592.0 - 184 * 256) / 4)
+        act(T.yi[:], T.sq[:], ["sq"], ["yi"], scale=0.5, bias=-10952.40625)
+        mm(T.PD[:, 0:ND], T.m16[:], T.Own[:, 0:ND], True, False, ["m16"] + allr("Own"), ["D"], "PD")
+        mm(T.PA[:, 0:128], T.SoP[:], W16, True, False, ["SoP", w16], ["V1", "Y1", "S2"], "PA")
+        mm(T.PB[:, 0:128], T.SoP[:], W16, True, False, [w16], ["V2", "S0"], "PB")
+        mm(T.PB[:, 0:128], T.I[:], T.c2k[:], False, False, [], ["V2"], "PB")
+        scan(T.R[:, 0:128], T.d0[:], T.PK[:, 0:128], A.add, A.max, ["K", "d0"], ["R0"], ["PK"])
+        scan(T.R[:, 128:256], T.d0[:], T.PK[:, 128:256], A.add, A.max, ["K", "d0"], ["R1"], ["PK"])
+        ts(T.NK[:, 0:8], T.R[:, 15:128:16], 4095, None, A.bitwise_and, None, ["R0"], ["n"])
+        ts(T.NK[:, 16:24], T.yi[:], 4095, None, A.bitwise_and, None, ["yi"], ["z"])
+        ts(T.NK[:, 24:40], T.R[:, 15:256:16], 12, 15, A.logical_shift_right, A.bitwise_and, ["R0", "R1"], ["kk"])
+        ts(T.NK[:, 8:16], T.R[:, 143:256:16], 4095, None, A.bitwise_and, None, ["R1"], ["c"])
+        tt(T.eq[:], T.NK[:, 0:8].indirect(bc), T.eT[:], A.is_equal, ["n", "bc", "eT"], ["eq"])
+        tt(T.ne[:], T.NK[:, 24:32], T.NK[:, 32:40], A.not_equal, ["kk"], ["ne"])
+        ts(T.c2[:], T.NK[:, 8:16], col(12), None, A.add, None, ["c", "s12"], ["c2"])
         scan(T.Sc[:], T.rst[:], T.eq[:], A.mult, A.add, ["rst", "eq"], ["Sc"])
-        act(T.gG[:], T.Sc[:].indirect(T.b2[:]), ["Sc", "b2", "nth"], ["gG"], f=AF.Sign, bias=T.nth[:, 0:1])
-        mm(T.PW[:, 0:128], T.gG[:], T.Ig[:], False, False, ["gG", "Ig"], ["WN"], "PW")
-        mm(T.PW[:, 128:256], T.gG[:], T.Ih[:], False, False, ["gG", "Ih"], ["WN"], "PW")
         tt(T.u2[:], T.c2[:], T.ne[:], A.mult, ["c2", "ne"], ["u2"])
-        cp(T.NKf[:], T.NK[:], ["n", "kk"], ["NKf"])
-        ts(T.go[:, 0:8], T.Sc[:, 15::16], T.par[:, 0:1], 4.0, A.subtract, A.is_ge, ["Sc", "par"], ["go"])
-        ts(T.Nt[:, 0::16], T.NK[:, 0:8], -2048.0, None, A.add, None, ["n"], ["Nt"])
-        ts(T.Zt[:, 0::16], T.zi[:], -2048.0, None, A.add, None, ["zi"], ["Zt"])
+        act(T.Nt[:, 0::16], T.NK[:, 0:8], ["n"], ["Nt"], bias=-2048.0)
+        act(T.Zt[:, 0::16], T.NK[:, 16:24], ["z"], ["Zt"], bias=-2048.0)
+        act(T.gK[:], T.NK[:, 32:40].indirect(bc), ["kk", "bc"], ["gK"])
+        act(T.gN[:], T.NK[:, 0:8].indirect(bc), ["n", "bc"], ["gN"], bias=-2048.0)
         mm(T.PW[:, 0:128], T.Nt[:], T.I[:], False, False, ["Nt"], ["WN"], "PW")
-        mm(T.PW[:, 128:256], T.Zt[:], T.I[:], False, True, ["Zt"], ["WN"], "PW")
-        act(T.gK[:], T.NKf[:, 8:16].indirect(bc), ["NKf", "bc"], ["gK"])
-        act(T.gN[:], T.NKf[:, 0:8].indirect(bc), ["NKf", "bc"], ["gN"])
-        if t < NV - 1:
-            mm(T.PT[:, 304:312], T.on[:], T.go[:, 0:8], True, True, ["on", "go"], ["Tc"], "PT")
-            act(T.jk[:], T.PT[:, 304:312], ["Tc"], ["jk", "Gs"], ["PT"], acc=T.Gs[:, 0:1])
-        mm(T.PB[:, 0:128], T.gK[:], T.I[:], True, True, ["gK"], ["QK"], "PB")
-        act(T.ab[:], T.PB[:, 0:128], ["QK", "s10"], ["ab"], ["PB"], f=AF.Abs, bias=col(10), scale=8192.0)
-        mm(T.PA[:, 128:136], T.I[:], T.cf[:], True, False, ["cf"], ["bS", "S0"], "PA")
-        mm(T.PY[:, 128:136], T.I[:], T.cf[:], True, False, ["cf"], ["bV"] + YK, "PY")
-        tt(T.cw[:], T.go[:, 0:8], T.u2[:], A.mult, ["go", "u2"], ["cw"])
-        tt(T.bM[:], T.cw[:, 0:8].indirect(bc), T.m16[:], A.mult, ["cw", "bc", "m16"], ["bM"])
-        ts(T.bC[:], T.cw[:, 0:8].indirect(bc), col(13), None, A.add, None, ["cw", "bc", "s13"], ["bC"])
+        mm(T.PW[:, 128:256], T.Zt[:], T.I[:], False, False, ["Zt"], ["WN"], "PW")
+        mm(T.PY[:, 0:128], T.gK[:], T.I[:], True, True, ["gK"], ["QK", "Y0", "S1"], "PY")
+        act(T.ab[:], T.PY[:, 0:128], ["QK", "s10"], ["ab"], ["PY"], f=AF.Abs, bias=col(10), scale=8192.0)
+        ts(T.ngo[:], T.Sc[:].indirect(T.b2[:]), T.par[:, 0:1], 4.0, A.subtract, A.is_lt, ["Sc", "b2", "par"], ["ngo"])
+        lin("V", T.cb[:], T.u2[:].indirect(bc), -1.0 / 8192, col(13), ["u2", "bc", "s13"], ["cb"])
+        mm(T.PW[:, 0:128], T.ngo[:], T.Ih[:], False, False, ["ngo", "Ih"], ["WN"], "PW")
+        mm(T.PW[:, 128:256], T.ngo[:], T.Ig[:], False, True, ["ngo", "Ig"], ["WN"], "PW")
+        mm(T.PD[:, 0:ND], T.ngo[:], T.Sel[:, 0:ND], False, False, ["ngo"] + allr("Sel"), ["D"], "PD")
+        tt(T.cM[:], T.cb[:], T.m16[:], A.mult, ["cb", "m16"], ["cM"])
+        mm(T.PD[:, 0:ND], T.cb[:], T.Sel[:, 0:ND], False, False, ["cb"], ["D"], "PD")
+        mm(T.PD[:, 0:ND], T.cM[:], T.Blk[:, 0:ND], False, True, ["cM"] + allr("Blk"), ["D"], "PD")
+        mm(T.PT[:, 144:152], T.cM[:], T.B8[:], True, True, ["cM", "B8"], ["Tb"], "PT")
+        mm(T.PA[:, 0:128], T.gN[:], T.I[:], False, True, ["gN"], ["V1"], "PA")
+        mm(T.PB[:, 0:128], T.gN[:], T.I[:], False, False, ["gN"], ["V2"], "PB")
+        act(T.sg[:], T.PA[:, 0:128], ["V1"], ["sg"], ["PA"], f=AF.Sign, bias=0.5)
+        if t < NV - 1: mm(T.PK[:, 384:392], T.on[:, 0:128], T.ngo[:, 0::16], True, True, ["on", "ngo"], ["Tc"], "PK")
         if t < NV - 1:
             ws = T["Ws%d" % (t + 1)]
-            ts(ws[:], T.PW[:, 0:256], -2048.0, None, A.add, None, ["WN"], ["Ws%d" % t], ["PW"])
-            op("G", lambda ws=ws, t=t: g.remote_dma_fused([RemoteDMATransfer(
-                dst_ids=[DstId(rid=rid, pnc=pid)], dma_engine_mask=mask_out, remote_sem=T.sem["arr%d" % (t + 1)],
-                srcs=[ws[:, 0:128], ws[:, 128:256]], dsts=[T["Wu%d" % (t + 1)][:]], alu_op=2)], local_sem=T.sem.sent),
-               ["Ws%d" % t], [], kind="send", val=len(eng_out))
-        mm(T.PA[:, 128:136], T.bM[:], T.B8f[:], False, True, ["bM", "B8f"], ["bS"], "PA")
-        mm(T.PY[:, 128:136], T.bM[:], T.B8f[:], False, True, ["bM"], ["bV"], "PY")
-        mm(T.PY[:, 0:128], T.bC[:], T.J[:], True, True, ["bC", "J"], YK, "PY")
-        mm(T.PA[:, 0:128], T.bC[:], T.J[:], True, True, ["bC"], ["cS", "S0"], "PA")
-        mm(T.PD[:, 0:128], T.gN[:], T.If[:], True, False, ["gN"], ["D"], "PD")
-        mm(T.PD[:, 0:128], T.SoP[:], T.W16[:], False, True, ["SoP", "W16"], ["D"], "PD")
-        mm(T.PK[:, 0:128], T.gN[:], T.If[:], True, False, ["gN"], ["K"], "PK")
-        mm(T.PK[:, 0:128], T.SoP[:], T.W16[:], False, False, ["SoP", "W16"], ["K"], "PK")
-        act(T.nB[:], T.PA[:, 128:136], ["bS"], ["nB"], ["PA"], scale=-8192.0)
-        for h in range(7, -1, -1):
-            st, ln = 8 * h * (h + 1), 16 * h + 16
-            if h >= HV:
-                ts(T.E[:, st:st + ln], T.PY[:, 128 - ln:128], T.PY[:, 128 + h:129 + h], 8192.0, A.not_equal, A.mult,
-                   ["Y0", "bV"], ["E%d" % h], ["PY"])
-            else:
-                act(T.E[:, st:st + ln], T.PA[:, 128 - ln:128], ["cS", "nB"], ["E%d" % h], ["PA"], f=AF.Abs,
-                    bias=T.nB[:, h:h + 1], scale=8192.0)
-        act(T.cB[:, 0:8], T.PA[:, 128:136], ["bS"], ["cB"], ["PA"], bias=2048.0 + PAD)
-        act(T.sg[:], T.PD[:, 0:128], ["D"], ["sg"], ["PD"], f=AF.Sign, bias=-2047.5)
-        mm(T.PK[:, 0:128], T.IN[:], T.ab[:], False, False, ["IN", "ab"], ["K"], "PK")
-        mm(T.PK[:, 0:128], T.Iod[:], T.sg[:], False, True, ["Iod", "sg"], ["K"], "PK")
-        if t == NV - 1:
-            act(T.tT[:], T.PW[:, 0:256], ["WN"], ["tT"], ["PW"], f=AF.Relu, bias=-2048.0)
-            mm(T.PT[:, 0:128], T.If[:], T.tT[:, 0:128], True, False, ["tT"], ["Tw"], "PT")
-            mm(T.PT[:, 0:128], T.If[:], T.tT[:, 128:256], False, True, ["tT"], ["Tw"], "PT")
-            act(T.wo[:], T.PT[:, 0:128], ["Tw"], ["wo"], ["PT"])
+            lin("V", ws[:], T.PW[:, 0:256], 1.0, 2048.0, ["WN"], ["Ws%d" % t], ["PW"])
+            def send(more, ws=ws, t=t):
+                op("G", lambda: g.remote_dma_fused([RemoteDMATransfer(
+                    dst_ids=[DstId(rid=rid, pnc=pid)], dma_engine_mask=mask_out, remote_sem=T.sem["arr%d" % (t + 1)],
+                    srcs=[ws[:, 0:128], ws[:, 128:256]], dsts=[T["Wu%d" % (t + 1)][:]], alu_op=2)],
+                    local_sem=T.sem.sent), ["Ws%d" % t] + more, [], kind="send", val=len(eng_out))
+            send([])
+        mm(T.PB[:, 0:128], T.IN[:], T.ab[:], False, False, ["IN", "ab"], ["V2"], "PB")
+        mm(T.PB[:, 0:128], T.Iod[:], T.sg[:], False, True, ["Iod", "sg"], ["V2"], "PB")
+        ts(T.E[:, 0:ND], T.PD[:, 0:ND], 0.0, 8192.0, A.not_equal, A.mult, ["D"], ["E"], ["PD"])
+        lin("V", T.o0[:, 0:8], T.PT[:, 144:152], 8192.0, 2048.0 + PAD, ["Tb"], ["o0"], ["PT"])
+        scan(T.Rd[:, 0:ND], T.E[:, 0:ND], T.dm[:, 0:ND], A.min, A.max, ["E"] + allr("dm"), ["Rd"])
+        tt(T.om[:], T.U[:].indirect(T.o0[:, 0:8]), T.ab[:], A.min, UK + ["o0", "ab"], ["om"])
+        tt(T.o1[:], T.Rd[:, 0:ND].indirect(T.en[:, 0:1]), T.o0[:], A.min, ["Rd", "en", "o0"], ["o1", "dl%d" % t])
+        if t < NV - 1:
+            act(T.jk[:], T.PK[:, 384:392], ["Tc"], ["jk", "Gs"], ["PK"], acc=T.Gs[:, 0:1])
+        else:
+            act(T.tT[:], T.PW[:, 0:256], ["WN"], ["tT"], ["PW"], f=AF.Relu, bias=2048.0)
+            mm(T.PT[:, 0:128], T.If[:], T.tT[:, 0:128], True, False, ["tT", "If"], ["Te"], "PT")
+            mm(T.PT[:, 0:128], T.If[:], T.tT[:, 128:256], False, True, ["tT"], ["Te"], "PT")
+            act(T.wo[:], T.PT[:, 0:128], ["Te"], ["wo"], ["PT"])
             dma("Y", T.yw[:], T.wo[:], ["wo"], [])
-        ts(T.o0[:], T.PY[:, 128:136], 2048.0 + PAD, None, A.add, None, ["bV"], ["o0"], ["PY"])
-        scan(T.Rd[:], T.E[:], T.dm[:], A.min, A.max, ["E%d" % h for h in range(8)] + ["dm%d" % h for h in range(8)], ["Rd"])
-        tt(T.om[:], T.U[:].indirect(T.o0[:]), T.ab[:], A.min, UK + ["o0", "ab"], ["om"])
-        tt(T.rr[:], T.Rd[:].indirect(T.en[:, 0:1]), T.cB[:], A.min, ["Rd", "en", "cB"], ["rr"])
-        if t < NV - 1: ts(T.ri[:, 0:1], T.Gs[:, 0:1], 0.5, -0.25, A.mult, A.add, ["Gs"], ["ri"])
-        tt(T.nw[:], T.om[:], T.PK[:, 0:128], A.max, ["om", "K"], ["nw"], ["PK"])
-        cp(T.o1[:], T.rr[:, 0:8], ["rr"], ["o1"])
-        if t < NV - 1: ts(T.par[:, 0:1], T.ri[:, 0:1], -2.0, T.Gs[:, 0:1], A.mult, A.add, ["Gs", "ri"], ["par"])
-        cp(T.U[:].indirect(T.o1[:]), T.nw[:], ["o1", "nw"], UK)
 
-    cuts = [0, 256, 768, 1280, 1664, 1920, 2048]
-    def high(c):
-        a, b = cuts[c], cuts[c + 1]
-        ts(T[HB[c]][:, 0:b - a], T.U[:, HI + a:HI + b], 4096.0, None, A.mult, None, UK, ["H%d" % c], [HB[c]])
+        def column(a):
+            sl = slice(16 * NB * a, 16 * NB * (a + 1))
+            tt(T.nw[:, sl], T.om[:, sl], T.PB[:, sl], A.max, ["om", "V2"], ["nw%d" % a], ["PB"])
+        column(NS - 1)
+        for a in range(NS - 1, -1, -1):
+            if a: column(a - 1)
+            cp(T.U[:].indirect(T.o1[:, NB * a:NB * (a + 1)]), T.nw[:, 16 * NB * a:16 * NB * (a + 1)],
+               ["o1", "nw%d" % a], UK)
+
     HB = ["PM", "PY", "PA", "PB", "PD", "PK"]
-    high(0)
-    for c in range(len(cuts) - 1):
-        a, b = cuts[c], cuts[c + 1]
-        if c + 2 < len(cuts): high(c + 1)
+    for c in range(len(CUTS) - 1):
+        a, b = CUTS[c], CUTS[c + 1]
+        act(T[HB[c]][:, 0:b - a], T.U[:, HI + a:HI + b], UK, ["H%d" % c], [HB[c]], scale=4096.0)
         tt(T.fo[:, a:b], T.U[:, LO + a:LO + b], T[HB[c]][:, 0:b - a], A.add, UK + ["H%d" % c], ["fo%d" % c], [HB[c]])
-        dma("Y" if c % 2 == 0 else "S", T.yf[:, a:b], T.fo[:, a:b], ["fo%d" % c], [])
+        dma("Y", T.yf[:, a:b], T.fo[:, a:b], ["fo%d" % c], [])
     emit(g, T, ops)

from concourse.bass import DstId, RemoteDMATransfer
from concourse.mybir import AluOpType as A, ActivationFunctionType as AF, AxisListType as AX

F32, BF, FH, I32, U16 = "float32", "bfloat16", "float16", "int32", "uint16"
NV = 4
FP = [("V", 0, 32), ("S", 32, 64), ("V", 64, 96), ("S", 96, 128)]
XP = [("V", 0, 32), ("S", 32, 64), ("V", 64, 84), ("S", 84, 128)]
TG = [(0, 64), (64, 128)]
XT = [(0, 64), (64, 128)]
NB = 4
PAD = 256
NDM = 328
FC = [0, 256, 640, 1152, 1664, 2048]
FS = [0, 128, 256, 320, 384]
CUTS = [0, 256, 768, 1280, 1664, 1920, 2048]
SCRATCH = {
    "fs": ("sbuf", [128, 2048], I32), "U": ("sbuf", [128, PAD + 4096], I32), "fo": ("sbuf", [128, 2048], F32),
    "th": ("sbuf", [128, 2048], I32),
    "r2": ("sbuf", [128, 8192], BF), "wi": ("sbuf", [128, 128], I32), "wo": ("sbuf", [128, 128], F32),
    "G": ("sbuf", [128, 2048], FH), "X": ("sbuf", [128, 2048], BF), "MX": ("sbuf", [128, 2048], BF),
    "W16": ("sbuf", [128, 256], FH), "e16": ("sbuf", [128, 128], FH), "off": ("sbuf", [128, 128], U16),
    "tb": ("sbuf", [128, 128], F32), "Mt": ("sbuf", [128, 128], BF), "eT": ("sbuf", [128, 128], F32),
    "R": ("sbuf", [128, 256], I32), "NK": ("sbuf", [128, 40], I32), "eq": ("sbuf", [128, 128], BF),
    "Sc": ("sbuf", [128, 128], BF), "ngo": ("sbuf", [128, 128], BF), "ne": ("sbuf", [128, 8], F32),
    "c2": ("sbuf", [128, 8], F32), "u2": ("sbuf", [128, 8], F32), "cb": ("sbuf", [128, 128], FH),
    "cM": ("sbuf", [128, 128], FH), "E": ("sbuf", [128, NDM], BF), "Rd": ("sbuf", [128, NDM], BF),
    "o0": ("sbuf", [128, 16], U16), "o1": ("sbuf", [128, 16], U16),
    "gK": ("sbuf", [128, 128], BF), "gN": ("sbuf", [128, 128], FH), "ab": ("sbuf", [128, 128], BF),
    "sg": ("sbuf", [128, 128], BF), "om": ("sbuf", [128, 128], F32), "nw": ("sbuf", [128, 128], I32),
    "Nt": ("sbuf", [128, 128], FH), "Zt": ("sbuf", [128, 128], FH), "sq": ("sbuf", [128, 8], F32),
    "yi": ("sbuf", [128, 8], I32),
    "tT": ("sbuf", [128, 256], F32), "jk": ("sbuf", [128, 8], F32), "Gs": ("sbuf", [128, 8], F32),
    "ri": ("sbuf", [128, 8], I32), "par": ("sbuf", [128, 8], F32),
    "pi": ("sbuf", [128, 8], I32), "sc": ("sbuf", [128, 32], F32), "Cm": ("sbuf", [128, 130], BF),
    "Ck": ("sbuf", [128, 128], BF), "Cg": ("sbuf", [128, 128], BF), "I": ("sbuf", [128, 128], BF),
    "If": ("sbuf", [128, 128], F32), "Dk": ("sbuf", [128, 2048], BF), "km": ("sbuf", [128, 16], F32),
    "SoN": ("sbuf", [128, 128], BF), "SoP": ("sbuf", [128, 128], BF), "Sh": ("sbuf", [128, 128], BF),
    "Rev": ("sbuf", [128, 128], BF), "BN": ("sbuf", [128, 256], BF),
    "m16": ("sbuf", [128, 128], BF), "rst": ("sbuf", [128, 128], BF), "d0": ("sbuf", [128, 128], BF),
    "B8": ("sbuf", [128, 8], BF), "BX": ("sbuf", [128, 16], BF), "BM": ("sbuf", [128, 16], BF),
    "wt": ("sbuf", [128, 8], BF), "Kc": ("sbuf", [128, 256], BF),
    "I16": ("sbuf", [128, 128], BF), "IN": ("sbuf", [128, 128], BF), "Iod": ("sbuf", [128, 128], BF),
    "Ig": ("sbuf", [128, 128], BF), "Ih": ("sbuf", [128, 128], BF), "Cw": ("sbuf", [128, 256], BF),
    "cm": ("sbuf", [128, 64], BF), "c2k": ("sbuf", [128, 128], BF), "on": ("sbuf", [128, 136], BF),
    "Sel": ("sbuf", [128, NDM], BF), "Blk": ("sbuf", [128, NDM], BF), "Own": ("sbuf", [128, NDM], BF),
    "dm": ("sbuf", [128, NDM], BF), "Up": ("sbuf", [128, NDM], BF),
    "bc": ("sbuf", [128, 8], U16), "b2": ("sbuf", [128, 8], U16), "en": ("sbuf", [128, 2], U16),
    "ends": ("sbuf", [128, 8], F32), "pick": ("sbuf", [128, 8], F32),
}
for _t in range(NV):
    SCRATCH["Wu%d" % _t] = ("sbuf", [128, 128], U16)
for _t in range(1, NV):
    SCRATCH["Ws%d" % _t] = ("sbuf", [128, 256], U16)
for _b in ("PY", "PA", "PB", "PM", "PK", "PD", "PT", "PW"):
    SCRATCH[_b] = ("psum", [128, 512], F32)
NDMA = 20
SEMAPHORES = ["sV", "sS", "sP", "sG", "sent", "arr1", "arr2", "arr3"] + ["d%d" % i for i in range(NDMA)]
MAGIC = 12582912.0
BIG = 67108864.0


def emit(g, T, ops):
    q = {"V": g.vector, "S": g.scalar, "P": g.tensor, "G": g, "Y": g.sync}
    wr, rd, bank = {}, {}, {}
    pos = {e: 0 for e in "VSPG"}
    known = {e: ({x: 0 for x in "VSPG"}, set()) for e in q}
    last = {}
    for i, o in enumerate(ops):
        e = o["e"]
        deps = set()
        for k in o["r"]:
            if k in wr: deps.add(wr[k])
        for k in o["w"]:
            if k in wr: deps.add(wr[k])
            deps.update(rd.get(k, ()))
        for b in o["b"]:
            for x, j in bank.setdefault(b, {}).items():
                if x != e: deps.add(j)
        o["waits"] = []
        if o["kind"] != "arrive":
            kc, kd = known[e]
            for j in sorted(deps, reverse=True):
                p = ops[j]
                if p["kind"] == "op":
                    if p["e"] == "P" and e == "P": continue
                    if kc[p["e"]] >= p["pos"]: continue
                    kc[p["e"]] = p["pos"]
                    p["sig"] = True
                else:
                    if j in kd: continue
                    kd.add(j)
                o["waits"].append(j)
                if p["kind"] != "arrive":
                    for x in "VSPG": kc[x] = max(kc[x], p["kc"][x])
                    kd.update(p["kd"])
            o["kc"], o["kd"] = dict(kc), set(kd)
        if o["kind"] == "op":
            pos[e] += 1
            o["pos"] = pos[e]
            last[e] = o
        for k in o["r"]: rd.setdefault(k, []).append(i)
        for k in o["w"]:
            wr[k] = i
            rd[k] = []
        for b in o["b"]: bank[b][e] = i
    for o in last.values(): o["sig"] = True
    cnt = {e: 0 for e in "VSPG"}
    nd, sent = 0, 0
    for o in ops:
        if o["kind"] == "op" and o.get("sig"):
            cnt[o["e"]] += 1
            o["sem"], o["val"] = T.sem["s" + o["e"]], cnt[o["e"]]
        elif o["kind"] == "dma":
            o["sem"], o["val"] = T.sem["d%d" % nd], 16
            nd += 1
    for o in ops:
        if o["kind"] == "arrive": continue
        for j in o["waits"]:
            q[o["e"]].wait_ge(ops[j]["sem"], ops[j]["val"])
        ins = o["f"]()
        if o["kind"] == "send": sent += o["val"]
        elif o["kind"] == "dma": ins.then_inc(o["sem"], 16)
        elif o.get("sig"): ins.then_inc(o["sem"], 1)
    for e in "VSPG":
        g.wait_ge(T.sem["s" + e], cnt[e])
    if sent: g.wait_ge(T.sem.sent, sent)
    for o in ops:
        if o["kind"] == "dma": g.wait_ge(o["sem"], 16)


def rank_program(g, core, T, topo):
    rank = T.rank_of(core)
    if rank is None:
        return
    n = len(T.cores)
    nxt, prv = T.cores[(rank + 1) % n], T.cores[(rank - 1) % n]
    eng_out = topo.engines(core, nxt)
    n_in = len(topo.engines(prv, core))
    mask_out = sum(1 << x for x in eng_out)
    rid, pid = topo.addr(nxt)[0], topo.addr(nxt)[1]
    v, s, pe = g.vector, g.scalar, g.tensor
    ops = []

    def op(e, f, r, w, b=(), kind="op", **kw):
        d = {"e": e, "f": f, "r": list(r), "w": list(w), "b": list(b), "kind": kind}
        d.update(kw)
        ops.append(d)

    def ts(out, in0, s1, s2, o0, o1, r, w, b=()):
        if s2 is None: op("V", lambda: v.tensor_scalar(out, in0, s1, None, o0), r, w, b)
        else: op("V", lambda: v.tensor_scalar(out, in0, s1, s2, o0, o1), r, w, b)

    def tt(out, a, c, o, r, w, b=()):
        op("V", lambda: v.tensor_tensor(out, a, c, o), r, w, b)

    def cp(out, a, r, w, b=()):
        op("V", lambda: v.tensor_copy(out, a), r, w, b)

    def scan(out, d0, d1, o0, o1, r, w, b=()):
        op("V", lambda: v.tensor_tensor_scan(out, d0, d1, 0.0, o0, o1), r, w, b)

    def ms(out, c, w):
        op("V", lambda: v.memset(out, c), [], w)

    def act(out, a, r, w, b=(), f=AF.Identity, bias=0.0, scale=1.0, acc=None):
        if acc is None: op("S", lambda: s.activation(out, a, f, bias=bias, scale=scale), r, w, b)
        else: op("S", lambda: s.activation(out, a, f, bias=bias, scale=scale, accum_out=acc), r, w, b)

    def lin(e, out, a, scale, bias, r, w, b=()):
        if e == "S": act(out, a, r, w, b, bias=bias, scale=scale)
        elif scale == 1.0: ts(out, a, bias, None, A.add, None, r, w, b)
        else: ts(out, a, scale, bias, A.mult, A.add, r, w, b)

    def mm(out, l, rh, st, sp, r, w, b):
        op("P", lambda: pe.matmul(out, l, rh, st, sp), r, w, [b])

    def dma(e, out, a, r, w):
        qq = g.sync if e == "Y" else g.scalar
        op(e, lambda: qq.dma_start(out, a), r, w, kind="dma")

    def iota(out, pat, base, w):
        op("G", lambda: g.iota(out, pat, base, 0, allow_small_or_imprecise_dtypes=True), [], w)

    def select(out, a, pat, cmp, base, mul, r, w):
        op("G", lambda: g.affine_select(out, a, pat, cmp, 0.0, base, mul), r, w)

    def col(i):
        return T.sc[:, i:i + 1]

    NP = len(FC) - 1
    UK = ["U%d" % i for i in range(3 * NP)] + ["Ud"]
    LO, HI = PAD, PAD + 2048
    NS = 8 // NB
    RL = [16 * r + 17 for r in range(NB)]
    RS = [NS * sum(RL[:r]) for r in range(NB + 1)]
    ND = RS[NB]

    dma("S", T.wi[:], T.wnd[:], [], ["wi"])
    for c in range(NP):
        dma("Y", T.fs[:, FC[c]:FC[c + 1]], T.fld[:, FC[c]:FC[c + 1]], [], ["fs%d" % c])
    dma("Y", T.r2[:, 0:4096], T.rec[:, :], [], ["ra"])
    dma("Y", T.r2[:, 4096:8192], T.rec[:, :], ["ra"], ["rb"])

    op("G", lambda: g.iota(T.pi[:, 0:1], [[0, 1]], 0, 1), [], ["pi0"])
    iota(T.Cm[:], [[1, 130]], -2, ["Cm"])
    iota(T.Ck[:], [[0, 8], [1, 16]], 0, ["Ck"])
    iota(T.Cg[:], [[1, 8], [0, 16]], 0, ["Cg"])
    for r in range(NB):
        iota(T.ends[:, r::NB], [[RL[r], NS]], RS[r] + RL[r] - 1, ["ends%d" % r])
    Cm, C1 = T.Cm[:, 2:130], T.Cm[:, 1:129]
    ms(T.on[:], 1.0, ["on"]); ms(T.cm[:], -15.0 / 32, ["cm"]); ms(T.c2k[:], 2048.0, ["c2k"])
    ms(T.d0[:], 4096.0, ["d0"]); ms(T.U[:, 0:PAD], 0, ["Ud"])
    for i, m in enumerate((15, 1, 16 * NB - 1)):
        ts(T.pi[:, 1 + i:2 + i], T.pi[:, 0:1], m, None, A.bitwise_and, None, ["pi0"], ["pi%d" % (1 + i)])
    ts(T.pi[:, 4:5], T.pi[:, 0:1], 4, None, A.logical_shift_right, None, ["pi0"], ["pi4"])
    ms(T.d0[:, 0:128:16], -BIG, ["d0"]); ms(T.par[:], 0.0, ["par"])
    cp(T.sc[:, 0:5], T.pi[:, 0:5], ["pi0", "pi1", "pi2", "pi3", "pi4"], ["s0"])
    P_, K_, O_, Q_, G_ = 0, 1, 2, 3, 4
    ms(T.Kc[0:64, 0:128], -(16.0 * 192 - 16) * 1024, ["Kc0"])
    ms(T.Kc[0:64, 128:256], (16.0 * 192 - 16) * 1024, ["Kc1"])
    ts(T.I[:], Cm, col(P_), None, A.is_equal, None, ["Cm", "s0"], ["I"])
    ts(T.km[:], T.Cm[:, 2:18], col(K_), None, A.is_equal, None, ["Cm", "s0"], ["km"])
    ts(col(6), col(O_), -1.0, None, A.add, None, ["s0"], ["s6"])
    ts(T.B8[:], T.Cm[:, 2:10], col(G_), None, A.is_equal, None, ["Cm", "s0"], ["B8"])
    for k in range(16):
        if k % 2: act(T.Dk[:, 128 * k:128 * k + 128], T.I[:], ["I", "km"], ["Dk%d" % k], scale=T.km[:, k:k + 1])
        else: ts(T.Dk[:, 128 * k:128 * k + 128], T.I[:], T.km[:, k:k + 1], None, A.mult, None, ["I", "km"], ["Dk%d" % k])
    ts(T.SoN[:], C1, col(P_), col(6), A.is_equal, A.mult, ["Cm", "s0", "s6"], ["SoN"])
    cp(T.bc[:], T.Cm[:, 2:10], ["Cm"], ["bc"])
    ms(T.Kc[64:128, :], 32.0, ["Kc2"])
    ms(T.Cw[:, 0:128], 0.0, ["Cw0"]); ms(T.Cw[:, 128:256], -8192.0, ["Cw1"])
    cp(T.Wu0[:], T.wi[:], ["wi"], ["Wu0"])
    for r in range(NB):
        a, b, ln = RS[r], RS[r + 1], RL[r]
        on = T.on[:, 0:b - a]
        top = [[16 * NB, NS], [-1, ln]]
        own = [[16 * NB, NS], [0, ln]]
        select(T.Up[:, a:b], on, [[-16 * NB, NS], [0, ln]], A.is_ge, -16 * r, 1, ["on"], ["Up%d" % r])
        select(T.Sel[:, a:b], on, top, A.is_equal, 16 * r + 16, -1, ["on"], ["Sel%d" % r])
        select(T.Blk[:, a:b], T.Up[:, a:b], own, A.is_ge, 16 * r + 15, -1, ["Up%d" % r], ["Blk%d" % r])
        select(T.Own[:, a:b], T.Blk[:, a:b], top, A.is_equal, 16 * r + 16, -1, ["Blk%d" % r], ["Own%d" % r])
        select(T.Up[:, a:b], T.Blk[:, a:b], top, A.is_gt, 16 * r + 16, -1, ["Blk%d" % r], ["Up%d" % r])

    def allr(name):
        return [name + str(r) for r in range(NB)]

    def cols(*ids):
        how = {7: (P_, 1.0, 15.0), 9: (K_, -1.0, 15.0), 10: (K_, 8192.0, -15.0 * 8192), 11: (O_, -2048.0, 0.0),
               12: (Q_, -2.0, PAD - 128.0), 13: (Q_, -2.0 / 8192, (PAD + 2048.0 - 128) / 8192), 14: (K_, 2.0, 1.0)}
        return [lambda i=i: act(col(i), col(how[i][0]), ["s0"], ["s%d" % i], bias=how[i][2], scale=how[i][1])
                for i in ids]
    lateS = cols(7, 9) + [
        lambda: act(T.I16[:], T.I[:], ["I"], ["I16"], scale=1.0 / 16),
        lambda: act(col(8), col(K_), ["s0", "s7"], ["s8"], bias=col(7), scale=-2.0),
        lambda: act(col(16), col(9), ["s9"], ["s16"], f=AF.Sign),
        lambda: act(T.BX[:, 0:8], T.B8[:], ["B8"], ["BX0"], scale=65536.0),
        lambda: act(T.BX[:, 8:16], T.B8[:], ["B8"], ["BX1"], scale=-65536.0),
    ] + cols(14, 11, 10, 12, 13) + [
        lambda: act(T.BM[:], T.BX[:], ["BX0", "BX1"], ["BM"], scale=-2.0),
        lambda: act(T.wt[:], T.B8[:], ["B8", "s14"], ["wt"], scale=col(14)),
    ]
    lastS = [
        lambda: act(T.IN[:], T.I[:], ["I"], ["IN"], scale=-1.0),
        lambda: act(T.Ig[:], T.I[:], ["I"], ["Ig"], scale=8192.0),
        lambda: act(T.Ih[:], T.I[:], ["I"], ["Ih"], scale=-8192.0),
        lambda: act(T.Iod[:], T.I[:], ["I", "s11"], ["Iod"], scale=col(11)),
        lambda: act(T.SoP[:], T.SoN[:], ["SoN"], ["SoP"], scale=-1.0),
        lambda: act(T.If[:], T.I[:], ["I"], ["If"]),
    ]
    lateV = [
        lambda: ts(T.BN[:, 0:128], T.Cg[:], col(G_), 65536.0, A.is_equal, A.mult, ["Cg", "s0"], ["BN0"]),
        lambda: ts(T.BN[:, 128:256], T.Cg[:], col(G_), -65536.0, A.is_equal, A.mult, ["Cg", "s0"], ["BN1"]),
        lambda: ts(T.m16[:], T.Ck[:], col(K_), -1.0, A.is_equal, A.mult, ["Ck", "s0"], ["m16"]),
        lambda: ts(T.rst[:], T.Ck[:], 0.0, None, A.not_equal, None, ["Ck"], ["rst"]),
        lambda: ts(T.b2[:], T.Cm[:, 2:10], 16.0, 15.0, A.mult, A.add, ["Cm"], ["b2"]),
        lambda: tt(T.pick[:], T.km[:, 0:8], T.ends[:], A.mult, ["km"] + allr("ends"), ["pick"]),
        lambda: ms(T.Zt[:], 0.0, ["Zt"]),
        lambda: ts(T.sc[:, 20:20 + NB], T.Cm[:, 2:2 + NB], 16.0, col(K_), A.mult, A.add, ["Cm", "s0"], ["s20"]),
        lambda: op("V", lambda: v.tensor_reduce(col(19), T.pick[:], AX.X, A.add), ["pick"], ["s19"]),
        lambda: ms(T.Nt[:], 0.0, ["Nt"]),
        lambda: ms(T.o0[:], 0, ["o0"]),
        lambda: cp(T.en[:, 0:1], col(19), ["s19"], ["en"]),
        lambda: ts(T.Sh[:], C1, col(P_), col(16), A.is_equal, A.mult, ["Cm", "s0", "s16"], ["Sh"]),
        lambda: ts(T.Rev[:], Cm, col(8), col(16), A.is_equal, A.mult, ["Cm", "s8", "s16"], ["Rev"]),
    ]

    def filler(late, cnt):
        for _ in range(min(cnt, len(late))): late.pop(0)()

    def floors():
        mm(T.PD[:, 0:ND], T.m16[:], T.Up[:, 0:ND], True, True, ["m16"] + allr("Up"), ["D"], "PD")
        for r in range(NB):
            act(T.dm[:, RS[r]:RS[r + 1]], T.PD[:, RS[r]:RS[r + 1]], ["D", "s20"], ["dm%d" % r], ["PD"],
                bias=col(20 + r), scale=-8192.0)

    def upper(c):
        m, b = FC[c] + FS[c], FC[c + 1]
        if m < b: act(T.U[:, HI + m:HI + b], T.th[:, m:b], ["th%d" % c], ["U%d" % (3 * c + 2)], bias=2047.0)

    lin("S", T.W16[:, 0:128], T.Wu0[:], 1.0, -2048.0, ["Wu0"], ["W16_0"])
    for c in range(NP):
        a, b = FC[c], FC[c + 1]
        m = min(a + FS[c], b)
        k = ["fs%d" % c]
        ts(T.U[:, LO + a:LO + b], T.fs[:, a:b], 4095, None, A.bitwise_and, None, k, ["U%d" % (3 * c)])
        if m > a: ts(T.U[:, HI + a:HI + m], T.fs[:, a:m], 12, None, A.logical_shift_right, None, k, ["U%d" % (3 * c + 1)])
        if m < b:
            act(T.th[:, m:b], T.fs[:, m:b], k, ["th%d" % c], bias=-2047.5 + 2.0 ** -13, scale=2.0 ** -12)
        if c: upper(c - 1)
        else: filler(lateS, 2)
        if c < 2: filler(lateV, 2)
    filler(lateS, 3)
    upper(NP - 1)

    HV = [(0, 64), (64, 128)]
    YB, SB = ["PY", "PA"], ["PB", "PY", "PA"]
    NG = len(TG)
    bc = T.bc[:, 0:8]
    for t in range(NV):
        Wu, wk = T["Wu%d" % t], "Wu%d" % t
        W16, w16 = T.W16[:, 128 * (t % 2):128 * (t % 2) + 128], "W16_%d" % (t % 2)
        if t:
            op("V", None, [], [wk], kind="arrive", sem=T.sem["arr%d" % t], val=n_in)

        def parts(P, ab, name):
            return [name + str(i) for i, p in enumerate(P) if p[-2] < ab[1] and ab[0] < p[-1]]

        def fgather(c):
            e, a, b = FP[c]
            lin(e, T.G[:, 16 * a:16 * b], T.U[:, LO:LO + 4096].indirect(Wu[:, a:b]), 1.0, -2048.0, UK + [wk], ["G%d" % c])

        def xgather(c):
            e, a, b = XP[c]
            win, rk = (T.r2[:, 0:8192], ["ra", "rb"]) if t else (T.r2[:, 0:4096], ["ra"])
            lin(e, T.X[:, 16 * a:16 * b], win.indirect(T.off[:, a:b]), 1.0, -8.0, rk + parts(HV, (a, b), "off"), ["X%d" % c])

        def extract(h):
            a, b = HV[h]
            y, yb, yk = T[YB[h]][:, 0:64], YB[h], ["Y%d" % h]
            mm(y, T.SoN[:], T.c2k[:, 0:64], True, False, ["SoN", "c2k"], yk, yb)
            mm(y, T.SoN[:], T.W16[:, 128 * (t % 2) + a:128 * (t % 2) + b], False, False, [w16], yk, yb)
            for k in range(16):
                mm(y, T.Dk[:, 128 * k:128 * k + 128], T.G[:, 16 * a + k:16 * b:16], False, k == 15,
                   ["Dk%d" % k] + parts(FP, HV[h], "G"), yk, yb)

        def below(h):
            a, b = HV[h]
            ts(T.tb[:, a:b], T[YB[h]][:, 0:64], -2048.0, 4096.0, A.is_lt, A.mult, ["Y%d" % h], ["tb%d" % h], [YB[h]])

        def name(h):
            a, b = HV[h]
            tt(T.e16[:, a:b], T[YB[h]][:, 0:64], T.tb[:, a:b], A.add, ["Y%d" % h, "tb%d" % h], ["e%d" % h], [YB[h]])

        def offsets(h):
            a, b = HV[h]
            if t:
                lin("V", T.off[:, a:b], T[YB[h]][:, 0:64], 1.0, 6144.0, ["Y%d" % h], ["off%d" % h], [YB[h]])
            else:
                below(h); filler(lateV, 2); name(h); filler(lateV, 2)
                lin("V", T.off[:, a:b], T.e16[:, a:b], 1.0, 2048.0, ["e%d" % h], ["off%d" % h])

        def total(h):
            a, b = TG[h]
            ps = T[SB[h]][:, 320:320 + b - a]
            mm(ps, T.I[:], T.cm[:, 0:b - a], True, False, ["cm"], ["S%d" % h], SB[h])
            for k in range(16):
                mm(ps, T.I16[:], T.X[:, 16 * a + k:16 * b:16], False, k == 15, ["I16"] + parts(XP, TG[h], "X"),
                   ["S%d" % h], SB[h])

        def xterm(h):
            a, b = XT[h]
            for k in range(16):
                mm(T.PK[a:b, k:256:16], T.X[:, 16 * a + k:16 * b:16], T.BX[:], False, False,
                   parts(XP, XT[h], "X") + ["BX0", "BX1"], ["K"], "PK")

        def mean(h):
            a, b = TG[h]
            ps = T[SB[h]][:, 320:320 + b - a]
            for j in range(2):
                ts(T.PM[:, 2 * a + j:2 * b:2], ps, MAGIC, -MAGIC, A.add, A.add, ["S%d" % h],
                   ["M%d_%d" % (h, j)], [SB[h], "PM"])
            lin("V" if h == NG - 1 else "S", T.Mt[:, a:b], ps, 1.0, 192.0, ["S%d" % h], ["Mt%d" % h], [SB[h]])

        def larger(h, k):
            a, b = TG[h]
            tt(T.MX[:, 256 * k + 2 * a:256 * k + 2 * b], T.X[:, 16 * a + k:16 * b:8], T.PM[:, 2 * a:2 * b], A.max,
               parts(XP, TG[h], "X") + ["M%d_0" % h, "M%d_1" % h], ["MX%d_%d" % (h, k)], ["PM"])

        EK, MK = ["e0", "e1"], ["Mt%d" % h for h in range(NG)]
        if t: lin("S", W16, Wu[:], 1.0, -2048.0, [wk], [w16])
        fgather(0); fgather(1)
        extract(0)
        fgather(2); fgather(3)
        if t: act(T.ri[:, 0:1], T.Gs[:, 0:1], ["Gs"], ["ri"], scale=0.5, bias=-0.25)
        mm(T.PK[:, 0:256], T.on[:, 0:128], T.Kc[:], True, False, ["on", "Kc0", "Kc1", "Kc2"], ["K"], "PK")
        extract(1)
        offsets(0)
        if not t: filler(lateS, 99)
        xgather(0); xgather(1)
        if t: act(T.par[:, 0:1], T.ri[:, 0:1], ["Gs", "ri"], ["par"], scale=-2.0, bias=T.Gs[:, 0:1])
        else: filler(lastS, 2)
        offsets(1)
        if not t: filler(lateV, 99)
        mm(T.PW[:, 0:256], T.I[:], T.Cw[:], True, False, ["Cw0", "Cw1"], ["WN"], "PW")
        mm(T.PW[:, 0:128], T.Sh[:], W16, False, False, [w16, "Sh"], ["WN"], "PW")
        mm(T.PW[:, 128:256], T.Rev[:], W16, False, False, [w16, "Rev"], ["WN"], "PW")
        for c in range(2, len(XP)): xgather(c)
        if not t: filler(lastS, 99)
        total(0)
        xterm(0)
        if t:
            below(0); below(1); name(0); name(1)
        mm(T.PT[:, 0:128], T.e16[:], T.I[:], True, True, EK, ["Te"], "PT")
        for h in range(NG):
            if h + 1 < NG: total(h + 1)
            if h + 2 == NG:
                for x in range(1, len(XT)): xterm(x)
            mean(h)
            if h == 0:
                act(T.eT[:], T.PT[:, 0:128], ["Te"], ["eT"], ["PT"], bias=2048.0)
                if not t: floors()
            if h + 1 < NG:
                for k in range(8): larger(h, k)
        mm(T.PK[:, 0:256], T.Mt[:], T.BN[:], False, False, MK + ["BN0", "BN1"], ["K"], "PK")
        mm(T.PK[:, 0:128], T.e16[:], T.I[:], False, False, EK, ["K"], "PK")
        mm(T.PK[:, 128:256], W16, T.I[:], False, False, [w16], ["K"], "PK")
        mm(T.PT[:, 128:136], T.Mt[:], T.wt[:], True, True, MK + ["wt"], ["Tu"], "PT")
        for k in range(8):
            larger(NG - 1, k)
            for j in range(2):
                mm(T.PK[:, k + 8 * j:256:16], T.MX[:, 256 * k + j:256 * k + 256:2], T.BM[:], False, k == 7 and j == 1,
                   ["MX%d_%d" % (h, k) for h in range(NG)] + ["BM"], ["K"], "PK")
        act(T.sq[:], T.PT[:, 128:136], ["Tu"], ["sq"], ["PT"], f=AF.Square, scale=0.25, bias=(592.0 - 184 * 256) / 4)
        act(T.yi[:], T.sq[:], ["sq"], ["yi"], scale=0.5, bias=-10952.40625)
        mm(T.PD[:, 0:ND], T.m16[:], T.Own[:, 0:ND], True, False, ["m16"] + allr("Own"), ["D"], "PD")
        mm(T.PA[:, 0:128], T.SoP[:], W16, True, False, ["SoP", w16], ["V1", "Y1", "S2"], "PA")
        mm(T.PB[:, 0:128], T.SoP[:], W16, True, False, [w16], ["V2", "S0"], "PB")
        mm(T.PB[:, 0:128], T.I[:], T.c2k[:], False, False, [], ["V2"], "PB")
        scan(T.R[:, 0:128], T.d0[:], T.PK[:, 0:128], A.add, A.max, ["K", "d0"], ["R0"], ["PK"])
        scan(T.R[:, 128:256], T.d0[:], T.PK[:, 128:256], A.add, A.max, ["K", "d0"], ["R1"], ["PK"])
        ts(T.NK[:, 0:8], T.R[:, 15:128:16], 4095, None, A.bitwise_and, None, ["R0"], ["n"])
        ts(T.NK[:, 16:24], T.yi[:], 4095, None, A.bitwise_and, None, ["yi"], ["z"])
        ts(T.NK[:, 24:40], T.R[:, 15:256:16], 12, 15, A.logical_shift_right, A.bitwise_and, ["R0", "R1"], ["kk"])
        ts(T.NK[:, 8:16], T.R[:, 143:256:16], 4095, None, A.bitwise_and, None, ["R1"], ["c"])
        tt(T.eq[:], T.NK[:, 0:8].indirect(bc), T.eT[:], A.is_equal, ["n", "bc", "eT"], ["eq"])
        tt(T.ne[:], T.NK[:, 24:32], T.NK[:, 32:40], A.not_equal, ["kk"], ["ne"])
        ts(T.c2[:], T.NK[:, 8:16], col(12), None, A.add, None, ["c", "s12"], ["c2"])
        scan(T.Sc[:], T.rst[:], T.eq[:], A.mult, A.add, ["rst", "eq"], ["Sc"])
        tt(T.u2[:], T.c2[:], T.ne[:], A.mult, ["c2", "ne"], ["u2"])
        act(T.Nt[:, 0::16], T.NK[:, 0:8], ["n"], ["Nt"], bias=-2048.0)
        act(T.Zt[:, 0::16], T.NK[:, 16:24], ["z"], ["Zt"], bias=-2048.0)
        act(T.gK[:], T.NK[:, 32:40].indirect(bc), ["kk", "bc"], ["gK"])
        act(T.gN[:], T.NK[:, 0:8].indirect(bc), ["n", "bc"], ["gN"], bias=-2048.0)
        mm(T.PW[:, 0:128], T.Nt[:], T.I[:], False, False, ["Nt"], ["WN"], "PW")
        mm(T.PW[:, 128:256], T.Zt[:], T.I[:], False, False, ["Zt"], ["WN"], "PW")
        mm(T.PY[:, 0:128], T.gK[:], T.I[:], True, True, ["gK"], ["QK", "Y0", "S1"], "PY")
        act(T.ab[:], T.PY[:, 0:128], ["QK", "s10"], ["ab"], ["PY"], f=AF.Abs, bias=col(10), scale=8192.0)
        ts(T.ngo[:], T.Sc[:].indirect(T.b2[:]), T.par[:, 0:1], 4.0, A.subtract, A.is_lt, ["Sc", "b2", "par"], ["ngo"])
        lin("V", T.cb[:], T.u2[:].indirect(bc), -1.0 / 8192, col(13), ["u2", "bc", "s13"], ["cb"])
        mm(T.PW[:, 0:128], T.ngo[:], T.Ih[:], False, False, ["ngo", "Ih"], ["WN"], "PW")
        mm(T.PW[:, 128:256], T.ngo[:], T.Ig[:], False, True, ["ngo", "Ig"], ["WN"], "PW")
        mm(T.PD[:, 0:ND], T.ngo[:], T.Sel[:, 0:ND], False, False, ["ngo"] + allr("Sel"), ["D"], "PD")
        tt(T.cM[:], T.cb[:], T.m16[:], A.mult, ["cb", "m16"], ["cM"])
        mm(T.PD[:, 0:ND], T.cb[:], T.Sel[:, 0:ND], False, False, ["cb"], ["D"], "PD")
        mm(T.PD[:, 0:ND], T.cM[:], T.Blk[:, 0:ND], False, True, ["cM"] + allr("Blk"), ["D"], "PD")
        mm(T.PT[:, 144:152], T.cM[:], T.B8[:], True, True, ["cM", "B8"], ["Tb"], "PT")
        mm(T.PA[:, 0:128], T.gN[:], T.I[:], False, True, ["gN"], ["V1"], "PA")
        mm(T.PB[:, 0:128], T.gN[:], T.I[:], False, False, ["gN"], ["V2"], "PB")
        act(T.sg[:], T.PA[:, 0:128], ["V1"], ["sg"], ["PA"], f=AF.Sign, bias=0.5)
        if t < NV - 1: mm(T.PK[:, 384:392], T.on[:, 0:128], T.ngo[:, 0::16], True, True, ["on", "ngo"], ["Tc"], "PK")
        if t < NV - 1:
            ws = T["Ws%d" % (t + 1)]
            lin("V", ws[:], T.PW[:, 0:256], 1.0, 2048.0, ["WN"], ["Ws%d" % t], ["PW"])
            def send(more, ws=ws, t=t):
                op("G", lambda: g.remote_dma_fused([RemoteDMATransfer(
                    dst_ids=[DstId(rid=rid, pnc=pid)], dma_engine_mask=mask_out, remote_sem=T.sem["arr%d" % (t + 1)],
                    srcs=[ws[:, 0:128], ws[:, 128:256]], dsts=[T["Wu%d" % (t + 1)][:]], alu_op=2)],
                    local_sem=T.sem.sent), ["Ws%d" % t] + more, [], kind="send", val=len(eng_out))
            send([])
        mm(T.PB[:, 0:128], T.IN[:], T.ab[:], False, False, ["IN", "ab"], ["V2"], "PB")
        mm(T.PB[:, 0:128], T.Iod[:], T.sg[:], False, True, ["Iod", "sg"], ["V2"], "PB")
        ts(T.E[:, 0:ND], T.PD[:, 0:ND], 0.0, 8192.0, A.not_equal, A.mult, ["D"], ["E"], ["PD"])
        lin("V", T.o0[:, 0:8], T.PT[:, 144:152], 8192.0, 2048.0 + PAD, ["Tb"], ["o0"], ["PT"])
        scan(T.Rd[:, 0:ND], T.E[:, 0:ND], T.dm[:, 0:ND], A.min, A.max, ["E"] + allr("dm"), ["Rd"])
        tt(T.om[:], T.U[:].indirect(T.o0[:, 0:8]), T.ab[:], A.min, UK + ["o0", "ab"], ["om"])
        tt(T.o1[:], T.Rd[:, 0:ND].indirect(T.en[:, 0:1]), T.o0[:], A.min, ["Rd", "en", "o0"], ["o1", "dl%d" % t])
        if t < NV - 1:
            act(T.jk[:], T.PK[:, 384:392], ["Tc"], ["jk", "Gs"], ["PK"], acc=T.Gs[:, 0:1])
        else:
            act(T.tT[:], T.PW[:, 0:256], ["WN"], ["tT"], ["PW"], f=AF.Relu, bias=2048.0)
            mm(T.PT[:, 0:128], T.If[:], T.tT[:, 0:128], True, False, ["tT", "If"], ["Te"], "PT")
            mm(T.PT[:, 0:128], T.If[:], T.tT[:, 128:256], False, True, ["tT"], ["Te"], "PT")
            act(T.wo[:], T.PT[:, 0:128], ["Te"], ["wo"], ["PT"])
            dma("Y", T.yw[:], T.wo[:], ["wo"], [])

        def column(a):
            sl = slice(16 * NB * a, 16 * NB * (a + 1))
            tt(T.nw[:, sl], T.om[:, sl], T.PB[:, sl], A.max, ["om", "V2"], ["nw%d" % a], ["PB"])
        column(NS - 1)
        for a in range(NS - 1, -1, -1):
            if a: column(a - 1)
            cp(T.U[:].indirect(T.o1[:, NB * a:NB * (a + 1)]), T.nw[:, 16 * NB * a:16 * NB * (a + 1)],
               ["o1", "nw%d" % a], UK)

    HB = ["PM", "PY", "PA", "PB", "PD", "PK"]
    for c in range(len(CUTS) - 1):
        a, b = CUTS[c], CUTS[c + 1]
        act(T[HB[c]][:, 0:b - a], T.U[:, HI + a:HI + b], UK, ["H%d" % c], [HB[c]], scale=4096.0)
        tt(T.fo[:, a:b], T.U[:, LO + a:LO + b], T[HB[c]][:, 0:b - a], A.add, UK + ["H%d" % c], ["fo%d" % c], [HB[c]])
        dma("Y", T.yf[:, a:b], T.fo[:, a:b], ["fo%d" % c], [])
    emit(g, T, ops)
